import numpy as np
import ml_dtypes


def mxq(x, axis, fmt="e4m3"):
    dtype, down = {"e4m3": (ml_dtypes.float8_e4m3fn, 7), "e5m2": (ml_dtypes.float8_e5m2, 14)}[fmt]
    v = np.moveaxis(np.asarray(x, np.float32).astype(ml_dtypes.bfloat16).astype(np.float64), axis, -1)
    blocks = v.reshape(v.shape[:-1] + (-1, 32))
    amax = np.abs(blocks).max(-1, keepdims=True)
    byte = np.maximum(np.where(amax > 0, np.frexp(amax)[1] - 1 + 127, 0) - down, 1)
    scale = np.exp2(byte - 127.0)
    codes = (blocks / scale).astype(np.float32).astype(dtype).astype(np.float64)
    return np.moveaxis((codes * scale).reshape(v.shape), -1, axis)


WIDE = False


def mx_kscale(k):
    if not WIDE:
        return np.ones(k)
    levels = np.array([10, -10, 5, -5, 0])
    if k % 512:
        return np.exp2(np.random.permutation(np.resize(levels, k // 32))).repeat(32)
    a = np.empty((k // 512, 16))
    for p in range(k // 512):
        a[p, :8] = np.random.permutation(np.resize(levels, 8))
        for g in range(8):
            far = levels[np.abs(levels - a[p, g]) >= 10]
            a[p, g + 8] = far[np.random.randint(len(far))]
    return np.exp2(a.ravel()).repeat(32)


def f64(x):
    return np.asarray(x).astype(np.float64)


def striped(idx):
    return np.tile(idx.reshape(-1, 16).T, (8, 1)).astype(np.uint16)


def unstriped(offs):
    return offs[:16].T.reshape(-1).astype(np.int64)


def pack_weight(w):
    k, n = w.shape
    w = f64(np.asarray(w, np.float32).astype(ml_dtypes.bfloat16)).reshape(k // 32, 32, n)
    amax = np.abs(w).max(1)
    byte = np.clip(np.where(amax > 0, np.frexp(amax)[1] - 1 + 127 - 7, 1), 1, 254)
    scaled = (w * np.exp2(127.0 - byte)[:, None, :]).reshape(k, n).astype(np.float32)
    words = np.ascontiguousarray(scaled.reshape(k // 512, 128, 4, n).transpose(0, 1, 3, 2)).astype(ml_dtypes.float8_e4m3fn).view(np.uint8)
    return words, np.ascontiguousarray(byte.astype(np.uint8).reshape(k // 512, 16, n))


def unpack_weight(words, scales):
    g, p, n, _ = words.shape
    vals = np.ascontiguousarray(words).view(ml_dtypes.float8_e4m3fn).astype(np.float64) * np.repeat(np.exp2(scales.astype(np.float64) - 127.0), 8, axis=1)[..., None]
    return vals.transpose(0, 1, 3, 2).reshape(g * 512, n)


def relu(v):
    return np.maximum(v, 0.0)


K, T, S, D, V, H, N, U = 512, 2048, 512, 3, 512, 512, 256, 1024
P = 2 ** 7


def setup_inputs():
    n = np.random.standard_normal
    s = mx_kscale(K)[:, None]
    u = mx_kscale(H)
    packed_w2 = pack_weight(n((H, N)) / np.sqrt(H) / u[:, None])
    return {
        "xT": (n((K, T)) * s).astype(np.float32),
        "w1": (n((K, H)) / np.sqrt(K) / s * u).astype(np.float32),
        "w2_words": packed_w2[0],
        "w2_scales": packed_w2[1],
        "gate": np.tile(np.random.uniform(0.2, 0.6, (D, 1, V)), (1, P, 1)).astype(np.float32),
        "emb": (0.5 * n((H, U)) * u[:, None]).astype(np.float32),
        "offs": striped(np.random.permutation(T)[:S]),
        "cell": striped(np.random.permutation(U)[:S]),
        "pos1": striped(np.random.permutation(U)[:V]),
        "pos2": striped(np.random.permutation(U)[:V]),
        "pos3": striped(np.random.permutation(U)[:V]),
    }


def reference(xT, w1, w2_words, w2_scales, gate, emb, offs, cell, pos1, pos2, pos3):
    xq = mxq(f64(xT)[:, unstriped(offs)], 0, "e4m3")
    up = np.zeros((H, U))
    up[:, unstriped(cell)] = relu(mxq(f64(w1), 0, "e4m3").T @ xq)
    z = up + f64(emb)
    y = relu(unpack_weight(w2_words, w2_scales).T @ mxq(z, 0, "e4m3"))
    return y[:, unstriped(pos1)] * f64(gate)[0, :1] + y[:, unstriped(pos2)] * f64(gate)[1, :1] + y[:, unstriped(pos3)] * f64(gate)[2, :1]

@@ -1,0 +1,264 @@
+from contextlib import ExitStack
+
+import concourse.mybir as mybir
+from concourse.masks import make_identity
+
+F32 = mybir.dt.float32
+BF16 = mybir.dt.bfloat16
+I32 = mybir.dt.int32
+U32 = mybir.dt.uint32
+U16 = mybir.dt.uint16
+U8 = mybir.dt.uint8
+FP8X4 = mybir.dt.float8_e4m3fn_x4
+ADD = mybir.AluOpType.add
+MULT = mybir.AluOpType.mult
+RELU = mybir.ActivationFunctionType.Relu
+COPY = mybir.ActivationFunctionType.Copy
+
+K, T, S, D, V, H, N, U = 512, 2048, 512, 3, 512, 512, 256, 1024
+P = 128
+PACK = 4
+HALF = S // 2
+CHUNK = 256
+BANK = 512
+FLOPS = 2 * K * H * S + 2 * H * N * U
+
+
+def tile_picked_devox_relu_e_kernel(
+    tc, xT, w1, w2_words, w2_scales, gate, emb, offs, cell, pos1, pos2, pos3, out
+):
+    nc = tc.nc
+    with ExitStack() as ctx:
+        keep = ctx.enter_context(tc.tile_pool(name="keep", bufs=1))
+        psum = ctx.enter_context(tc.psum_pool(name="psum", bufs=1))
+
+        def sb(name, shape, dtype):
+            return keep.tile(shape, dtype, name=name, align_bytes=64)
+
+        def bank(b, name):
+            return psum.tile([P, BANK], F32, name=name, tag="bank%d" % b)
+
+        def load_list(name, src):
+            tile = keep.tile([P, S // 16], U16, name=name)
+            nc.sync.dma_start(tile[:], src)
+            return tile
+
+        w1_raw = sb("w1_raw", [P, PACK, H], F32)
+        nc.sync.dma_start(out=w1_raw[:], in_=w1.rearrange("(p j) c -> p j c", j=PACK))
+        offs_sb = load_list("offs_sb", offs)
+        x_rows = xT.rearrange("(p j) t -> p j t", j=PACK)
+        x_plane = []
+        for j in range(PACK):
+            plane = sb("x_plane%d" % j, [P, T], F32)
+            nc.sync.dma_start(out=plane[:], in_=x_rows[:, j, :])
+            x_plane.append(plane)
+        cell_sb = load_list("cell_sb", cell)
+        emb_rows = emb.rearrange("(p t) r -> p t r", t=PACK)
+        emb_plane = {}
+        for t in (0, 1, 3):
+            emb_plane[t] = sb("emb_plane%d" % t, [P, U], F32)
+            nc.sync.dma_start(out=emb_plane[t][:], in_=emb_rows[:, t, :])
+        addend = sb("addend", [P, 2, U], F32)
+        nc.sync.dma_start(out=addend[:, 0, :], in_=emb_rows[:, 2, :])
+        w2_codes = sb("w2_codes", [P, N], I32)
+        nc.sync.dma_start(out=w2_codes[:], in_=w2_words[0].rearrange("p n t -> p (n t)").bitcast(I32))
+        w2_sc = sb("w2_sc", [P, N], U8)
+        nc.gpsimd.memset(w2_sc[:], 0)
+        for q in range(4):
+            nc.sync.dma_start(
+                out=w2_sc[32 * q : 32 * q + 4, :].bitcast(I32),
+                in_=w2_scales[0, 4 * q : 4 * q + 4, :].bitcast(I32),
+            )
+        gate_sb = sb("gate_sb", [P, D, V], F32)
+        nc.sync.dma_start(out=gate_sb[:], in_=gate.rearrange("d p v -> p d v"))
+        pos_sb = [load_list("pos%d_sb" % d, src) for d, src in enumerate((pos1, pos2, pos3))]
+
+        ident = sb("ident", [P, P], F32)
+        make_identity(nc, ident[:])
+
+        up = {}
+        for t in range(PACK):
+            up[t] = sb("up%d" % t, [P, 2 * U if t == 2 else U], F32)
+            nc.vector.memset(up[t][:], 0.0)
+
+        w1_bf = sb("w1_bf", [P, PACK * H], BF16)
+        nc.scalar.activation(
+            w1_bf[:].rearrange("p (t m j) -> p t m j", t=PACK, j=PACK),
+            w1_raw[:].rearrange("p j (m t) -> p t m j", t=PACK),
+            COPY,
+        )
+        w1_codes = sb("w1_codes", [P, H], U32)
+        w1_sc = sb("w1_sc", [P, H], U8)
+
+        x_bf = [sb("x_bf%d" % s, [P, HALF, PACK], BF16) for s in range(2)]
+        x_codes = [sb("x_codes%d" % s, [P, HALF], U32) for s in range(2)]
+        x_sc = [sb("x_sc%d" % s, [P, HALF], U8) for s in range(2)]
+        cols = HALF // 16
+
+        def gather_x(j, s):
+            nc.vector.tensor_copy(x_bf[s][:, :, j], x_plane[j][:].indirect(offs_sb[:, s * cols : (s + 1) * cols]))
+
+        def quantize_x(s):
+            nc.vector.quantize_mx(
+                out=x_codes[s][:].bitcast(FP8X4), scales=x_sc[s][:], in_=x_bf[s][:].rearrange("p n j -> p (n j)")
+            )
+
+        for j in range(PACK - 1):
+            gather_x(j, 0)
+            gather_x(j, 1)
+        nc.vector.quantize_mx(out=w1_codes[:].bitcast(FP8X4), scales=w1_sc[:], in_=w1_bf[:])
+
+        h = {t: sb("h%d" % t, [P, S], F32) for t in range(PACK)}
+        order = (0, 1, 3, 2)
+
+        def first_product(s):
+            for b, t in enumerate(order):
+                acc = bank(b, "h_acc%d_%d" % (s, t))
+                nc.tensor.matmul_mx(
+                    out=acc[:, :HALF],
+                    lhsT=w1_codes[:, t * P : (t + 1) * P].bitcast(FP8X4),
+                    lhsT_scale=w1_sc[:, t * P : (t + 1) * P],
+                    rhs=x_codes[s][:].bitcast(FP8X4),
+                    rhs_scale=x_sc[s][:],
+                    start=True,
+                    stop=True,
+                )
+                nc.scalar.activation(h[t][:, s * HALF : (s + 1) * HALF], acc[:, :HALF], RELU)
+
+        def scatter(t, a, b):
+            nc.vector.tensor_copy(up[t][:].indirect(cell_sb[:, a // 16 : b // 16]), h[t][:, a:b])
+
+        gather_x(3, 0)
+        quantize_x(0)
+        first_product(0)
+        gather_x(3, 1)
+        scatter(0, 0, HALF)
+        quantize_x(1)
+        first_product(1)
+        scatter(1, 0, HALF)
+        scatter(0, HALF, S)
+        scatter(1, HALF, S)
+        scatter(3, 0, S)
+        scatter(2, 0, S)
+
+        def turn(dst, src, start, stop):
+            nc.tensor.matmul(dst, src, ident[:], start=start, stop=stop, is_transpose=True)
+
+        nch = U // CHUNK
+        words = [sb("words%d" % c, [P, 2, CHUNK], F32) for c in range(nch)]
+        pair_acc = [bank(4 + c, "pair_acc%d" % c) for c in range(nch)]
+
+        def pair_slot(c, b, e):
+            o = (2 * b + e) * P
+            return pair_acc[c][:, o : o + P]
+
+        def cells(c, b):
+            o = c * CHUNK + b * P
+            return slice(o, o + P)
+
+        for e in range(2):
+            for c in range(nch):
+                for b in range(2):
+                    turn(pair_slot(c, b, e), emb_plane[e][:, cells(c, b)], e == 0 and b == 0, False)
+        for e in range(2):
+            for c in range(nch):
+                for b in range(2):
+                    turn(pair_slot(c, b, e), up[e][:, cells(c, b)], False, e == 1 and b == 1)
+        third_acc = [bank(2 + g, "third_acc%d" % g) for g in range(2)]
+        for g in range(2):
+            for b in range(4):
+                o = g * BANK + b * P
+                turn(third_acc[g][:, b * P : (b + 1) * P], emb_plane[3][:, o : o + P], b == 0, False)
+        pair_t = []
+        for c in range(nch):
+            tile = sb("pair_t%d" % c, [P, 2, P, 2], BF16)
+            nc.scalar.activation(tile[:], pair_acc[c][:].rearrange("r (b e p) -> r b p e", b=2, e=2), COPY)
+            pair_t.append(tile)
+        for g in range(2):
+            back = bank(g, "pair_back%d" % g)
+            for i in range(2):
+                c = 2 * g + i
+                src = pair_t[c][:].rearrange("r b p e -> r (b p e)").bitcast(F32)
+                for b in range(2):
+                    o = i * CHUNK + b * P
+                    turn(back[:, o : o + P], src[:, b * P : (b + 1) * P], True, True)
+            for i in range(2):
+                nc.scalar.copy(words[2 * g + i][:, 0, :], back[:, i * CHUNK : (i + 1) * CHUNK])
+
+        for g in range(2):
+            for b in range(4):
+                o = g * BANK + b * P
+                turn(third_acc[g][:, b * P : (b + 1) * P], up[3][:, o : o + P], False, b == 3)
+        for g in range(2):
+            third_t = sb("third_t%d" % g, [P, BANK], F32)
+            nc.scalar.activation(third_t[:], third_acc[g][:], COPY)
+            back = bank(4 + g, "third_back%d" % g)
+            for b in range(4):
+                turn(back[:, b * P : (b + 1) * P], third_t[:, b * P : (b + 1) * P], True, True)
+            nc.scalar.activation(addend[:, 1, g * BANK : (g + 1) * BANK], back[:], COPY)
+
+        y = [sb("y%d" % m, [P, U], F32) for m in range(N // P)]
+        z_bf = [sb("z_bf%d" % c, [P, CHUNK * PACK], BF16) for c in range(nch)]
+        z_codes = [sb("z_codes%d" % c, [P, CHUNK], U32) for c in range(nch)]
+        z_sc = [sb("z_sc%d" % c, [P, CHUNK], U8) for c in range(nch)]
+        up2 = up[2][:].rearrange("p (e r) -> p e r", e=2)
+        for c in range(nch):
+            span = slice(c * CHUNK, (c + 1) * CHUNK)
+            nc.vector.tensor_tensor(
+                words[c][:, 1, :].bitcast(BF16).rearrange("p (g i e) -> p g e i", i=4, e=2),
+                up2[:, :, span].rearrange("p e (g i) -> p g e i", i=4),
+                addend[:, :, span].rearrange("p e (g i) -> p g e i", i=4),
+                ADD,
+            )
+            nc.scalar.copy(
+                z_bf[c][:].bitcast(F32).rearrange("p (g i u) -> p g u i", i=4, u=2),
+                words[c][:].rearrange("p u (g i) -> p g u i", i=4),
+            )
+        y_bank = (6, 7, 0, 1, 2, 3, 4, 5)
+        y_acc = {}
+        for c in range(nch):
+            nc.vector.quantize_mx(out=z_codes[c][:].bitcast(FP8X4), scales=z_sc[c][:], in_=z_bf[c][:])
+            for m in range(2):
+                acc = bank(y_bank[2 * c + m], "y_acc%d_%d" % (c, m))
+                nc.tensor.matmul_mx(
+                    out=acc[:, :CHUNK],
+                    lhsT=w2_codes[:, m * P : (m + 1) * P].bitcast(FP8X4),
+                    lhsT_scale=w2_sc[:, m * P : (m + 1) * P],
+                    rhs=z_codes[c][:].bitcast(FP8X4),
+                    rhs_scale=z_sc[c][:],
+                    start=True,
+                    stop=True,
+                )
+                y_acc[c, m] = acc
+            nc.scalar.activation(y[0][:, c * CHUNK : (c + 1) * CHUNK], y_acc[c, 0][:, :CHUNK], RELU)
+        for c in range(nch):
+            nc.scalar.activation(y[1][:, c * CHUNK : (c + 1) * CHUNK], y_acc[c, 1][:, :CHUNK], RELU)
+
+        term = {}
+        part = {}
+        for m in range(2):
+            for d in range(D):
+                term[m, d] = sb("term%d_%d" % (m, d), [P, V], F32)
+
+        def fetch(m, d):
+            nc.vector.tensor_tensor(term[m, d][:], y[m][:].indirect(pos_sb[d][:]), gate_sb[:, d, :], MULT)
+
+        def add2(m):
+            part[m] = sb("part%d" % m, [P, V], F32)
+            nc.vector.tensor_tensor(part[m][:], term[m, 0][:], term[m, 1][:], ADD)
+
+        def finish(m):
+            res = sb("res%d" % m, [P, V], F32)
+            nc.vector.tensor_tensor(res[:], part[m][:], term[m, 2][:], ADD)
+            nc.sync.dma_start(out=out[m * P : (m + 1) * P, :], in_=res[:])
+
+        fetch(0, 0)
+        fetch(0, 1)
+        fetch(0, 2)
+        add2(0)
+        fetch(1, 0)
+        finish(0)
+        fetch(1, 1)
+        fetch(1, 2)
+        add2(1)
+        finish(1)

@@ -55,11 +55,12 @@ def tile_picked_devox_relu_e_kernel(
         cell_sb = load_list("cell_sb", cell)
         emb_rows = emb.rearrange("(p t) r -> p t r", t=PACK)
         emb_plane = {}
-        for t in (0, 1, 3):
+        for t in (0, 1):
             emb_plane[t] = sb("emb_plane%d" % t, [P, U], F32)
             nc.sync.dma_start(out=emb_plane[t][:], in_=emb_rows[:, t, :])
-        addend = sb("addend", [P, 2, U], F32)
-        nc.sync.dma_start(out=addend[:, 0, :], in_=emb_rows[:, 2, :])
+        up = {t: sb("up%d" % t, [P, U if t < 2 else 2 * U], F32) for t in range(PACK)}
+        nc.sync.dma_start(out=up[3][:, U:], in_=emb_rows[:, 2, :])
+        nc.sync.dma_start(out=up[2][:, U:], in_=emb_rows[:, 3, :])
         w2_codes = sb("w2_codes", [P, N], I32)
         nc.sync.dma_start(out=w2_codes[:], in_=w2_words[0].rearrange("p n t -> p (n t)").bitcast(I32))
         w2_sc = sb("w2_sc", [P, N], U8)
@@ -76,10 +77,8 @@ def tile_picked_devox_relu_e_kernel(
         ident = sb("ident", [P, P], F32)
         make_identity(nc, ident[:])
 
-        up = {}
         for t in range(PACK):
-            up[t] = sb("up%d" % t, [P, 2 * U if t == 2 else U], F32)
-            nc.vector.memset(up[t][:], 0.0)
+            nc.vector.memset(up[t][:, :U], 0.0)
 
         w1_bf = sb("w1_bf", [P, PACK * H], BF16)
         nc.scalar.activation(
@@ -91,55 +90,49 @@ def tile_picked_devox_relu_e_kernel(
         w1_sc = sb("w1_sc", [P, H], U8)
 
         x_bf = [sb("x_bf%d" % s, [P, HALF, PACK], BF16) for s in range(2)]
-        x_codes = [sb("x_codes%d" % s, [P, HALF], U32) for s in range(2)]
-        x_sc = [sb("x_sc%d" % s, [P, HALF], U8) for s in range(2)]
+        x_codes = sb("x_codes", [P, S], U32)
+        x_sc = sb("x_sc", [P, S], U8)
         cols = HALF // 16
 
         def gather_x(j, s):
             nc.vector.tensor_copy(x_bf[s][:, :, j], x_plane[j][:].indirect(offs_sb[:, s * cols : (s + 1) * cols]))
 
-        def quantize_x(s):
+        def quantize_x(a, b):
+            s = a // HALF
+            flat = x_bf[s][:].rearrange("p n j -> p (n j)")
             nc.vector.quantize_mx(
-                out=x_codes[s][:].bitcast(FP8X4), scales=x_sc[s][:], in_=x_bf[s][:].rearrange("p n j -> p (n j)")
+                out=x_codes[:, a:b].bitcast(FP8X4),
+                scales=x_sc[:, a:b],
+                in_=flat[:, (a - s * HALF) * PACK : (b - s * HALF) * PACK],
             )
 
         for j in range(PACK - 1):
             gather_x(j, 0)
             gather_x(j, 1)
         nc.vector.quantize_mx(out=w1_codes[:].bitcast(FP8X4), scales=w1_sc[:], in_=w1_bf[:])
+        gather_x(PACK - 1, 0)
+        gather_x(PACK - 1, 1)
+        quantize_x(0, P)
+        quantize_x(P, HALF)
+        quantize_x(HALF, S)
 
         h = {t: sb("h%d" % t, [P, S], F32) for t in range(PACK)}
-        order = (0, 1, 3, 2)
-
-        def first_product(s):
-            for b, t in enumerate(order):
-                acc = bank(b, "h_acc%d_%d" % (s, t))
+        steps = ((0, (0, P)), (1, (0, HALF)), (0, (P, HALF, S)), (1, (HALF, S)), (3, (0, S)), (2, (0, S)))
+        for i, (t, cuts) in enumerate(steps):
+            acc = bank(i % 4, "h_acc%d" % i)
+            a, b = cuts[0], cuts[-1]
+            for lo, hi in zip(cuts[:-1], cuts[1:]):
                 nc.tensor.matmul_mx(
-                    out=acc[:, :HALF],
+                    out=acc[:, lo - a : hi - a],
                     lhsT=w1_codes[:, t * P : (t + 1) * P].bitcast(FP8X4),
                     lhsT_scale=w1_sc[:, t * P : (t + 1) * P],
-                    rhs=x_codes[s][:].bitcast(FP8X4),
-                    rhs_scale=x_sc[s][:],
+                    rhs=x_codes[:, lo:hi].bitcast(FP8X4),
+                    rhs_scale=x_sc[:, lo:hi],
                     start=True,
                     stop=True,
                 )
-                nc.scalar.activation(h[t][:, s * HALF : (s + 1) * HALF], acc[:, :HALF], RELU)
-
-        def scatter(t, a, b):
+            nc.scalar.activation(h[t][:, a:b], acc[:, : b - a], RELU)
             nc.vector.tensor_copy(up[t][:].indirect(cell_sb[:, a // 16 : b // 16]), h[t][:, a:b])
-
-        gather_x(3, 0)
-        quantize_x(0)
-        first_product(0)
-        gather_x(3, 1)
-        scatter(0, 0, HALF)
-        quantize_x(1)
-        first_product(1)
-        scatter(1, 0, HALF)
-        scatter(0, HALF, S)
-        scatter(1, HALF, S)
-        scatter(3, 0, S)
-        scatter(2, 0, S)
 
         def turn(dst, src, start, stop):
             nc.tensor.matmul(dst, src, ident[:], start=start, stop=stop, is_transpose=True)
@@ -164,11 +157,6 @@ def tile_picked_devox_relu_e_kernel(
             for c in range(nch):
                 for b in range(2):
                     turn(pair_slot(c, b, e), up[e][:, cells(c, b)], False, e == 1 and b == 1)
-        third_acc = [bank(2 + g, "third_acc%d" % g) for g in range(2)]
-        for g in range(2):
-            for b in range(4):
-                o = g * BANK + b * P
-                turn(third_acc[g][:, b * P : (b + 1) * P], emb_plane[3][:, o : o + P], b == 0, False)
         pair_t = []
         for c in range(nch):
             tile = sb("pair_t%d" % c, [P, 2, P, 2], BF16)
@@ -185,80 +173,110 @@ def tile_picked_devox_relu_e_kernel(
             for i in range(2):
                 nc.scalar.copy(words[2 * g + i][:, 0, :], back[:, i * CHUNK : (i + 1) * CHUNK])
 
-        for g in range(2):
-            for b in range(4):
-                o = g * BANK + b * P
-                turn(third_acc[g][:, b * P : (b + 1) * P], up[3][:, o : o + P], False, b == 3)
-        for g in range(2):
-            third_t = sb("third_t%d" % g, [P, BANK], F32)
-            nc.scalar.activation(third_t[:], third_acc[g][:], COPY)
-            back = bank(4 + g, "third_back%d" % g)
-            for b in range(4):
-                turn(back[:, b * P : (b + 1) * P], third_t[:, b * P : (b + 1) * P], True, True)
-            nc.scalar.activation(addend[:, 1, g * BANK : (g + 1) * BANK], back[:], COPY)
-
         y = [sb("y%d" % m, [P, U], F32) for m in range(N // P)]
         z_bf = [sb("z_bf%d" % c, [P, CHUNK * PACK], BF16) for c in range(nch)]
         z_codes = [sb("z_codes%d" % c, [P, CHUNK], U32) for c in range(nch)]
         z_sc = [sb("z_sc%d" % c, [P, CHUNK], U8) for c in range(nch)]
         up2 = up[2][:].rearrange("p (e r) -> p e r", e=2)
+        up3 = up[3][:].rearrange("p (e r) -> p e r", e=2)[:, ::-1, :]
         for c in range(nch):
             span = slice(c * CHUNK, (c + 1) * CHUNK)
             nc.vector.tensor_tensor(
                 words[c][:, 1, :].bitcast(BF16).rearrange("p (g i e) -> p g e i", i=4, e=2),
                 up2[:, :, span].rearrange("p e (g i) -> p g e i", i=4),
-                addend[:, :, span].rearrange("p e (g i) -> p g e i", i=4),
+                up3[:, :, span].rearrange("p e (g i) -> p g e i", i=4),
                 ADD,
             )
             nc.scalar.copy(
                 z_bf[c][:].bitcast(F32).rearrange("p (g i u) -> p g u i", i=4, u=2),
                 words[c][:].rearrange("p u (g i) -> p g u i", i=4),
             )
-        y_bank = (6, 7, 0, 1, 2, 3, 4, 5)
-        y_acc = {}
+        y0_bank = (2, 3, 4, 5)
+
+        def second_product(acc, m, c):
+            nc.tensor.matmul_mx(
+                out=acc,
+                lhsT=w2_codes[:, m * P : (m + 1) * P].bitcast(FP8X4),
+                lhsT_scale=w2_sc[:, m * P : (m + 1) * P],
+                rhs=z_codes[c][:].bitcast(FP8X4),
+                rhs_scale=z_sc[c][:],
+                start=True,
+                stop=True,
+            )
+
         for c in range(nch):
             nc.vector.quantize_mx(out=z_codes[c][:].bitcast(FP8X4), scales=z_sc[c][:], in_=z_bf[c][:])
-            for m in range(2):
-                acc = bank(y_bank[2 * c + m], "y_acc%d_%d" % (c, m))
-                nc.tensor.matmul_mx(
-                    out=acc[:, :CHUNK],
-                    lhsT=w2_codes[:, m * P : (m + 1) * P].bitcast(FP8X4),
-                    lhsT_scale=w2_sc[:, m * P : (m + 1) * P],
-                    rhs=z_codes[c][:].bitcast(FP8X4),
-                    rhs_scale=z_sc[c][:],
-                    start=True,
-                    stop=True,
-                )
-                y_acc[c, m] = acc
-            nc.scalar.activation(y[0][:, c * CHUNK : (c + 1) * CHUNK], y_acc[c, 0][:, :CHUNK], RELU)
-        for c in range(nch):
-            nc.scalar.activation(y[1][:, c * CHUNK : (c + 1) * CHUNK], y_acc[c, 1][:, :CHUNK], RELU)
+            acc = bank(y0_bank[c], "y0_acc%d" % c)
+            second_product(acc[:, :CHUNK], 0, c)
+            if c == nch - 2:
+                nc.vector.tensor_scalar_max(y[0][:, c * CHUNK : (c + 1) * CHUNK], acc[:, :CHUNK], 0.0)
+            else:
+                nc.scalar.activation(y[0][:, c * CHUNK : (c + 1) * CHUNK], acc[:, :CHUNK], RELU)
+        for g in range(2):
+            acc = bank(y0_bank[2 + g], "y1_acc%d" % g)
+            for i in range(2):
+                second_product(acc[:, i * CHUNK : (i + 1) * CHUNK], 1, 2 * g + i)
+            nc.scalar.activation(y[1][:, g * BANK : (g + 1) * BANK], acc[:], RELU)
 
         term = {}
-        part = {}
-        for m in range(2):
-            for d in range(D):
-                term[m, d] = sb("term%d_%d" % (m, d), [P, V], F32)
+        HV = V // 2
 
-        def fetch(m, d):
-            nc.vector.tensor_tensor(term[m, d][:], y[m][:].indirect(pos_sb[d][:]), gate_sb[:, d, :], MULT)
+        def fetch(m, d, a, b):
+            nc.vector.tensor_tensor(
+                term[m, d][:, a:b], y[m][:].indirect(pos_sb[d][:, a // 16 : b // 16]), gate_sb[:, d, a:b], MULT
+            )
 
-        def add2(m):
-            part[m] = sb("part%d" % m, [P, V], F32)
-            nc.vector.tensor_tensor(part[m][:], term[m, 0][:], term[m, 1][:], ADD)
+        sum0 = [bank(g, "sum0_%d" % g) for g in range(2)]
+        sum1 = bank(2, "sum1")
 
-        def finish(m):
-            res = sb("res%d" % m, [P, V], F32)
-            nc.vector.tensor_tensor(res[:], part[m][:], term[m, 2][:], ADD)
-            nc.sync.dma_start(out=out[m * P : (m + 1) * P, :], in_=res[:])
+        def pile0(d, halves=(0, 1)):
+            for g in halves:
+                for b in range(2):
+                    o = g * HV + b * P
+                    turn(sum0[g][:, b * P : (b + 1) * P], term[0, d][:, o : o + P], d == 0 and b == 0, d == D - 1 and b == 1)
 
-        fetch(0, 0)
-        fetch(0, 1)
-        fetch(0, 2)
-        add2(0)
-        fetch(1, 0)
-        finish(0)
-        fetch(1, 1)
-        fetch(1, 2)
-        add2(1)
-        finish(1)
+        def pile1(d):
+            for b in range(4):
+                turn(sum1[:, b * P : (b + 1) * P], term[1, d][:, b * P : (b + 1) * P], d == 0 and b == 0, d == 1 and b == 3)
+
+        def new_term(m, d, slot):
+            term[m, d] = keep.tile([P, V], F32, name="term%d_%d" % (m, d), tag="term_slot%d" % slot, align_bytes=64)
+
+        new_term(0, 0, 0)
+        new_term(0, 1, 1)
+        new_term(1, 0, 2)
+        new_term(1, 1, 3)
+        fetch(0, 0, 0, V)
+        pile0(0)
+        fetch(0, 1, 0, V)
+        pile0(1)
+        fetch(1, 0, 0, V)
+        pile1(0)
+        fetch(1, 1, 0, V)
+        pile1(1)
+        sum1_t = sb("sum1_t", [P, V], F32)
+        nc.scalar.activation(sum1_t[:], sum1[:], COPY)
+        back1 = bank(3, "back1")
+        for b in range(4):
+            turn(back1[:, b * P : (b + 1) * P], sum1_t[:, b * P : (b + 1) * P], True, True)
+        new_term(0, 2, 2)
+        for g in range(2):
+            fetch(0, 2, g * HV, (g + 1) * HV)
+            pile0(2, (g,))
+        for g in range(2):
+            sum0_t = sb("sum0_t%d" % g, [P, HV], F32)
+            nc.scalar.activation(sum0_t[:], sum0[g][:, :HV], COPY)
+            back0 = bank(6 + g, "back0_%d" % g)
+            for b in range(2):
+                turn(back0[:, b * P : (b + 1) * P], sum0_t[:, b * P : (b + 1) * P], True, True)
+            res = sb("res0_%d" % g, [P, HV], F32)
+            nc.scalar.activation(res[:], back0[:, :HV], COPY)
+            nc.scalar.dma_start(out=out[0:P, g * HV : (g + 1) * HV], in_=res[:])
+        new_term(1, 2, 3)
+        for g in range(2):
+            fetch(1, 2, g * HV, (g + 1) * HV)
+        for g in range(2):
+            span = slice(g * HV, (g + 1) * HV)
+            res = sb("res1_%d" % g, [P, HV], F32)
+            nc.vector.tensor_tensor(res[:], back1[:, span], term[1, 2][:, span], ADD)
+            nc.sync.dma_start(out=out[P : 2 * P, span], in_=res[:])

@@ -137,9 +137,11 @@ def tile_picked_devox_relu_e_kernel(
         def turn(dst, src, start, stop):
             nc.tensor.matmul(dst, src, ident[:], start=start, stop=stop, is_transpose=True)
 
-        nch = U // CHUNK
-        words = [sb("words%d" % c, [P, 2, CHUNK], F32) for c in range(nch)]
-        pair_acc = [bank(4 + c, "pair_acc%d" % c) for c in range(nch)]
+        cuts = (0, 256, 512, 768, 896, 1024)
+        chunks = list(zip(cuts[:-1], cuts[1:]))
+        nch = len(chunks)
+        words = [sb("words%d" % c, [P, 2, hi - lo], F32) for c, (lo, hi) in enumerate(chunks)]
+        pair_acc = [bank(4 + c, "pair_acc%d" % c) for c in range(4)]
 
         def pair_slot(c, b, e):
             o = (2 * b + e) * P
@@ -150,15 +152,15 @@ def tile_picked_devox_relu_e_kernel(
             return slice(o, o + P)
 
         for e in range(2):
-            for c in range(nch):
+            for c in range(4):
                 for b in range(2):
                     turn(pair_slot(c, b, e), emb_plane[e][:, cells(c, b)], e == 0 and b == 0, False)
         for e in range(2):
-            for c in range(nch):
+            for c in range(4):
                 for b in range(2):
                     turn(pair_slot(c, b, e), up[e][:, cells(c, b)], False, e == 1 and b == 1)
         pair_t = []
-        for c in range(nch):
+        for c in range(4):
             tile = sb("pair_t%d" % c, [P, 2, P, 2], BF16)
             nc.scalar.activation(tile[:], pair_acc[c][:].rearrange("r (b e p) -> r b p e", b=2, e=2), COPY)
             pair_t.append(tile)
@@ -170,28 +172,27 @@ def tile_picked_devox_relu_e_kernel(
                 for b in range(2):
                     o = i * CHUNK + b * P
                     turn(back[:, o : o + P], src[:, b * P : (b + 1) * P], True, True)
-            for i in range(2):
-                nc.scalar.copy(words[2 * g + i][:, 0, :], back[:, i * CHUNK : (i + 1) * CHUNK])
+            for c, (lo, hi) in enumerate(chunks):
+                if lo // BANK == g:
+                    nc.scalar.copy(words[c][:, 0, :], back[:, lo - g * BANK : hi - g * BANK])
 
         y = [sb("y%d" % m, [P, U], F32) for m in range(N // P)]
-        z_bf = [sb("z_bf%d" % c, [P, CHUNK * PACK], BF16) for c in range(nch)]
-        z_codes = [sb("z_codes%d" % c, [P, CHUNK], U32) for c in range(nch)]
-        z_sc = [sb("z_sc%d" % c, [P, CHUNK], U8) for c in range(nch)]
+        z_bf = [sb("z_bf%d" % c, [P, (hi - lo) * PACK], BF16) for c, (lo, hi) in enumerate(chunks)]
+        z_codes = [sb("z_codes%d" % c, [P, hi - lo], U32) for c, (lo, hi) in enumerate(chunks)]
+        z_sc = [sb("z_sc%d" % c, [P, hi - lo], U8) for c, (lo, hi) in enumerate(chunks)]
         up2 = up[2][:].rearrange("p (e r) -> p e r", e=2)
         up3 = up[3][:].rearrange("p (e r) -> p e r", e=2)[:, ::-1, :]
-        for c in range(nch):
-            span = slice(c * CHUNK, (c + 1) * CHUNK)
+        for c, (lo, hi) in enumerate(chunks):
             nc.vector.tensor_tensor(
-                words[c][:, 1, :].bitcast(BF16).rearrange("p (g i e) -> p g e i", i=4, e=2),
-                up2[:, :, span].rearrange("p e (g i) -> p g e i", i=4),
-                up3[:, :, span].rearrange("p e (g i) -> p g e i", i=4),
+                words[c][:, 1, :].bitcast(BF16).rearrange("p (g i e) -> p g e i", i=2, e=2),
+                up2[:, :, lo:hi].rearrange("p e (g i) -> p g e i", i=2),
+                up3[:, :, lo:hi].rearrange("p e (g i) -> p g e i", i=2),
                 ADD,
             )
             nc.scalar.copy(
-                z_bf[c][:].bitcast(F32).rearrange("p (g i u) -> p g u i", i=4, u=2),
-                words[c][:].rearrange("p u (g i) -> p g u i", i=4),
+                z_bf[c][:].bitcast(F32).rearrange("p (g i u) -> p g u i", i=2, u=2),
+                words[c][:].rearrange("p u (g i) -> p g u i", i=2),
             )
-        y0_bank = (2, 3, 4, 5)
 
         def second_product(acc, m, c):
             nc.tensor.matmul_mx(
@@ -204,79 +205,76 @@ def tile_picked_devox_relu_e_kernel(
                 stop=True,
             )
 
-        for c in range(nch):
+        for c, (lo, hi) in enumerate(chunks):
             nc.vector.quantize_mx(out=z_codes[c][:].bitcast(FP8X4), scales=z_sc[c][:], in_=z_bf[c][:])
-            acc = bank(y0_bank[c], "y0_acc%d" % c)
-            second_product(acc[:, :CHUNK], 0, c)
-            if c == nch - 2:
-                nc.vector.tensor_scalar_max(y[0][:, c * CHUNK : (c + 1) * CHUNK], acc[:, :CHUNK], 0.0)
+            acc = bank(2 + c, "y0_acc%d" % c)
+            second_product(acc[:, : hi - lo], 0, c)
+            if c == 2:
+                nc.vector.tensor_scalar_max(y[0][:, lo:hi], acc[:, : hi - lo], 0.0)
             else:
-                nc.scalar.activation(y[0][:, c * CHUNK : (c + 1) * CHUNK], acc[:, :CHUNK], RELU)
+                nc.scalar.activation(y[0][:, lo:hi], acc[:, : hi - lo], RELU)
         for g in range(2):
-            acc = bank(y0_bank[2 + g], "y1_acc%d" % g)
-            for i in range(2):
-                second_product(acc[:, i * CHUNK : (i + 1) * CHUNK], 1, 2 * g + i)
+            acc = bank(5 + g, "y1_acc%d" % g)
+            for c, (lo, hi) in enumerate(chunks):
+                if lo // BANK == g:
+                    second_product(acc[:, lo - g * BANK : hi - g * BANK], 1, c)
             nc.scalar.activation(y[1][:, g * BANK : (g + 1) * BANK], acc[:], RELU)
 
         term = {}
         HV = V // 2
+
+        def new_term(m, d, slot):
+            term[m, d] = keep.tile([P, V], F32, name="term%d_%d" % (m, d), tag="term_slot%d" % slot, align_bytes=64)
 
         def fetch(m, d, a, b):
             nc.vector.tensor_tensor(
                 term[m, d][:, a:b], y[m][:].indirect(pos_sb[d][:, a // 16 : b // 16]), gate_sb[:, d, a:b], MULT
             )
 
+        def pile(acc, m, d, g, last):
+            for i in range(2):
+                o = g * HV + i * P
+                turn(acc[:, i * P : (i + 1) * P], term[m, d][:, o : o + P], d == 0 and i == 0, d == last and i == 1)
+
+        def turn_back(acc, b, name):
+            turned = sb(name + "_t", [P, HV], F32)
+            nc.scalar.activation(turned[:], acc[:, :HV], COPY)
+            back = bank(b, name + "_back")
+            for i in range(2):
+                turn(back[:, i * P : (i + 1) * P], turned[:, i * P : (i + 1) * P], True, True)
+            return back
+
         sum0 = [bank(g, "sum0_%d" % g) for g in range(2)]
-        sum1 = bank(2, "sum1")
-
-        def pile0(d, halves=(0, 1)):
-            for g in halves:
-                for b in range(2):
-                    o = g * HV + b * P
-                    turn(sum0[g][:, b * P : (b + 1) * P], term[0, d][:, o : o + P], d == 0 and b == 0, d == D - 1 and b == 1)
-
-        def pile1(d):
-            for b in range(4):
-                turn(sum1[:, b * P : (b + 1) * P], term[1, d][:, b * P : (b + 1) * P], d == 0 and b == 0, d == 1 and b == 3)
-
-        def new_term(m, d, slot):
-            term[m, d] = keep.tile([P, V], F32, name="term%d_%d" % (m, d), tag="term_slot%d" % slot, align_bytes=64)
-
-        new_term(0, 0, 0)
-        new_term(0, 1, 1)
-        new_term(1, 0, 2)
-        new_term(1, 1, 3)
-        fetch(0, 0, 0, V)
-        pile0(0)
-        fetch(0, 1, 0, V)
-        pile0(1)
-        fetch(1, 0, 0, V)
-        pile1(0)
-        fetch(1, 1, 0, V)
-        pile1(1)
-        sum1_t = sb("sum1_t", [P, V], F32)
-        nc.scalar.activation(sum1_t[:], sum1[:], COPY)
-        back1 = bank(3, "back1")
-        for b in range(4):
-            turn(back1[:, b * P : (b + 1) * P], sum1_t[:, b * P : (b + 1) * P], True, True)
+        for d in range(2):
+            new_term(0, d, d)
+            fetch(0, d, 0, V)
+            for g in range(2):
+                pile(sum0[g], 0, d, g, 2)
         new_term(0, 2, 2)
         for g in range(2):
             fetch(0, 2, g * HV, (g + 1) * HV)
-            pile0(2, (g,))
-        for g in range(2):
-            sum0_t = sb("sum0_t%d" % g, [P, HV], F32)
-            nc.scalar.activation(sum0_t[:], sum0[g][:, :HV], COPY)
-            back0 = bank(6 + g, "back0_%d" % g)
-            for b in range(2):
-                turn(back0[:, b * P : (b + 1) * P], sum0_t[:, b * P : (b + 1) * P], True, True)
+            pile(sum0[g], 0, 2, g, 2)
+            back0 = turn_back(sum0[g], 2 + g, "sum0_%d" % g)
             res = sb("res0_%d" % g, [P, HV], F32)
             nc.scalar.activation(res[:], back0[:, :HV], COPY)
-            nc.scalar.dma_start(out=out[0:P, g * HV : (g + 1) * HV], in_=res[:])
+            nc.sync.dma_start(out=out[0:P, g * HV : (g + 1) * HV], in_=res[:])
+
+        sum1 = [bank((4, 7)[g], "sum1_%d" % g) for g in range(2)]
+        new_term(1, 0, 3)
+        fetch(1, 0, 0, V)
+        for g in range(2):
+            pile(sum1[g], 1, 0, g, 1)
+        new_term(1, 1, 4)
+        back1 = []
+        for g in range(2):
+            fetch(1, 1, g * HV, (g + 1) * HV)
+            pile(sum1[g], 1, 1, g, 1)
+            back1.append(turn_back(sum1[g], 5 + g, "sum1_%d" % g))
         new_term(1, 2, 3)
         for g in range(2):
             fetch(1, 2, g * HV, (g + 1) * HV)
         for g in range(2):
             span = slice(g * HV, (g + 1) * HV)
             res = sb("res1_%d" % g, [P, HV], F32)
-            nc.vector.tensor_tensor(res[:], back1[:, span], term[1, 2][:, span], ADD)
-            nc.sync.dma_start(out=out[P : 2 * P, span], in_=res[:])
+            nc.vector.tensor_tensor(res[:], back1[g][:, :HV], term[1, 2][:, span], ADD)
+            (nc.sync, nc.scalar)[g].dma_start(out=out[P : 2 * P, span], in_=res[:])

@@ -43,15 +43,18 @@ def tile_picked_devox_relu_e_kernel(
             nc.sync.dma_start(tile[:], src)
             return tile
 
-        w1_raw = sb("w1_raw", [P, PACK, H], F32)
-        nc.sync.dma_start(out=w1_raw[:], in_=w1.rearrange("(p j) c -> p j c", j=PACK))
-        offs_sb = load_list("offs_sb", offs)
         x_rows = xT.rearrange("(p j) t -> p j t", j=PACK)
         x_plane = []
         for j in range(PACK):
             plane = sb("x_plane%d" % j, [P, T], F32)
             nc.sync.dma_start(out=plane[:], in_=x_rows[:, j, :])
             x_plane.append(plane)
+            if j == 0:
+                offs_sb = load_list("offs_sb", offs)
+        w1_rows = w1.rearrange("(p j) c -> p j c", j=PACK)
+        w1_raw = sb("w1_raw", [P, PACK, H], F32)
+        for u in range(2):
+            nc.sync.dma_start(out=w1_raw[:, 2 * u : 2 * u + 2, :], in_=w1_rows[:, 2 * u : 2 * u + 2, :])
         cell_sb = load_list("cell_sb", cell)
         emb_rows = emb.rearrange("(p t) r -> p t r", t=PACK)
         emb_plane = {}
@@ -80,14 +83,17 @@ def tile_picked_devox_relu_e_kernel(
         for t in range(PACK):
             nc.vector.memset(up[t][:, :U], 0.0)
 
-        w1_bf = sb("w1_bf", [P, PACK * H], BF16)
-        nc.scalar.activation(
-            w1_bf[:].rearrange("p (t m j) -> p t m j", t=PACK, j=PACK),
-            w1_raw[:].rearrange("p j (m t) -> p t m j", t=PACK),
-            COPY,
-        )
-        w1_codes = sb("w1_codes", [P, H], U32)
-        w1_sc = sb("w1_sc", [P, H], U8)
+        w1_bf = {t: sb("w1_bf%d" % t, [P, P, PACK], BF16) for t in (0, 1, 3)}
+        w1_codes = [sb("w1_codes%d" % t, [P, P], U32) for t in range(PACK)]
+        w1_sc = [sb("w1_sc%d" % t, [P, P], U8) for t in range(PACK)]
+
+        def deal(t, lo, hi):
+            return w1_bf[t][:, :, lo:hi], w1_raw[:, lo:hi, :].rearrange("p j (m t) -> p t m j", t=PACK)[:, t, :, :]
+
+        def quantize_w1(t):
+            nc.vector.quantize_mx(
+                out=w1_codes[t][:].bitcast(FP8X4), scales=w1_sc[t][:], in_=w1_bf[t][:].rearrange("p m j -> p (m j)")
+            )
 
         x_bf = [sb("x_bf%d" % s, [P, HALF, PACK], BF16) for s in range(2)]
         x_codes = sb("x_codes", [P, S], U32)
@@ -106,33 +112,40 @@ def tile_picked_devox_relu_e_kernel(
                 in_=flat[:, (a - s * HALF) * PACK : (b - s * HALF) * PACK],
             )
 
-        for j in range(PACK - 1):
+        for j in range(PACK):
             gather_x(j, 0)
             gather_x(j, 1)
-        nc.vector.quantize_mx(out=w1_codes[:].bitcast(FP8X4), scales=w1_sc[:], in_=w1_bf[:])
-        gather_x(PACK - 1, 0)
-        gather_x(PACK - 1, 1)
-        quantize_x(0, P)
-        quantize_x(P, HALF)
+        quantize_x(0, HALF)
         quantize_x(HALF, S)
+        for t in (0, 1):
+            nc.scalar.activation(*deal(t, 0, 2), COPY)
+        for t in (0, 1):
+            nc.vector.tensor_copy(*deal(t, 2, PACK))
+        for t in (0, 1):
+            quantize_w1(t)
+        nc.scalar.activation(*deal(3, 0, PACK), COPY)
+        w1_bf[2] = keep.tile([P, P, PACK], BF16, name="w1_bf2", tag="w1_bf0", align_bytes=64)
+        nc.vector.tensor_copy(*deal(2, 0, PACK))
+        quantize_w1(3)
+        quantize_w1(2)
 
-        h = {t: sb("h%d" % t, [P, S], F32) for t in range(PACK)}
-        steps = ((0, (0, P)), (1, (0, HALF)), (0, (P, HALF, S)), (1, (HALF, S)), (3, (0, S)), (2, (0, S)))
+        steps = ((0, (0, P)), (1, (0, S)), (0, (P, HALF, S)), (3, (0, S)), (2, (0, S)))
         for i, (t, cuts) in enumerate(steps):
-            acc = bank(i % 4, "h_acc%d" % i)
+            acc = bank((0, 7, 0, 5, 6)[i], "h_acc%d" % i)
             a, b = cuts[0], cuts[-1]
             for lo, hi in zip(cuts[:-1], cuts[1:]):
                 nc.tensor.matmul_mx(
                     out=acc[:, lo - a : hi - a],
-                    lhsT=w1_codes[:, t * P : (t + 1) * P].bitcast(FP8X4),
-                    lhsT_scale=w1_sc[:, t * P : (t + 1) * P],
+                    lhsT=w1_codes[t][:].bitcast(FP8X4),
+                    lhsT_scale=w1_sc[t][:],
                     rhs=x_codes[:, lo:hi].bitcast(FP8X4),
                     rhs_scale=x_sc[:, lo:hi],
                     start=True,
                     stop=True,
                 )
-            nc.scalar.activation(h[t][:, a:b], acc[:, : b - a], RELU)
-            nc.vector.tensor_copy(up[t][:].indirect(cell_sb[:, a // 16 : b // 16]), h[t][:, a:b])
+            h = keep.tile([P, b - a], F32, name="h%d" % i, tag="h_step%d" % i, align_bytes=64)
+            nc.scalar.activation(h[:], acc[:, : b - a], RELU)
+            nc.vector.tensor_copy(up[t][:].indirect(cell_sb[:, a // 16 : b // 16]), h[:])
 
         def turn(dst, src, start, stop):
             nc.tensor.matmul(dst, src, ident[:], start=start, stop=stop, is_transpose=True)
@@ -141,7 +154,7 @@ def tile_picked_devox_relu_e_kernel(
         chunks = list(zip(cuts[:-1], cuts[1:]))
         nch = len(chunks)
         words = [sb("words%d" % c, [P, 2, hi - lo], F32) for c, (lo, hi) in enumerate(chunks)]
-        pair_acc = [bank(4 + c, "pair_acc%d" % c) for c in range(4)]
+        pair_acc = [bank((7, 0, 5, 6)[c], "pair_acc%d" % c) for c in range(4)]
 
         def pair_slot(c, b, e):
             o = (2 * b + e) * P
@@ -165,7 +178,7 @@ def tile_picked_devox_relu_e_kernel(
             nc.scalar.activation(tile[:], pair_acc[c][:].rearrange("r (b e p) -> r b p e", b=2, e=2), COPY)
             pair_t.append(tile)
         for g in range(2):
-            back = bank(g, "pair_back%d" % g)
+            back = bank(1 + g, "pair_back%d" % g)
             for i in range(2):
                 c = 2 * g + i
                 src = pair_t[c][:].rearrange("r b p e -> r (b p e)").bitcast(F32)
@@ -207,7 +220,7 @@ def tile_picked_devox_relu_e_kernel(
 
         for c, (lo, hi) in enumerate(chunks):
             nc.vector.quantize_mx(out=z_codes[c][:].bitcast(FP8X4), scales=z_sc[c][:], in_=z_bf[c][:])
-            acc = bank(2 + c, "y0_acc%d" % c)
+            acc = bank((3, 4, 7, 0, 5)[c], "y0_acc%d" % c)
             second_product(acc[:, : hi - lo], 0, c)
             if c == 2:
                 nc.vector.tensor_scalar_max(y[0][:, lo:hi], acc[:, : hi - lo], 0.0)

@@ -19,7 +19,6 @@ K, T, S, D, V, H, N, U = 512, 2048, 512, 3, 512, 512, 256, 1024
 P = 128
 PACK = 4
 HALF = S // 2
-CHUNK = 256
 BANK = 512
 FLOPS = 2 * K * H * S + 2 * H * N * U
 
@@ -32,8 +31,8 @@ def tile_picked_devox_relu_e_kernel(
         keep = ctx.enter_context(tc.tile_pool(name="keep", bufs=1))
         psum = ctx.enter_context(tc.psum_pool(name="psum", bufs=1))
 
-        def sb(name, shape, dtype):
-            return keep.tile(shape, dtype, name=name, align_bytes=64)
+        def sb(name, shape, dtype, tag=None):
+            return keep.tile(shape, dtype, name=name, tag=tag or name, align_bytes=64)
 
         def bank(b, name):
             return psum.tile([P, BANK], F32, name=name, tag="bank%d" % b)
@@ -57,13 +56,11 @@ def tile_picked_devox_relu_e_kernel(
             nc.sync.dma_start(out=w1_raw[:, 2 * u : 2 * u + 2, :], in_=w1_rows[:, 2 * u : 2 * u + 2, :])
         cell_sb = load_list("cell_sb", cell)
         emb_rows = emb.rearrange("(p t) r -> p t r", t=PACK)
-        emb_plane = {}
-        for t in (0, 1):
-            emb_plane[t] = sb("emb_plane%d" % t, [P, U], F32)
-            nc.sync.dma_start(out=emb_plane[t][:], in_=emb_rows[:, t, :])
-        up = {t: sb("up%d" % t, [P, U if t < 2 else 2 * U], F32) for t in range(PACK)}
-        nc.sync.dma_start(out=up[3][:, U:], in_=emb_rows[:, 2, :])
-        nc.sync.dma_start(out=up[2][:, U:], in_=emb_rows[:, 3, :])
+        emb_plane = {t: sb("emb_plane%d" % t, [P, U], F32) for t in (0, 3)}
+        words = sb("words", [P, 2 * U], F32)
+        nc.sync.dma_start(out=emb_plane[0][:], in_=emb_rows[:, 0, :])
+        nc.sync.dma_start(out=words[:].rearrange("p (u r) -> p u r", u=2), in_=emb_rows[:, 1:3, :])
+        nc.sync.dma_start(out=emb_plane[3][:], in_=emb_rows[:, 3, :])
         w2_codes = sb("w2_codes", [P, N], I32)
         nc.sync.dma_start(out=w2_codes[:], in_=w2_words[0].rearrange("p n t -> p (n t)").bitcast(I32))
         w2_sc = sb("w2_sc", [P, N], U8)
@@ -73,17 +70,33 @@ def tile_picked_devox_relu_e_kernel(
                 out=w2_sc[32 * q : 32 * q + 4, :].bitcast(I32),
                 in_=w2_scales[0, 4 * q : 4 * q + 4, :].bitcast(I32),
             )
-        gate_sb = sb("gate_sb", [P, D, V], F32)
-        nc.sync.dma_start(out=gate_sb[:], in_=gate.rearrange("d p v -> p d v"))
+        gate_sb = [sb("gate%d" % d, [P, V], F32) for d in range(D)]
+        for d in range(D):
+            nc.sync.dma_start(out=gate_sb[d][:], in_=gate[d])
         pos_sb = [load_list("pos%d_sb" % d, src) for d, src in enumerate((pos1, pos2, pos3))]
 
         ident = sb("ident", [P, P], F32)
         make_identity(nc, ident[:])
 
+        up = [sb("up%d" % t, [P, U], F32) for t in range(PACK)]
         for t in range(PACK):
-            nc.vector.memset(up[t][:, :U], 0.0)
+            nc.vector.memset(up[t][:], 0.0)
 
-        w1_bf = {t: sb("w1_bf%d" % t, [P, P, PACK], BF16) for t in (0, 1, 3)}
+        x_bf = [sb("x_bf%d" % s, [P, HALF, PACK], BF16) for s in range(2)]
+        x_codes = sb("x_codes", [P, S], U32)
+        x_sc = sb("x_sc", [P, S], U8)
+        for j in range(PACK):
+            for s in range(2):
+                entries = offs_sb[:, s * HALF // 16 : (s + 1) * HALF // 16]
+                nc.vector.tensor_copy(x_bf[s][:, :, j], x_plane[j][:].indirect(entries))
+        for s in range(2):
+            nc.vector.quantize_mx(
+                out=x_codes[:, s * HALF : (s + 1) * HALF].bitcast(FP8X4),
+                scales=x_sc[:, s * HALF : (s + 1) * HALF],
+                in_=x_bf[s][:].rearrange("p n j -> p (n j)"),
+            )
+
+        w1_bf = {t: sb("w1_bf%d" % t, [P, P, PACK], BF16) for t in range(3)}
         w1_codes = [sb("w1_codes%d" % t, [P, P], U32) for t in range(PACK)]
         w1_sc = [sb("w1_sc%d" % t, [P, P], U8) for t in range(PACK)]
 
@@ -95,47 +108,25 @@ def tile_picked_devox_relu_e_kernel(
                 out=w1_codes[t][:].bitcast(FP8X4), scales=w1_sc[t][:], in_=w1_bf[t][:].rearrange("p m j -> p (m j)")
             )
 
-        x_bf = [sb("x_bf%d" % s, [P, HALF, PACK], BF16) for s in range(2)]
-        x_codes = sb("x_codes", [P, S], U32)
-        x_sc = sb("x_sc", [P, S], U8)
-        cols = HALF // 16
-
-        def gather_x(j, s):
-            nc.vector.tensor_copy(x_bf[s][:, :, j], x_plane[j][:].indirect(offs_sb[:, s * cols : (s + 1) * cols]))
-
-        def quantize_x(a, b):
-            s = a // HALF
-            flat = x_bf[s][:].rearrange("p n j -> p (n j)")
-            nc.vector.quantize_mx(
-                out=x_codes[:, a:b].bitcast(FP8X4),
-                scales=x_sc[:, a:b],
-                in_=flat[:, (a - s * HALF) * PACK : (b - s * HALF) * PACK],
-            )
-
-        for j in range(PACK):
-            gather_x(j, 0)
-            gather_x(j, 1)
-        quantize_x(0, HALF)
-        quantize_x(HALF, S)
         for t in (0, 1):
             nc.scalar.activation(*deal(t, 0, 2), COPY)
         for t in (0, 1):
             nc.vector.tensor_copy(*deal(t, 2, PACK))
         for t in (0, 1):
             quantize_w1(t)
-        nc.scalar.activation(*deal(3, 0, PACK), COPY)
-        w1_bf[2] = keep.tile([P, P, PACK], BF16, name="w1_bf2", tag="w1_bf0", align_bytes=64)
-        nc.vector.tensor_copy(*deal(2, 0, PACK))
-        quantize_w1(3)
-        quantize_w1(2)
+        nc.scalar.activation(*deal(2, 0, PACK), COPY)
+        w1_bf[3] = sb("w1_bf3", [P, P, PACK], BF16, tag="w1_bf0")
+        nc.vector.tensor_copy(*deal(3, 0, PACK))
+        for t in (2, 3):
+            quantize_w1(t)
 
-        steps = ((0, (0, P)), (1, (0, S)), (0, (P, HALF, S)), (3, (0, S)), (2, (0, S)))
-        for i, (t, cuts) in enumerate(steps):
-            acc = bank((0, 7, 0, 5, 6)[i], "h_acc%d" % i)
-            a, b = cuts[0], cuts[-1]
+        steps = ((0, 0, (0, P)), (1, 1, (0, S)), (0, 0, (P, HALF, S)), (2, 2, (0, S)), (3, 2, (0, S)))
+        for i, (t, b, cuts) in enumerate(steps):
+            acc = bank(b, "h_acc%d" % i)
+            first, last = cuts[0], cuts[-1]
             for lo, hi in zip(cuts[:-1], cuts[1:]):
                 nc.tensor.matmul_mx(
-                    out=acc[:, lo - a : hi - a],
+                    out=acc[:, lo - first : hi - first],
                     lhsT=w1_codes[t][:].bitcast(FP8X4),
                     lhsT_scale=w1_sc[t][:],
                     rhs=x_codes[:, lo:hi].bitcast(FP8X4),
@@ -143,69 +134,30 @@ def tile_picked_devox_relu_e_kernel(
                     start=True,
                     stop=True,
                 )
-            h = keep.tile([P, b - a], F32, name="h%d" % i, tag="h_step%d" % i, align_bytes=64)
-            nc.scalar.activation(h[:], acc[:, : b - a], RELU)
-            nc.vector.tensor_copy(up[t][:].indirect(cell_sb[:, a // 16 : b // 16]), h[:])
+            h = sb("h%d" % i, [P, last - first], F32)
+            nc.scalar.activation(h[:], acc[:, : last - first], RELU)
+            nc.vector.tensor_copy(up[t][:].indirect(cell_sb[:, first // 16 : last // 16]), h[:])
 
-        def turn(dst, src, start, stop):
-            nc.tensor.matmul(dst, src, ident[:], start=start, stop=stop, is_transpose=True)
+        halves = words[:].bitcast(BF16).rearrange("p (u r e) -> p u r e", u=2, e=2)
+        nc.gpsimd.tensor_tensor(halves[:, 0, :, 1], up[1][:], words[:, :U], ADD)
+        nc.gpsimd.tensor_tensor(halves[:, 0, :, 0], up[0][:], emb_plane[0][:], ADD)
+        nc.gpsimd.tensor_tensor(halves[:, 1, :, 0], up[2][:], words[:, U:], ADD)
 
-        cuts = (0, 256, 512, 768, 896, 1024)
+        cuts = (0, 128, 384, 640, 768, 1024)
         chunks = list(zip(cuts[:-1], cuts[1:]))
-        nch = len(chunks)
-        words = [sb("words%d" % c, [P, 2, hi - lo], F32) for c, (lo, hi) in enumerate(chunks)]
-        pair_acc = [bank((7, 0, 5, 6)[c], "pair_acc%d" % c) for c in range(4)]
-
-        def pair_slot(c, b, e):
-            o = (2 * b + e) * P
-            return pair_acc[c][:, o : o + P]
-
-        def cells(c, b):
-            o = c * CHUNK + b * P
-            return slice(o, o + P)
-
-        for e in range(2):
-            for c in range(4):
-                for b in range(2):
-                    turn(pair_slot(c, b, e), emb_plane[e][:, cells(c, b)], e == 0 and b == 0, False)
-        for e in range(2):
-            for c in range(4):
-                for b in range(2):
-                    turn(pair_slot(c, b, e), up[e][:, cells(c, b)], False, e == 1 and b == 1)
-        pair_t = []
-        for c in range(4):
-            tile = sb("pair_t%d" % c, [P, 2, P, 2], BF16)
-            nc.scalar.activation(tile[:], pair_acc[c][:].rearrange("r (b e p) -> r b p e", b=2, e=2), COPY)
-            pair_t.append(tile)
-        for g in range(2):
-            back = bank(1 + g, "pair_back%d" % g)
-            for i in range(2):
-                c = 2 * g + i
-                src = pair_t[c][:].rearrange("r b p e -> r (b p e)").bitcast(F32)
-                for b in range(2):
-                    o = i * CHUNK + b * P
-                    turn(back[:, o : o + P], src[:, b * P : (b + 1) * P], True, True)
-            for c, (lo, hi) in enumerate(chunks):
-                if lo // BANK == g:
-                    nc.scalar.copy(words[c][:, 0, :], back[:, lo - g * BANK : hi - g * BANK])
-
-        y = [sb("y%d" % m, [P, U], F32) for m in range(N // P)]
         z_bf = [sb("z_bf%d" % c, [P, (hi - lo) * PACK], BF16) for c, (lo, hi) in enumerate(chunks)]
         z_codes = [sb("z_codes%d" % c, [P, hi - lo], U32) for c, (lo, hi) in enumerate(chunks)]
         z_sc = [sb("z_sc%d" % c, [P, hi - lo], U8) for c, (lo, hi) in enumerate(chunks)]
-        up2 = up[2][:].rearrange("p (e r) -> p e r", e=2)
-        up3 = up[3][:].rearrange("p (e r) -> p e r", e=2)[:, ::-1, :]
+        pairs = words[:].rearrange("p (u r) -> p u r", u=2)
         for c, (lo, hi) in enumerate(chunks):
-            nc.vector.tensor_tensor(
-                words[c][:, 1, :].bitcast(BF16).rearrange("p (g i e) -> p g e i", i=2, e=2),
-                up2[:, :, lo:hi].rearrange("p e (g i) -> p g e i", i=2),
-                up3[:, :, lo:hi].rearrange("p e (g i) -> p g e i", i=2),
-                ADD,
+            nc.vector.tensor_tensor(halves[:, 1, lo:hi, 1], up[3][:, lo:hi], emb_plane[3][:, lo:hi], ADD)
+            weave = nc.vector.tensor_copy if c == len(chunks) - 1 else nc.scalar.copy
+            weave(
+                z_bf[c][:].bitcast(F32).rearrange("p (g i u) -> p g u i", i=4, u=2),
+                pairs[:, :, lo:hi].rearrange("p u (g i) -> p g u i", i=4),
             )
-            nc.scalar.copy(
-                z_bf[c][:].bitcast(F32).rearrange("p (g i u) -> p g u i", i=2, u=2),
-                words[c][:].rearrange("p u (g i) -> p g u i", i=2),
-            )
+
+        y = [sb("y0", [P, U], F32, tag="words"), sb("y1", [P, U], F32)]
 
         def second_product(acc, m, c):
             nc.tensor.matmul_mx(
@@ -218,76 +170,73 @@ def tile_picked_devox_relu_e_kernel(
                 stop=True,
             )
 
-        for c, (lo, hi) in enumerate(chunks):
+        for c in (0, 1, 4, 2, 3):
+            lo, hi = chunks[c]
             nc.vector.quantize_mx(out=z_codes[c][:].bitcast(FP8X4), scales=z_sc[c][:], in_=z_bf[c][:])
-            acc = bank((3, 4, 7, 0, 5)[c], "y0_acc%d" % c)
+            acc = bank(c, "y0_acc%d" % c)
             second_product(acc[:, : hi - lo], 0, c)
-            if c == 2:
+            if c in (2,):
                 nc.vector.tensor_scalar_max(y[0][:, lo:hi], acc[:, : hi - lo], 0.0)
             else:
                 nc.scalar.activation(y[0][:, lo:hi], acc[:, : hi - lo], RELU)
-        for g in range(2):
-            acc = bank(5 + g, "y1_acc%d" % g)
-            for c, (lo, hi) in enumerate(chunks):
-                if lo // BANK == g:
-                    second_product(acc[:, lo - g * BANK : hi - g * BANK], 1, c)
-            nc.scalar.activation(y[1][:, g * BANK : (g + 1) * BANK], acc[:], RELU)
+        for b, group in ((2, (0, 1)), (3, (2, 3)), (4, (4,))):
+            acc = bank(b, "y1_acc%d" % b)
+            first, last = chunks[group[0]][0], chunks[group[-1]][1]
+            for c in group:
+                lo, hi = chunks[c]
+                second_product(acc[:, lo - first : hi - first], 1, c)
+            nc.scalar.activation(y[1][:, first:last], acc[:, : last - first], RELU)
 
-        term = {}
-        HV = V // 2
+        def turn(dst, src, start, stop):
+            nc.tensor.matmul(dst, src, ident[:], start=start, stop=stop, is_transpose=True)
 
-        def new_term(m, d, slot):
-            term[m, d] = keep.tile([P, V], F32, name="term%d_%d" % (m, d), tag="term_slot%d" % slot, align_bytes=64)
-
-        def fetch(m, d, a, b):
+        def fetch(term, m, d, lo, hi):
             nc.vector.tensor_tensor(
-                term[m, d][:, a:b], y[m][:].indirect(pos_sb[d][:, a // 16 : b // 16]), gate_sb[:, d, a:b], MULT
+                term[:, lo:hi], y[m][:].indirect(pos_sb[d][:, lo // 16 : hi // 16]), gate_sb[d][:, lo:hi], MULT
             )
 
-        def pile(acc, m, d, g, last):
-            for i in range(2):
-                o = g * HV + i * P
-                turn(acc[:, i * P : (i + 1) * P], term[m, d][:, o : o + P], d == 0 and i == 0, d == last and i == 1)
+        def pile(acc, term, lo, hi, first, last):
+            for o in range(lo, hi, P):
+                turn(acc[:, o - lo : o - lo + P], term[:, o : o + P], first and o == lo, last and o + P == hi)
 
-        def turn_back(acc, b, name):
-            turned = sb(name + "_t", [P, HV], F32)
-            nc.scalar.activation(turned[:], acc[:, :HV], COPY)
+        def turn_back(acc, width, b, name):
+            turned = sb(name + "_t", [P, width], F32)
+            nc.scalar.activation(turned[:], acc[:, :width], COPY)
             back = bank(b, name + "_back")
-            for i in range(2):
-                turn(back[:, i * P : (i + 1) * P], turned[:, i * P : (i + 1) * P], True, True)
+            for o in range(0, width, P):
+                turn(back[:, o : o + P], turned[:, o : o + P], True, True)
             return back
 
-        sum0 = [bank(g, "sum0_%d" % g) for g in range(2)]
+        spans0 = ((0, 256), (256, 384), (384, 512))
+        spans1 = ((0, 256), (256, 512))
+        sum0 = [bank((5, 6, 7)[g], "sum0_%d" % g) for g in range(3)]
         for d in range(2):
-            new_term(0, d, d)
-            fetch(0, d, 0, V)
-            for g in range(2):
-                pile(sum0[g], 0, d, g, 2)
-        new_term(0, 2, 2)
-        for g in range(2):
-            fetch(0, 2, g * HV, (g + 1) * HV)
-            pile(sum0[g], 0, 2, g, 2)
-            back0 = turn_back(sum0[g], 2 + g, "sum0_%d" % g)
-            res = sb("res0_%d" % g, [P, HV], F32)
-            nc.scalar.activation(res[:], back0[:, :HV], COPY)
-            nc.sync.dma_start(out=out[0:P, g * HV : (g + 1) * HV], in_=res[:])
-
-        sum1 = [bank((4, 7)[g], "sum1_%d" % g) for g in range(2)]
-        new_term(1, 0, 3)
-        fetch(1, 0, 0, V)
-        for g in range(2):
-            pile(sum1[g], 1, 0, g, 1)
-        new_term(1, 1, 4)
-        back1 = []
-        for g in range(2):
-            fetch(1, 1, g * HV, (g + 1) * HV)
-            pile(sum1[g], 1, 1, g, 1)
-            back1.append(turn_back(sum1[g], 5 + g, "sum1_%d" % g))
-        new_term(1, 2, 3)
-        for g in range(2):
-            fetch(1, 2, g * HV, (g + 1) * HV)
-        for g in range(2):
-            span = slice(g * HV, (g + 1) * HV)
-            res = sb("res1_%d" % g, [P, HV], F32)
-            nc.vector.tensor_tensor(res[:], back1[g][:, :HV], term[1, 2][:, span], ADD)
-            (nc.sync, nc.scalar)[g].dma_start(out=out[P : 2 * P, span], in_=res[:])
+            term = sb("term0_%d" % d, [P, V], F32)
+            fetch(term, 0, d, 0, V)
+            for g, (lo, hi) in enumerate(spans0):
+                pile(sum0[g], term, lo, hi, d == 0, d == 1 and g == 2)
+        backs = [turn_back(sum0[2], P, 4, "sum0_2")]
+        sum1 = [bank(g, "sum1_%d" % g) for g in range(2)]
+        for d in range(2):
+            term = sb("term1_%d" % d, [P, V], F32)
+            fetch(term, 1, d, 0, V)
+            for g, (lo, hi) in enumerate(spans1):
+                pile(sum1[g], term, lo, hi, d == 0, d == 1)
+        backs.extend(turn_back(sum1[g], hi - lo, 2 + g, "sum1_%d" % g) for g, (lo, hi) in enumerate(spans1))
+        last0 = sb("term0_2", [P, V], F32, tag="gate0")
+        for g, (lo, hi) in enumerate(spans0[:2]):
+            fetch(last0, 0, 2, lo, hi)
+            pile(sum0[g], last0, lo, hi, False, True)
+            back0 = turn_back(sum0[g], hi - lo, (7, 0)[g], "sum0_%d" % g)
+            res = sb("res0_%d" % g, [P, hi - lo], F32)
+            nc.scalar.activation(res[:], back0[:, : hi - lo], COPY)
+            nc.sync.dma_start(out=out[0:P, lo:hi], in_=res[:])
+        fetch(last0, 0, 2, *spans0[2])
+        last1 = sb("term1_2", [P, V], F32, tag="gate1")
+        for lo, hi in spans1:
+            fetch(last1, 1, 2, lo, hi)
+        ends = [(0, last0, spans0[2])] + [(1, last1, span) for span in spans1]
+        for g, (m, term, (lo, hi)) in enumerate(ends):
+            res = sb("res_end%d" % g, [P, hi - lo], F32)
+            nc.vector.tensor_tensor(res[:], backs[g][:, : hi - lo], term[:, lo:hi], ADD)
+            (nc.sync, nc.sync, nc.scalar)[g].dma_start(out=out[m * P : (m + 1) * P, lo:hi], in_=res[:])

@@ -56,11 +56,11 @@ def tile_picked_devox_relu_e_kernel(
             nc.sync.dma_start(out=w1_raw[:, 2 * u : 2 * u + 2, :], in_=w1_rows[:, 2 * u : 2 * u + 2, :])
         cell_sb = load_list("cell_sb", cell)
         emb_rows = emb.rearrange("(p t) r -> p t r", t=PACK)
-        emb_plane = {t: sb("emb_plane%d" % t, [P, U], F32) for t in (0, 3)}
         words = sb("words", [P, 2 * U], F32)
-        nc.sync.dma_start(out=emb_plane[0][:], in_=emb_rows[:, 0, :])
-        nc.sync.dma_start(out=words[:].rearrange("p (u r) -> p u r", u=2), in_=emb_rows[:, 1:3, :])
-        nc.sync.dma_start(out=emb_plane[3][:], in_=emb_rows[:, 3, :])
+        emb_plane = {t: sb("emb_plane%d" % t, [P, U], F32)[:] for t in (0, 1, 3)}
+        emb_plane[2] = words[:, U:]
+        for t in (1, 0, 2, 3):
+            nc.sync.dma_start(out=emb_plane[t], in_=emb_rows[:, t, :])
         w2_codes = sb("w2_codes", [P, N], I32)
         nc.sync.dma_start(out=w2_codes[:], in_=w2_words[0].rearrange("p n t -> p (n t)").bitcast(I32))
         w2_sc = sb("w2_sc", [P, N], U8)
@@ -120,7 +120,7 @@ def tile_picked_devox_relu_e_kernel(
         for t in (2, 3):
             quantize_w1(t)
 
-        steps = ((0, 0, (0, P)), (1, 1, (0, S)), (0, 0, (P, HALF, S)), (2, 2, (0, S)), (3, 2, (0, S)))
+        steps = ((0, 0, (0, P)), (1, 1, (0, S)), (0, 0, (P, HALF, S)), (2, 0, (0, S)), (3, 0, (0, S)))
         for i, (t, b, cuts) in enumerate(steps):
             acc = bank(b, "h_acc%d" % i)
             first, last = cuts[0], cuts[-1]
@@ -139,9 +139,8 @@ def tile_picked_devox_relu_e_kernel(
             nc.vector.tensor_copy(up[t][:].indirect(cell_sb[:, first // 16 : last // 16]), h[:])
 
         halves = words[:].bitcast(BF16).rearrange("p (u r e) -> p u r e", u=2, e=2)
-        nc.gpsimd.tensor_tensor(halves[:, 0, :, 1], up[1][:], words[:, :U], ADD)
-        nc.gpsimd.tensor_tensor(halves[:, 0, :, 0], up[0][:], emb_plane[0][:], ADD)
-        nc.gpsimd.tensor_tensor(halves[:, 1, :, 0], up[2][:], words[:, U:], ADD)
+        for t, lo, hi in ((1, 0, U), (0, 0, U), (2, 0, U // 2), (2, U // 2, U)):
+            nc.gpsimd.tensor_tensor(halves[:, t // 2, lo:hi, t % 2], up[t][:, lo:hi], emb_plane[t][:, lo:hi], ADD)
 
         cuts = (0, 128, 384, 640, 768, 1024)
         chunks = list(zip(cuts[:-1], cuts[1:]))
@@ -175,11 +174,11 @@ def tile_picked_devox_relu_e_kernel(
             nc.vector.quantize_mx(out=z_codes[c][:].bitcast(FP8X4), scales=z_sc[c][:], in_=z_bf[c][:])
             acc = bank(c, "y0_acc%d" % c)
             second_product(acc[:, : hi - lo], 0, c)
-            if c in (2,):
+            if c in (3,):
                 nc.vector.tensor_scalar_max(y[0][:, lo:hi], acc[:, : hi - lo], 0.0)
             else:
                 nc.scalar.activation(y[0][:, lo:hi], acc[:, : hi - lo], RELU)
-        for b, group in ((2, (0, 1)), (3, (2, 3)), (4, (4,))):
+        for b, group in ((1, (0, 1)), (4, (4,)), (2, (2, 3))):
             acc = bank(b, "y1_acc%d" % b)
             first, last = chunks[group[0]][0], chunks[group[-1]][1]
             for c in group:
@@ -215,14 +214,14 @@ def tile_picked_devox_relu_e_kernel(
             fetch(term, 0, d, 0, V)
             for g, (lo, hi) in enumerate(spans0):
                 pile(sum0[g], term, lo, hi, d == 0, d == 1 and g == 2)
-        backs = [turn_back(sum0[2], P, 4, "sum0_2")]
-        sum1 = [bank(g, "sum1_%d" % g) for g in range(2)]
+        backs = [turn_back(sum0[2], P, 1, "sum0_2")]
+        sum1 = [bank((0, 3)[g], "sum1_%d" % g) for g in range(2)]
         for d in range(2):
             term = sb("term1_%d" % d, [P, V], F32)
             fetch(term, 1, d, 0, V)
             for g, (lo, hi) in enumerate(spans1):
                 pile(sum1[g], term, lo, hi, d == 0, d == 1)
-        backs.extend(turn_back(sum1[g], hi - lo, 2 + g, "sum1_%d" % g) for g, (lo, hi) in enumerate(spans1))
+        backs.extend(turn_back(sum1[g], hi - lo, (4, 2)[g], "sum1_%d" % g) for g, (lo, hi) in enumerate(spans1))
         last0 = sb("term0_2", [P, V], F32, tag="gate0")
         for g, (lo, hi) in enumerate(spans0[:2]):
             fetch(last0, 0, 2, lo, hi)
@@ -239,4 +238,4 @@ def tile_picked_devox_relu_e_kernel(
         for g, (m, term, (lo, hi)) in enumerate(ends):
             res = sb("res_end%d" % g, [P, hi - lo], F32)
             nc.vector.tensor_tensor(res[:], backs[g][:, : hi - lo], term[:, lo:hi], ADD)
-            (nc.sync, nc.sync, nc.scalar)[g].dma_start(out=out[m * P : (m + 1) * P, lo:hi], in_=res[:])
+            nc.sync.dma_start(out=out[m * P : (m + 1) * P, lo:hi], in_=res[:])

@@ -29,6 +29,7 @@ def tile_picked_devox_relu_e_kernel(
     nc = tc.nc
     with ExitStack() as ctx:
         keep = ctx.enter_context(tc.tile_pool(name="keep", bufs=1))
+        shared = ctx.enter_context(tc.tile_pool(name="shared", bufs=1))
         psum = ctx.enter_context(tc.psum_pool(name="psum", bufs=1))
 
         def sb(name, shape, dtype, tag=None):
@@ -51,15 +52,18 @@ def tile_picked_devox_relu_e_kernel(
             if j == 0:
                 offs_sb = load_list("offs_sb", offs)
         w1_rows = w1.rearrange("(p j) c -> p j c", j=PACK)
-        w1_raw = sb("w1_raw", [P, PACK, H], F32)
-        for u in range(2):
-            nc.sync.dma_start(out=w1_raw[:, 2 * u : 2 * u + 2, :], in_=w1_rows[:, 2 * u : 2 * u + 2, :])
+        w1_raw = [sb("w1_raw%d" % s, [P, PACK, H // 2], F32) for s in range(2)]
+        nc.sync.dma_start(out=w1_raw[0][:], in_=w1_rows[:, :, : H // 2])
         cell_sb = load_list("cell_sb", cell)
+        nc.sync.dma_start(out=w1_raw[1][:], in_=w1_rows[:, :, H // 2 :])
         emb_rows = emb.rearrange("(p t) r -> p t r", t=PACK)
         words = sb("words", [P, 2 * U], F32)
         emb_plane = {t: sb("emb_plane%d" % t, [P, U], F32)[:] for t in (0, 1, 3)}
         emb_plane[2] = words[:, U:]
-        for t in (1, 0, 2, 3):
+        for t in range(2):
+            for e in range(2):
+                nc.sync.dma_start(out=emb_plane[t][e::2, :], in_=emb_rows[t * P // 2 : (t + 1) * P // 2, e, :])
+        for t in (2, 3):
             nc.sync.dma_start(out=emb_plane[t], in_=emb_rows[:, t, :])
         w2_codes = sb("w2_codes", [P, N], I32)
         nc.sync.dma_start(out=w2_codes[:], in_=w2_words[0].rearrange("p n t -> p (n t)").bitcast(I32))
@@ -83,66 +87,98 @@ def tile_picked_devox_relu_e_kernel(
             nc.vector.memset(up[t][:], 0.0)
 
         x_bf = [sb("x_bf%d" % s, [P, HALF, PACK], BF16) for s in range(2)]
-        x_codes = sb("x_codes", [P, S], U32)
-        x_sc = sb("x_sc", [P, S], U8)
         for j in range(PACK):
             for s in range(2):
                 entries = offs_sb[:, s * HALF // 16 : (s + 1) * HALF // 16]
                 nc.vector.tensor_copy(x_bf[s][:, :, j], x_plane[j][:].indirect(entries))
-        for s in range(2):
+        x_codes, x_sc = {}, {}
+
+        def quantize_x(s):
+            x_codes[s] = sb("x_codes%d" % s, [P, HALF], U32)
             nc.vector.quantize_mx(
-                out=x_codes[:, s * HALF : (s + 1) * HALF].bitcast(FP8X4),
-                scales=x_sc[:, s * HALF : (s + 1) * HALF],
-                in_=x_bf[s][:].rearrange("p n j -> p (n j)"),
+                out=x_codes[s][:].bitcast(FP8X4), scales=x_sc[s][:], in_=x_bf[s][:].rearrange("p n j -> p (n j)")
             )
 
-        w1_bf = {t: sb("w1_bf%d" % t, [P, P, PACK], BF16) for t in range(3)}
+        x_sc[0] = sb("x_sc0", [P, HALF], U8)
+        quantize_x(0)
+
+        w1_bf = {t: sb("w1_bf%d" % t, [P, P, PACK], BF16) for t in (2,)}
+        w1_bf[0] = shared.tile([P, P, PACK], BF16, name="w1_bf0", align_bytes=64, offset=0)
         w1_codes = [sb("w1_codes%d" % t, [P, P], U32) for t in range(PACK)]
         w1_sc = [sb("w1_sc%d" % t, [P, P], U8) for t in range(PACK)]
 
-        def deal(t, lo, hi):
-            return w1_bf[t][:, :, lo:hi], w1_raw[:, lo:hi, :].rearrange("p j (m t) -> p t m j", t=PACK)[:, t, :, :]
+        columns = [raw[:].rearrange("p j (q t) -> p q t j", t=PACK) for raw in w1_raw]
+
+        def deal_pairs(t):
+            return w1_bf[t][:].rearrange("p (q e) j -> p q e j", e=2), columns[t][:, :, 0:2, :]
+
+        def deal_single(t, s):
+            nc.scalar.activation(w1_bf[t][:, s * P // 2 : (s + 1) * P // 2, :], columns[s][:, :, t, :], COPY)
 
         def quantize_w1(t):
             nc.vector.quantize_mx(
                 out=w1_codes[t][:].bitcast(FP8X4), scales=w1_sc[t][:], in_=w1_bf[t][:].rearrange("p m j -> p (m j)")
             )
 
-        for t in (0, 1):
-            nc.scalar.activation(*deal(t, 0, 2), COPY)
-        for t in (0, 1):
-            nc.vector.tensor_copy(*deal(t, 2, PACK))
-        for t in (0, 1):
-            quantize_w1(t)
-        nc.scalar.activation(*deal(2, 0, PACK), COPY)
-        w1_bf[3] = sb("w1_bf3", [P, P, PACK], BF16, tag="w1_bf0")
-        nc.vector.tensor_copy(*deal(3, 0, PACK))
-        for t in (2, 3):
-            quantize_w1(t)
+        nc.scalar.activation(*deal_pairs(0), COPY)
+        quantize_w1(0)
+        x_sc[1] = shared.tile([P, HALF], U8, name="x_sc1", align_bytes=64, offset=0)
+        quantize_x(1)
+        w1_bf[1] = shared.tile([P, P, PACK], BF16, name="w1_bf1", align_bytes=64, offset=HALF)
+        nc.vector.tensor_copy(*deal_pairs(1))
+        quantize_w1(1)
+        for s in range(2):
+            deal_single(2, s)
+        quantize_w1(2)
 
-        steps = ((0, 0, (0, P)), (1, 1, (0, S)), (0, 0, (P, HALF, S)), (2, 0, (0, S)), (3, 0, (0, S)))
+        steps = ((0, 0, (0, P)), (0, 1, (P, HALF, S)), (1, 0, (0, HALF, S)), (2, 1, (0, HALF, S)), (3, 0, (0, HALF, S)))
         for i, (t, b, cuts) in enumerate(steps):
             acc = bank(b, "h_acc%d" % i)
             first, last = cuts[0], cuts[-1]
             for lo, hi in zip(cuts[:-1], cuts[1:]):
+                s = lo // HALF
                 nc.tensor.matmul_mx(
                     out=acc[:, lo - first : hi - first],
                     lhsT=w1_codes[t][:].bitcast(FP8X4),
                     lhsT_scale=w1_sc[t][:],
-                    rhs=x_codes[:, lo:hi].bitcast(FP8X4),
-                    rhs_scale=x_sc[:, lo:hi],
+                    rhs=x_codes[s][:, lo - s * HALF : hi - s * HALF].bitcast(FP8X4),
+                    rhs_scale=x_sc[s][:, lo - s * HALF : hi - s * HALF],
                     start=True,
                     stop=True,
                 )
-            h = sb("h%d" % i, [P, last - first], F32)
+            h = sb("h%d" % i, [P, last - first], F32, tag="w1_raw1" if t == 2 else None)
             nc.scalar.activation(h[:], acc[:, : last - first], RELU)
             nc.vector.tensor_copy(up[t][:].indirect(cell_sb[:, first // 16 : last // 16]), h[:])
+            if i == 0:
+                w1_bf[3] = sb("w1_bf3", [P, P, PACK], BF16, tag="h0")
+                for s in range(2):
+                    deal_single(3, s)
+                quantize_w1(3)
 
         halves = words[:].bitcast(BF16).rearrange("p (u r e) -> p u r e", u=2, e=2)
-        for t, lo, hi in ((1, 0, U), (0, 0, U), (2, 0, U // 2), (2, U // 2, U)):
-            nc.gpsimd.tensor_tensor(halves[:, t // 2, lo:hi, t % 2], up[t][:, lo:hi], emb_plane[t][:, lo:hi], ADD)
+        nc.gpsimd.tensor_tensor(halves[:, 1, :, 0], up[2][:], emb_plane[2], ADD)
 
-        cuts = (0, 128, 384, 640, 768, 1024)
+        def turn(dst, src, start, stop):
+            nc.tensor.matmul(dst, src, ident[:], start=start, stop=stop, is_transpose=True)
+
+        pair_acc = [bank(4 + c, "pair_acc%d" % c) for c in range(4)]
+        sources = (emb_plane[0], emb_plane[1], up[0][:], up[1][:])
+        for n, source in enumerate(sources):
+            for r in range(U // P):
+                o = (2 * (r % 2) + n % 2) * P
+                opens, closes = n == 0 and r % 2 == 0, n == 3 and r % 2 == 1
+                turn(pair_acc[r // 2][:, o : o + P], source[:, r * P : (r + 1) * P], opens, closes)
+        for g in range(2):
+            back = bank(2 + g, "pair_back%d" % g)
+            for i in range(2):
+                turned = sb("pair_t%d" % (2 * g + i), [P, BANK], BF16)
+                nc.scalar.activation(turned[:], pair_acc[2 * g + i][:], COPY)
+                for b in range(2):
+                    o = (2 * i + b) * P
+                    turn(back[:, o : o + P], turned[:].bitcast(F32)[:, b * P : (b + 1) * P], True, True)
+            nc.scalar.copy(words[:, g * BANK : (g + 1) * BANK], back[:])
+
+        cuts = (0, 128, 384, 640, 896, 1024)
         chunks = list(zip(cuts[:-1], cuts[1:]))
         z_bf = [sb("z_bf%d" % c, [P, (hi - lo) * PACK], BF16) for c, (lo, hi) in enumerate(chunks)]
         z_codes = [sb("z_codes%d" % c, [P, hi - lo], U32) for c, (lo, hi) in enumerate(chunks)]
@@ -150,8 +186,7 @@ def tile_picked_devox_relu_e_kernel(
         pairs = words[:].rearrange("p (u r) -> p u r", u=2)
         for c, (lo, hi) in enumerate(chunks):
             nc.vector.tensor_tensor(halves[:, 1, lo:hi, 1], up[3][:, lo:hi], emb_plane[3][:, lo:hi], ADD)
-            weave = nc.vector.tensor_copy if c == len(chunks) - 1 else nc.scalar.copy
-            weave(
+            nc.scalar.copy(
                 z_bf[c][:].bitcast(F32).rearrange("p (g i u) -> p g u i", i=4, u=2),
                 pairs[:, :, lo:hi].rearrange("p u (g i) -> p g u i", i=4),
             )
@@ -169,25 +204,21 @@ def tile_picked_devox_relu_e_kernel(
                 stop=True,
             )
 
-        for c in (0, 1, 4, 2, 3):
-            lo, hi = chunks[c]
+        for c, (lo, hi) in enumerate(chunks):
             nc.vector.quantize_mx(out=z_codes[c][:].bitcast(FP8X4), scales=z_sc[c][:], in_=z_bf[c][:])
             acc = bank(c, "y0_acc%d" % c)
             second_product(acc[:, : hi - lo], 0, c)
-            if c in (3,):
+            if c == len(chunks) - 1:
                 nc.vector.tensor_scalar_max(y[0][:, lo:hi], acc[:, : hi - lo], 0.0)
             else:
                 nc.scalar.activation(y[0][:, lo:hi], acc[:, : hi - lo], RELU)
-        for b, group in ((1, (0, 1)), (4, (4,)), (2, (2, 3))):
+        for b, group in ((1, (0, 1)), (2, (2,)), (3, (3, 4))):
             acc = bank(b, "y1_acc%d" % b)
             first, last = chunks[group[0]][0], chunks[group[-1]][1]
             for c in group:
                 lo, hi = chunks[c]
                 second_product(acc[:, lo - first : hi - first], 1, c)
             nc.scalar.activation(y[1][:, first:last], acc[:, : last - first], RELU)
-
-        def turn(dst, src, start, stop):
-            nc.tensor.matmul(dst, src, ident[:], start=start, stop=stop, is_transpose=True)
 
         def fetch(term, m, d, lo, hi):
             nc.vector.tensor_tensor(
@@ -215,13 +246,13 @@ def tile_picked_devox_relu_e_kernel(
             for g, (lo, hi) in enumerate(spans0):
                 pile(sum0[g], term, lo, hi, d == 0, d == 1 and g == 2)
         backs = [turn_back(sum0[2], P, 1, "sum0_2")]
-        sum1 = [bank((0, 3)[g], "sum1_%d" % g) for g in range(2)]
+        sum1 = [bank((0, 4)[g], "sum1_%d" % g) for g in range(2)]
         for d in range(2):
             term = sb("term1_%d" % d, [P, V], F32)
             fetch(term, 1, d, 0, V)
             for g, (lo, hi) in enumerate(spans1):
                 pile(sum1[g], term, lo, hi, d == 0, d == 1)
-        backs.extend(turn_back(sum1[g], hi - lo, (4, 2)[g], "sum1_%d" % g) for g, (lo, hi) in enumerate(spans1))
+        backs.extend(turn_back(sum1[g], hi - lo, (2, 3)[g], "sum1_%d" % g) for g, (lo, hi) in enumerate(spans1))
         last0 = sb("term0_2", [P, V], F32, tag="gate0")
         for g, (lo, hi) in enumerate(spans0[:2]):
             fetch(last0, 0, 2, lo, hi)

@@ -187,8 +187,8 @@ def tile_picked_devox_relu_e_kernel(
         for c, (lo, hi) in enumerate(chunks):
             nc.vector.tensor_tensor(halves[:, 1, lo:hi, 1], up[3][:, lo:hi], emb_plane[3][:, lo:hi], ADD)
             nc.scalar.copy(
-                z_bf[c][:].bitcast(F32).rearrange("p (g i u) -> p g u i", i=4, u=2),
-                pairs[:, :, lo:hi].rearrange("p u (g i) -> p g u i", i=4),
+                z_bf[c][:].bitcast(F32).rearrange("p (r u) -> p r u", u=2),
+                pairs[:, :, lo:hi].rearrange("p u r -> p r u"),
             )
 
         y = [sb("y0", [P, U], F32, tag="words"), sb("y1", [P, U], F32)]

@@ -53,7 +53,8 @@ def tile_picked_devox_relu_e_kernel(
                 offs_sb = load_list("offs_sb", offs)
         w1_rows = w1.rearrange("(p j) c -> p j c", j=PACK)
         w1_raw = [sb("w1_raw%d" % s, [P, PACK, H // 2], F32) for s in range(2)]
-        nc.sync.dma_start(out=w1_raw[0][:], in_=w1_rows[:, :, : H // 2])
+        for u in range(2):
+            nc.sync.dma_start(out=w1_raw[0][:, 2 * u : 2 * u + 2, :], in_=w1_rows[:, 2 * u : 2 * u + 2, : H // 2])
         cell_sb = load_list("cell_sb", cell)
         nc.sync.dma_start(out=w1_raw[1][:], in_=w1_rows[:, :, H // 2 :])
         emb_rows = emb.rearrange("(p t) r -> p t r", t=PACK)
@@ -82,9 +83,11 @@ def tile_picked_devox_relu_e_kernel(
         ident = sb("ident", [P, P], F32)
         make_identity(nc, ident[:])
 
-        up = [sb("up%d" % t, [P, U], F32) for t in range(PACK)]
-        for t in range(PACK):
+        up = [sb("up%d" % t, [P, U], F32) for t in range(PACK + 1)]
+        for t in (PACK, 0):
             nc.vector.memset(up[t][:], 0.0)
+        for t in (1, 2, 3):
+            nc.gpsimd.memset(up[t][:], 0.0)
 
         x_bf = [sb("x_bf%d" % s, [P, HALF, PACK], BF16) for s in range(2)]
         for j in range(PACK):
@@ -93,14 +96,17 @@ def tile_picked_devox_relu_e_kernel(
                 nc.vector.tensor_copy(x_bf[s][:, :, j], x_plane[j][:].indirect(entries))
         x_codes, x_sc = {}, {}
 
-        def quantize_x(s):
-            x_codes[s] = sb("x_codes%d" % s, [P, HALF], U32)
+        def quantize_x(lo, hi):
+            s = lo // HALF
+            x_codes[lo] = sb("x_codes%d" % lo, [P, hi - lo], U32)
             nc.vector.quantize_mx(
-                out=x_codes[s][:].bitcast(FP8X4), scales=x_sc[s][:], in_=x_bf[s][:].rearrange("p n j -> p (n j)")
+                out=x_codes[lo][:].bitcast(FP8X4),
+                scales=x_sc[lo][:],
+                in_=x_bf[s][:, lo - s * HALF : hi - s * HALF, :].rearrange("p n j -> p (n j)"),
             )
 
-        x_sc[0] = sb("x_sc0", [P, HALF], U8)
-        quantize_x(0)
+        x_sc[0] = sb("x_sc0", [P, P], U8)
+        quantize_x(0, P)
 
         w1_bf = {t: sb("w1_bf%d" % t, [P, P, PACK], BF16) for t in (2,)}
         w1_bf[0] = shared.tile([P, P, PACK], BF16, name="w1_bf0", align_bytes=64, offset=0)
@@ -120,35 +126,38 @@ def tile_picked_devox_relu_e_kernel(
                 out=w1_codes[t][:].bitcast(FP8X4), scales=w1_sc[t][:], in_=w1_bf[t][:].rearrange("p m j -> p (m j)")
             )
 
-        nc.scalar.activation(*deal_pairs(0), COPY)
+        dst, src = deal_pairs(0)
+        for u in range(2):
+            nc.scalar.activation(dst[:, :, :, 2 * u : 2 * u + 2], src[:, :, :, 2 * u : 2 * u + 2], COPY)
         quantize_w1(0)
-        x_sc[1] = shared.tile([P, HALF], U8, name="x_sc1", align_bytes=64, offset=0)
-        quantize_x(1)
-        w1_bf[1] = shared.tile([P, P, PACK], BF16, name="w1_bf1", align_bytes=64, offset=HALF)
+        for lo, hi in ((P, HALF), (HALF, S)):
+            x_sc[lo] = shared.tile([P, hi - lo], U8, name="x_sc%d" % lo, align_bytes=64, offset=lo)
+            quantize_x(lo, hi)
+        w1_bf[1] = shared.tile([P, P, PACK], BF16, name="w1_bf1", align_bytes=64, offset=S)
         nc.vector.tensor_copy(*deal_pairs(1))
         quantize_w1(1)
         for s in range(2):
             deal_single(2, s)
         quantize_w1(2)
 
-        steps = ((0, 0, (0, P)), (0, 1, (P, HALF, S)), (1, 0, (0, HALF, S)), (2, 1, (0, HALF, S)), (3, 0, (0, HALF, S)))
+        whole = (0, P, HALF, S)
+        steps = ((0, 0, (0, P)), (0, 1, (P, HALF, S)), (1, 0, whole), (2, 1, whole), (3, 0, whole))
         for i, (t, b, cuts) in enumerate(steps):
             acc = bank(b, "h_acc%d" % i)
             first, last = cuts[0], cuts[-1]
             for lo, hi in zip(cuts[:-1], cuts[1:]):
-                s = lo // HALF
                 nc.tensor.matmul_mx(
                     out=acc[:, lo - first : hi - first],
                     lhsT=w1_codes[t][:].bitcast(FP8X4),
                     lhsT_scale=w1_sc[t][:],
-                    rhs=x_codes[s][:, lo - s * HALF : hi - s * HALF].bitcast(FP8X4),
-                    rhs_scale=x_sc[s][:, lo - s * HALF : hi - s * HALF],
+                    rhs=x_codes[lo][:].bitcast(FP8X4),
+                    rhs_scale=x_sc[lo][:],
                     start=True,
                     stop=True,
                 )
             h = sb("h%d" % i, [P, last - first], F32, tag="w1_raw1" if t == 2 else None)
             nc.scalar.activation(h[:], acc[:, : last - first], RELU)
-            nc.vector.tensor_copy(up[t][:].indirect(cell_sb[:, first // 16 : last // 16]), h[:])
+            nc.vector.tensor_copy(up[PACK if i == 0 else t][:].indirect(cell_sb[:, first // 16 : last // 16]), h[:])
             if i == 0:
                 w1_bf[3] = sb("w1_bf3", [P, P, PACK], BF16, tag="h0")
                 for s in range(2):
@@ -162,11 +171,11 @@ def tile_picked_devox_relu_e_kernel(
             nc.tensor.matmul(dst, src, ident[:], start=start, stop=stop, is_transpose=True)
 
         pair_acc = [bank(4 + c, "pair_acc%d" % c) for c in range(4)]
-        sources = (emb_plane[0], emb_plane[1], up[0][:], up[1][:])
-        for n, source in enumerate(sources):
+        sources = ((0, emb_plane[0]), (1, emb_plane[1]), (0, up[PACK][:]), (0, up[0][:]), (1, up[1][:]))
+        for n, (t, source) in enumerate(sources):
             for r in range(U // P):
-                o = (2 * (r % 2) + n % 2) * P
-                opens, closes = n == 0 and r % 2 == 0, n == 3 and r % 2 == 1
+                o = (2 * (r % 2) + t) * P
+                opens, closes = n == 0 and r % 2 == 0, n == len(sources) - 1 and r % 2 == 1
                 turn(pair_acc[r // 2][:, o : o + P], source[:, r * P : (r + 1) * P], opens, closes)
         for g in range(2):
             back = bank(2 + g, "pair_back%d" % g)

@@ -58,14 +58,15 @@ def tile_picked_devox_relu_e_kernel(
         cell_sb = load_list("cell_sb", cell)
         nc.sync.dma_start(out=w1_raw[1][:], in_=w1_rows[:, :, H // 2 :])
         emb_rows = emb.rearrange("(p t) r -> p t r", t=PACK)
-        words = sb("words", [P, 2 * U], F32)
+        parts = ((0, 768), (768, U))
+        words = [sb("words%d" % n, [P, 2 * (hi - lo)], F32) for n, (lo, hi) in enumerate(parts)]
         emb_plane = {t: sb("emb_plane%d" % t, [P, U], F32)[:] for t in (0, 1, 3)}
-        emb_plane[2] = words[:, U:]
         for t in range(2):
             for e in range(2):
                 nc.sync.dma_start(out=emb_plane[t][e::2, :], in_=emb_rows[t * P // 2 : (t + 1) * P // 2, e, :])
-        for t in (2, 3):
-            nc.sync.dma_start(out=emb_plane[t], in_=emb_rows[:, t, :])
+        for n, (lo, hi) in enumerate(parts):
+            nc.sync.dma_start(out=words[n][:, hi - lo :], in_=emb_rows[:, 2, lo:hi])
+        nc.sync.dma_start(out=emb_plane[3], in_=emb_rows[:, 3, :])
         w2_codes = sb("w2_codes", [P, N], I32)
         nc.sync.dma_start(out=w2_codes[:], in_=w2_words[0].rearrange("p n t -> p (n t)").bitcast(I32))
         w2_sc = sb("w2_sc", [P, N], U8)
@@ -164,11 +165,25 @@ def tile_picked_devox_relu_e_kernel(
                     deal_single(3, s)
                 quantize_w1(3)
 
-        halves = words[:].bitcast(BF16).rearrange("p (u r e) -> p u r e", u=2, e=2)
-        nc.gpsimd.tensor_tensor(halves[:, 1, :, 0], up[2][:], emb_plane[2], ADD)
+        halves = [part[:].bitcast(BF16).rearrange("p (u r e) -> p u r e", u=2, e=2) for part in words]
+        for n in (1, 0):
+            lo, hi = parts[n]
+            nc.gpsimd.tensor_tensor(halves[n][:, 1, :, 0], up[2][:, lo:hi], words[n][:, hi - lo :], ADD)
 
         def turn(dst, src, start, stop):
             nc.tensor.matmul(dst, src, ident[:], start=start, stop=stop, is_transpose=True)
+
+        emb_psum = []
+        for g in range(2):
+            flipped = bank(2 + g, "emb_flip%d" % g)
+            for b in range(3):
+                o = (3 * g + b) * P
+                turn(flipped[:, b * P : (b + 1) * P], emb_plane[3][:, o : o + P], True, True)
+            staged = sb("emb_t%d" % g, [P, 3 * P], F32)
+            nc.scalar.copy(staged[:], flipped[:, : 3 * P])
+            emb_psum.append(bank(g, "emb_back%d" % g))
+            for b in range(3):
+                turn(emb_psum[g][:, b * P : (b + 1) * P], staged[:, b * P : (b + 1) * P], True, True)
 
         pair_acc = [bank(4 + c, "pair_acc%d" % c) for c in range(4)]
         sources = ((0, emb_plane[0]), (1, emb_plane[1]), (0, up[PACK][:]), (0, up[0][:]), (1, up[1][:]))
@@ -177,7 +192,7 @@ def tile_picked_devox_relu_e_kernel(
                 o = (2 * (r % 2) + t) * P
                 opens, closes = n == 0 and r % 2 == 0, n == len(sources) - 1 and r % 2 == 1
                 turn(pair_acc[r // 2][:, o : o + P], source[:, r * P : (r + 1) * P], opens, closes)
-        for g in range(2):
+        for g in (1, 0):
             back = bank(2 + g, "pair_back%d" % g)
             for i in range(2):
                 turned = sb("pair_t%d" % (2 * g + i), [P, BANK], BF16)
@@ -185,22 +200,44 @@ def tile_picked_devox_relu_e_kernel(
                 for b in range(2):
                     o = (2 * i + b) * P
                     turn(back[:, o : o + P], turned[:].bitcast(F32)[:, b * P : (b + 1) * P], True, True)
-            nc.scalar.copy(words[:, g * BANK : (g + 1) * BANK], back[:])
+            if g == 0:
+                nc.scalar.copy(words[0][:, :BANK], back[:])
+            else:
+                nc.scalar.copy(words[1][:, :256], back[:, 256:])
+                nc.scalar.copy(words[0][:, BANK:768], back[:, :256])
 
-        cuts = (0, 128, 384, 640, 896, 1024)
+        cuts = (0, 128, 384, 640, 768, 1024)
         chunks = list(zip(cuts[:-1], cuts[1:]))
-        z_bf = [sb("z_bf%d" % c, [P, (hi - lo) * PACK], BF16) for c, (lo, hi) in enumerate(chunks)]
-        z_codes = [sb("z_codes%d" % c, [P, hi - lo], U32) for c, (lo, hi) in enumerate(chunks)]
+        z_bf = [
+            sb("z_bf%d" % c, [P, (hi - lo) * PACK], BF16, tag="pair_t1" if c == 3 else None)
+            for c, (lo, hi) in enumerate(chunks)
+        ]
+        z_codes = {c: sb("z_codes%d" % c, [P, hi - lo], U32) for c, (lo, hi) in enumerate(chunks[:4])}
         z_sc = [sb("z_sc%d" % c, [P, hi - lo], U8) for c, (lo, hi) in enumerate(chunks)]
-        pairs = words[:].rearrange("p (u r) -> p u r", u=2)
-        for c, (lo, hi) in enumerate(chunks):
-            nc.vector.tensor_tensor(halves[:, 1, lo:hi, 1], up[3][:, lo:hi], emb_plane[3][:, lo:hi], ADD)
+        pairs = [part[:].rearrange("p (u r) -> p u r", u=2) for part in words]
+
+        def weave(c):
+            lo, hi = chunks[c]
+            n = lo // 768
             nc.scalar.copy(
                 z_bf[c][:].bitcast(F32).rearrange("p (r u) -> p r u", u=2),
-                pairs[:, :, lo:hi].rearrange("p u r -> p r u"),
+                pairs[n][:, :, lo - 768 * n : hi - 768 * n].rearrange("p u r -> p r u"),
             )
 
-        y = [sb("y0", [P, U], F32, tag="words"), sb("y1", [P, U], F32)]
+        lo, hi = chunks[4]
+        weave(4)
+        nc.gpsimd.tensor_tensor(
+            z_bf[4][:].rearrange("p (r t) -> p r t", t=PACK)[:, :, 3], up[3][:, lo:hi], emb_plane[3][:, lo:hi], ADD
+        )
+        for c, (lo, hi) in enumerate(chunks[:4]):
+            g = lo // 384
+            nc.vector.tensor_tensor(
+                halves[0][:, 1, lo:hi, 1], up[3][:, lo:hi], emb_psum[g][:, lo - 384 * g : hi - 384 * g], ADD
+            )
+            weave(c)
+
+        z_codes[4] = sb("z_codes4", [P, 256], U32, tag="up3")
+        y = [sb("y0", [P, U], F32, tag="words0"), sb("y1", [P, U], F32)]
 
         def second_product(acc, m, c):
             nc.tensor.matmul_mx(
@@ -213,15 +250,16 @@ def tile_picked_devox_relu_e_kernel(
                 stop=True,
             )
 
-        for c, (lo, hi) in enumerate(chunks):
+        for c in (0, 4, 1, 2, 3):
+            lo, hi = chunks[c]
             nc.vector.quantize_mx(out=z_codes[c][:].bitcast(FP8X4), scales=z_sc[c][:], in_=z_bf[c][:])
-            acc = bank(c, "y0_acc%d" % c)
+            acc = bank(2 + c, "y0_acc%d" % c)
             second_product(acc[:, : hi - lo], 0, c)
-            if c == len(chunks) - 1:
+            if c == 3:
                 nc.vector.tensor_scalar_max(y[0][:, lo:hi], acc[:, : hi - lo], 0.0)
             else:
                 nc.scalar.activation(y[0][:, lo:hi], acc[:, : hi - lo], RELU)
-        for b, group in ((1, (0, 1)), (2, (2,)), (3, (3, 4))):
+        for b, group in ((3, (4,)), (4, (0, 1)), (5, (2, 3))):
             acc = bank(b, "y1_acc%d" % b)
             first, last = chunks[group[0]][0], chunks[group[-1]][1]
             for c in group:
@@ -248,25 +286,25 @@ def tile_picked_devox_relu_e_kernel(
 
         spans0 = ((0, 256), (256, 384), (384, 512))
         spans1 = ((0, 256), (256, 512))
-        sum0 = [bank((5, 6, 7)[g], "sum0_%d" % g) for g in range(3)]
+        sum0 = [bank((0, 1, 7)[g], "sum0_%d" % g) for g in range(3)]
         for d in range(2):
             term = sb("term0_%d" % d, [P, V], F32)
             fetch(term, 0, d, 0, V)
             for g, (lo, hi) in enumerate(spans0):
                 pile(sum0[g], term, lo, hi, d == 0, d == 1 and g == 2)
-        backs = [turn_back(sum0[2], P, 1, "sum0_2")]
-        sum1 = [bank((0, 4)[g], "sum1_%d" % g) for g in range(2)]
+        backs = [turn_back(sum0[2], P, 3, "sum0_2")]
+        sum1 = [bank((2, 6)[g], "sum1_%d" % g) for g in range(2)]
         for d in range(2):
             term = sb("term1_%d" % d, [P, V], F32)
             fetch(term, 1, d, 0, V)
             for g, (lo, hi) in enumerate(spans1):
                 pile(sum1[g], term, lo, hi, d == 0, d == 1)
-        backs.extend(turn_back(sum1[g], hi - lo, (2, 3)[g], "sum1_%d" % g) for g, (lo, hi) in enumerate(spans1))
+        backs.extend(turn_back(sum1[g], hi - lo, (4, 5)[g], "sum1_%d" % g) for g, (lo, hi) in enumerate(spans1))
         last0 = sb("term0_2", [P, V], F32, tag="gate0")
         for g, (lo, hi) in enumerate(spans0[:2]):
             fetch(last0, 0, 2, lo, hi)
             pile(sum0[g], last0, lo, hi, False, True)
-            back0 = turn_back(sum0[g], hi - lo, (7, 0)[g], "sum0_%d" % g)
+            back0 = turn_back(sum0[g], hi - lo, (7, 2)[g], "sum0_%d" % g)
             res = sb("res0_%d" % g, [P, hi - lo], F32)
             nc.scalar.activation(res[:], back0[:, : hi - lo], COPY)
             nc.sync.dma_start(out=out[0:P, lo:hi], in_=res[:])

@@ -58,7 +58,7 @@ def tile_picked_devox_relu_e_kernel(
         cell_sb = load_list("cell_sb", cell)
         nc.sync.dma_start(out=w1_raw[1][:], in_=w1_rows[:, :, H // 2 :])
         emb_rows = emb.rearrange("(p t) r -> p t r", t=PACK)
-        parts = ((0, 768), (768, U))
+        parts = ((0, 896), (896, U))
         words = [sb("words%d" % n, [P, 2 * (hi - lo)], F32) for n, (lo, hi) in enumerate(parts)]
         emb_plane = {t: sb("emb_plane%d" % t, [P, U], F32)[:] for t in (0, 1, 3)}
         for t in range(2):
@@ -166,7 +166,7 @@ def tile_picked_devox_relu_e_kernel(
                 quantize_w1(3)
 
         halves = [part[:].bitcast(BF16).rearrange("p (u r e) -> p u r e", u=2, e=2) for part in words]
-        for n in (1, 0):
+        for n in range(2):
             lo, hi = parts[n]
             nc.gpsimd.tensor_tensor(halves[n][:, 1, :, 0], up[2][:, lo:hi], words[n][:, hi - lo :], ADD)
 
@@ -176,13 +176,13 @@ def tile_picked_devox_relu_e_kernel(
         emb_psum = []
         for g in range(2):
             flipped = bank(2 + g, "emb_flip%d" % g)
-            for b in range(3):
+            for b in range(3 + g):
                 o = (3 * g + b) * P
                 turn(flipped[:, b * P : (b + 1) * P], emb_plane[3][:, o : o + P], True, True)
-            staged = sb("emb_t%d" % g, [P, 3 * P], F32)
-            nc.scalar.copy(staged[:], flipped[:, : 3 * P])
+            staged = sb("emb_t%d" % g, [P, (3 + g) * P], F32)
+            nc.scalar.copy(staged[:], flipped[:, : (3 + g) * P])
             emb_psum.append(bank(g, "emb_back%d" % g))
-            for b in range(3):
+            for b in range(3 + g):
                 turn(emb_psum[g][:, b * P : (b + 1) * P], staged[:, b * P : (b + 1) * P], True, True)
 
         pair_acc = [bank(4 + c, "pair_acc%d" % c) for c in range(4)]
@@ -203,40 +203,40 @@ def tile_picked_devox_relu_e_kernel(
             if g == 0:
                 nc.scalar.copy(words[0][:, :BANK], back[:])
             else:
-                nc.scalar.copy(words[1][:, :256], back[:, 256:])
-                nc.scalar.copy(words[0][:, BANK:768], back[:, :256])
+                nc.scalar.copy(words[1][:, :P], back[:, 384:])
+                nc.scalar.copy(words[0][:, BANK:896], back[:, :384])
 
-        cuts = (0, 128, 384, 640, 768, 1024)
+        cuts = (0, 128, 384, 640, 768, 896, 1024)
         chunks = list(zip(cuts[:-1], cuts[1:]))
         z_bf = [
-            sb("z_bf%d" % c, [P, (hi - lo) * PACK], BF16, tag="pair_t1" if c == 3 else None)
+            sb("z_bf%d" % c, [P, (hi - lo) * PACK], BF16, tag={3: "pair_t1", 4: "pair_t0"}.get(c))
             for c, (lo, hi) in enumerate(chunks)
         ]
-        z_codes = {c: sb("z_codes%d" % c, [P, hi - lo], U32) for c, (lo, hi) in enumerate(chunks[:4])}
+        z_codes = {c: sb("z_codes%d" % c, [P, hi - lo], U32) for c, (lo, hi) in enumerate(chunks[:5])}
         z_sc = [sb("z_sc%d" % c, [P, hi - lo], U8) for c, (lo, hi) in enumerate(chunks)]
         pairs = [part[:].rearrange("p (u r) -> p u r", u=2) for part in words]
 
         def weave(c):
             lo, hi = chunks[c]
-            n = lo // 768
+            n = lo // 896
             nc.scalar.copy(
                 z_bf[c][:].bitcast(F32).rearrange("p (r u) -> p r u", u=2),
-                pairs[n][:, :, lo - 768 * n : hi - 768 * n].rearrange("p u r -> p r u"),
+                pairs[n][:, :, lo - 896 * n : hi - 896 * n].rearrange("p u r -> p r u"),
             )
 
-        lo, hi = chunks[4]
-        weave(4)
+        lo, hi = chunks[5]
+        weave(5)
         nc.gpsimd.tensor_tensor(
-            z_bf[4][:].rearrange("p (r t) -> p r t", t=PACK)[:, :, 3], up[3][:, lo:hi], emb_plane[3][:, lo:hi], ADD
+            z_bf[5][:].rearrange("p (r t) -> p r t", t=PACK)[:, :, 3], up[3][:, lo:hi], emb_plane[3][:, lo:hi], ADD
         )
-        for c, (lo, hi) in enumerate(chunks[:4]):
-            g = lo // 384
+        for c, (lo, hi) in enumerate(chunks[:5]):
+            g = min(lo // 384, 1)
             nc.vector.tensor_tensor(
                 halves[0][:, 1, lo:hi, 1], up[3][:, lo:hi], emb_psum[g][:, lo - 384 * g : hi - 384 * g], ADD
             )
             weave(c)
 
-        z_codes[4] = sb("z_codes4", [P, 256], U32, tag="up3")
+        z_codes[5] = sb("z_codes5", [P, P], U32, tag="up3")
         y = [sb("y0", [P, U], F32, tag="words0"), sb("y1", [P, U], F32)]
 
         def second_product(acc, m, c):
@@ -250,16 +250,16 @@ def tile_picked_devox_relu_e_kernel(
                 stop=True,
             )
 
-        for c in (0, 4, 1, 2, 3):
+        for c in (0, 5, 1, 2, 3, 4):
             lo, hi = chunks[c]
             nc.vector.quantize_mx(out=z_codes[c][:].bitcast(FP8X4), scales=z_sc[c][:], in_=z_bf[c][:])
             acc = bank(2 + c, "y0_acc%d" % c)
             second_product(acc[:, : hi - lo], 0, c)
-            if c == 3:
+            if c == 4:
                 nc.vector.tensor_scalar_max(y[0][:, lo:hi], acc[:, : hi - lo], 0.0)
             else:
                 nc.scalar.activation(y[0][:, lo:hi], acc[:, : hi - lo], RELU)
-        for b, group in ((3, (4,)), (4, (0, 1)), (5, (2, 3))):
+        for b, group in ((4, (0, 1)), (5, (2, 3)), (6, (4, 5))):
             acc = bank(b, "y1_acc%d" % b)
             first, last = chunks[group[0]][0], chunks[group[-1]][1]
             for c in group:
@@ -292,14 +292,14 @@ def tile_picked_devox_relu_e_kernel(
             fetch(term, 0, d, 0, V)
             for g, (lo, hi) in enumerate(spans0):
                 pile(sum0[g], term, lo, hi, d == 0, d == 1 and g == 2)
-        backs = [turn_back(sum0[2], P, 3, "sum0_2")]
-        sum1 = [bank((2, 6)[g], "sum1_%d" % g) for g in range(2)]
+        backs = [turn_back(sum0[2], P, 4, "sum0_2")]
+        sum1 = [bank((2, 3)[g], "sum1_%d" % g) for g in range(2)]
         for d in range(2):
             term = sb("term1_%d" % d, [P, V], F32)
             fetch(term, 1, d, 0, V)
             for g, (lo, hi) in enumerate(spans1):
                 pile(sum1[g], term, lo, hi, d == 0, d == 1)
-        backs.extend(turn_back(sum1[g], hi - lo, (4, 5)[g], "sum1_%d" % g) for g, (lo, hi) in enumerate(spans1))
+        backs.extend(turn_back(sum1[g], hi - lo, (5, 6)[g], "sum1_%d" % g) for g, (lo, hi) in enumerate(spans1))
         last0 = sb("term0_2", [P, V], F32, tag="gate0")
         for g, (lo, hi) in enumerate(spans0[:2]):
             fetch(last0, 0, 2, lo, hi)

@@ -269,51 +269,61 @@ def tile_picked_devox_relu_e_kernel(
 
         def fetch(term, m, d, lo, hi):
             nc.vector.tensor_tensor(
-                term[:, lo:hi], y[m][:].indirect(pos_sb[d][:, lo // 16 : hi // 16]), gate_sb[d][:, lo:hi], MULT
+                term, y[m][:].indirect(pos_sb[d][:, lo // 16 : hi // 16]), gate_sb[d][:, lo:hi], MULT
             )
 
         def pile(acc, term, lo, hi, first, last):
             for o in range(lo, hi, P):
                 turn(acc[:, o - lo : o - lo + P], term[:, o : o + P], first and o == lo, last and o + P == hi)
 
+        TURNED = 4096
+
         def turn_back(acc, width, b, name):
-            turned = sb(name + "_t", [P, width], F32)
+            turned = shared.tile([P, width], F32, name=name + "_t", align_bytes=64, offset=TURNED + b * BANK * 4)
             nc.scalar.activation(turned[:], acc[:, :width], COPY)
             back = bank(b, name + "_back")
             for o in range(0, width, P):
                 turn(back[:, o : o + P], turned[:, o : o + P], True, True)
             return back
 
-        spans0 = ((0, 256), (256, 384), (384, 512))
-        spans1 = ((0, 256), (256, 512))
-        sum0 = [bank((0, 1, 7)[g], "sum0_%d" % g) for g in range(3)]
-        for d in range(2):
-            term = sb("term0_%d" % d, [P, V], F32)
-            fetch(term, 0, d, 0, V)
-            for g, (lo, hi) in enumerate(spans0):
-                pile(sum0[g], term, lo, hi, d == 0, d == 1 and g == 2)
-        backs = [turn_back(sum0[2], P, 4, "sum0_2")]
-        sum1 = [bank((2, 3)[g], "sum1_%d" % g) for g in range(2)]
-        for d in range(2):
-            term = sb("term1_%d" % d, [P, V], F32)
-            fetch(term, 1, d, 0, V)
-            for g, (lo, hi) in enumerate(spans1):
-                pile(sum1[g], term, lo, hi, d == 0, d == 1)
-        backs.extend(turn_back(sum1[g], hi - lo, (5, 6)[g], "sum1_%d" % g) for g, (lo, hi) in enumerate(spans1))
-        last0 = sb("term0_2", [P, V], F32, tag="gate0")
-        for g, (lo, hi) in enumerate(spans0[:2]):
-            fetch(last0, 0, 2, lo, hi)
-            pile(sum0[g], last0, lo, hi, False, True)
-            back0 = turn_back(sum0[g], hi - lo, (7, 2)[g], "sum0_%d" % g)
-            res = sb("res0_%d" % g, [P, hi - lo], F32)
-            nc.scalar.activation(res[:], back0[:, : hi - lo], COPY)
-            nc.sync.dma_start(out=out[0:P, lo:hi], in_=res[:])
-        fetch(last0, 0, 2, *spans0[2])
-        last1 = sb("term1_2", [P, V], F32, tag="gate1")
-        for lo, hi in spans1:
-            fetch(last1, 1, 2, lo, hi)
-        ends = [(0, last0, spans0[2])] + [(1, last1, span) for span in spans1]
-        for g, (m, term, (lo, hi)) in enumerate(ends):
+        spans = ((0, 0, V), (1, 0, 256), (1, 256, V))
+        sums = [bank(g, "sum%d" % g) for g in range(len(spans))]
+        backs = []
+        for m in range(2):
+            for d in range(2):
+                term = sb("term%d_%d" % (m, d), [P, V], F32)
+                if d == 0:
+                    fetch(term[:], m, d, 0, V)
+                for g, (rows, lo, hi) in enumerate(spans):
+                    if rows == m:
+                        if d == 1:
+                            fetch(term[:, lo:hi], m, d, lo, hi)
+                        pile(sums[g], term, lo, hi, d == 0, d == 1)
+                        if d == 1:
+                            backs.append(turn_back(sums[g], hi - lo, (4, 5, 6)[g], "sum%d" % g))
+
+        ends = (
+            (0, 0, 256, backs[0][:, :256], None),
+            (0, 256, V, backs[0][:, 256:], None),
+            (1, 0, 256, backs[1][:, :256], TURNED + 4 * BANK * 4),
+            (1, 256, 384, backs[2][:, :P], TURNED + 4 * BANK * 4 + 1024),
+            (1, 384, V, backs[2][:, P : 2 * P], TURNED + 5 * BANK * 4),
+        )
+        last0 = sb("last0", [P, V], F32, tag="gate0")
+        lasts = []
+
+        def finish(g):
+            m, lo, hi, partial, tag = ends[g]
             res = sb("res_end%d" % g, [P, hi - lo], F32)
-            nc.vector.tensor_tensor(res[:], backs[g][:, : hi - lo], term[:, lo:hi], ADD)
+            nc.vector.tensor_tensor(res[:], partial, lasts[g][:], ADD)
             nc.sync.dma_start(out=out[m * P : (m + 1) * P, lo:hi], in_=res[:])
+
+        for g, (m, lo, hi, partial, tag) in enumerate(ends):
+            if m == 0:
+                lasts.append(last0[:, lo:hi])
+            else:
+                lasts.append(shared.tile([P, hi - lo], F32, name="last%d" % g, align_bytes=64, offset=tag))
+            fetch(lasts[g][:], m, 2, lo, hi)
+            if g > 0:
+                finish(g - 1)
+        finish(len(ends) - 1)

@@ -20,6 +20,12 @@ P = 128
 PACK = 4
 HALF = S // 2
 BANK = 512
+BANK_BYTES = 4 * BANK
+FIFTH = PACK
+SPLIT = 896
+CELL_CUTS = (0, 128, 384, 640, 768, SPLIT, U)
+EMB_CUT = 384
+LAST = 64
 FLOPS = 2 * K * H * S + 2 * H * N * U
 
 
@@ -34,6 +40,9 @@ def tile_picked_devox_relu_e_kernel(
 
         def sb(name, shape, dtype, tag=None):
             return keep.tile(shape, dtype, name=name, tag=tag or name, align_bytes=64)
+
+        def placed(name, shape, dtype, offset):
+            return shared.tile(shape, dtype, name=name, align_bytes=64, offset=offset)
 
         def bank(b, name):
             return psum.tile([P, BANK], F32, name=name, tag="bank%d" % b)
@@ -55,10 +64,10 @@ def tile_picked_devox_relu_e_kernel(
         w1_raw = [sb("w1_raw%d" % s, [P, PACK, H // 2], F32) for s in range(2)]
         for u in range(2):
             nc.sync.dma_start(out=w1_raw[0][:, 2 * u : 2 * u + 2, :], in_=w1_rows[:, 2 * u : 2 * u + 2, : H // 2])
-        cell_sb = load_list("cell_sb", cell)
         nc.sync.dma_start(out=w1_raw[1][:], in_=w1_rows[:, :, H // 2 :])
+        cell_sb = load_list("cell_sb", cell)
         emb_rows = emb.rearrange("(p t) r -> p t r", t=PACK)
-        parts = ((0, 896), (896, U))
+        parts = ((0, SPLIT), (SPLIT, U))
         words = [sb("words%d" % n, [P, 2 * (hi - lo)], F32) for n, (lo, hi) in enumerate(parts)]
         emb_plane = {t: sb("emb_plane%d" % t, [P, U], F32)[:] for t in (0, 1, 3)}
         for t in range(2):
@@ -85,7 +94,7 @@ def tile_picked_devox_relu_e_kernel(
         make_identity(nc, ident[:])
 
         up = [sb("up%d" % t, [P, U], F32) for t in range(PACK + 1)]
-        for t in (PACK, 0):
+        for t in (FIFTH, 0):
             nc.vector.memset(up[t][:], 0.0)
         for t in (1, 2, 3):
             nc.gpsimd.memset(up[t][:], 0.0)
@@ -95,101 +104,93 @@ def tile_picked_devox_relu_e_kernel(
             for s in range(2):
                 entries = offs_sb[:, s * HALF // 16 : (s + 1) * HALF // 16]
                 nc.vector.tensor_copy(x_bf[s][:, :, j], x_plane[j][:].indirect(entries))
-        x_codes, x_sc = {}, {}
+        x_codes, x_sc = [], []
 
-        def quantize_x(lo, hi):
-            s = lo // HALF
-            x_codes[lo] = sb("x_codes%d" % lo, [P, hi - lo], U32)
+        def quantize_x(s, scales):
+            x_codes.append(sb("x_codes%d" % s, [P, HALF], U32))
+            x_sc.append(scales)
             nc.vector.quantize_mx(
-                out=x_codes[lo][:].bitcast(FP8X4),
-                scales=x_sc[lo][:],
-                in_=x_bf[s][:, lo - s * HALF : hi - s * HALF, :].rearrange("p n j -> p (n j)"),
+                out=x_codes[s][:].bitcast(FP8X4), scales=scales[:], in_=x_bf[s][:].rearrange("p n j -> p (n j)")
             )
 
-        x_sc[0] = sb("x_sc0", [P, P], U8)
-        quantize_x(0, P)
+        quantize_x(0, sb("x_sc0", [P, HALF], U8))
 
-        w1_bf = {t: sb("w1_bf%d" % t, [P, P, PACK], BF16) for t in (2,)}
-        w1_bf[0] = shared.tile([P, P, PACK], BF16, name="w1_bf0", align_bytes=64, offset=0)
+        w1_bf = {2: sb("w1_bf2", [P, P, PACK], BF16), 0: placed("w1_bf0", [P, P, PACK], BF16, 0)}
         w1_codes = [sb("w1_codes%d" % t, [P, P], U32) for t in range(PACK)]
         w1_sc = [sb("w1_sc%d" % t, [P, P], U8) for t in range(PACK)]
-
         columns = [raw[:].rearrange("p j (q t) -> p q t j", t=PACK) for raw in w1_raw]
 
-        def deal_pairs(t):
-            return w1_bf[t][:].rearrange("p (q e) j -> p q e j", e=2), columns[t][:, :, 0:2, :]
+        def pair_views(s):
+            return w1_bf[s][:].rearrange("p (q e) j -> p q e j", e=2), columns[s][:, :, 0:2, :]
 
-        def deal_single(t, s):
-            nc.scalar.activation(w1_bf[t][:, s * P // 2 : (s + 1) * P // 2, :], columns[s][:, :, t, :], COPY)
+        def deal_plane(t):
+            for s in range(2):
+                nc.scalar.activation(w1_bf[t][:, s * P // 2 : (s + 1) * P // 2, :], columns[s][:, :, t, :], COPY)
 
         def quantize_w1(t):
             nc.vector.quantize_mx(
                 out=w1_codes[t][:].bitcast(FP8X4), scales=w1_sc[t][:], in_=w1_bf[t][:].rearrange("p m j -> p (m j)")
             )
 
-        dst, src = deal_pairs(0)
+        dst, src = pair_views(0)
         for u in range(2):
             nc.scalar.activation(dst[:, :, :, 2 * u : 2 * u + 2], src[:, :, :, 2 * u : 2 * u + 2], COPY)
         quantize_w1(0)
-        for lo, hi in ((P, HALF), (HALF, S)):
-            x_sc[lo] = shared.tile([P, hi - lo], U8, name="x_sc%d" % lo, align_bytes=64, offset=lo)
-            quantize_x(lo, hi)
-        w1_bf[1] = shared.tile([P, P, PACK], BF16, name="w1_bf1", align_bytes=64, offset=S)
-        nc.vector.tensor_copy(*deal_pairs(1))
+        quantize_x(1, placed("x_sc1", [P, HALF], U8, HALF))
+        w1_bf[1] = placed("w1_bf1", [P, P, PACK], BF16, S)
+        nc.vector.tensor_copy(*pair_views(1))
         quantize_w1(1)
-        for s in range(2):
-            deal_single(2, s)
+        deal_plane(2)
         quantize_w1(2)
 
-        whole = (0, P, HALF, S)
-        steps = ((0, 0, (0, P)), (0, 1, (P, HALF, S)), (1, 0, whole), (2, 1, whole), (3, 0, whole))
-        for i, (t, b, cuts) in enumerate(steps):
+        whole = (0, HALF, S)
+        steps = ((0, 0, (0, P), FIFTH), (0, 1, (P, HALF, S), 0), (1, 0, whole, 1), (2, 1, whole, 2), (3, 0, whole, 3))
+        for i, (t, b, cuts, window) in enumerate(steps):
             acc = bank(b, "h_acc%d" % i)
             first, last = cuts[0], cuts[-1]
             for lo, hi in zip(cuts[:-1], cuts[1:]):
+                s = lo // HALF
+                picked = slice(lo - s * HALF, hi - s * HALF)
                 nc.tensor.matmul_mx(
                     out=acc[:, lo - first : hi - first],
                     lhsT=w1_codes[t][:].bitcast(FP8X4),
                     lhsT_scale=w1_sc[t][:],
-                    rhs=x_codes[lo][:].bitcast(FP8X4),
-                    rhs_scale=x_sc[lo][:],
+                    rhs=x_codes[s][:, picked].bitcast(FP8X4),
+                    rhs_scale=x_sc[s][:, picked],
                     start=True,
                     stop=True,
                 )
             h = sb("h%d" % i, [P, last - first], F32, tag="w1_raw1" if t == 2 else None)
             nc.scalar.activation(h[:], acc[:, : last - first], RELU)
-            nc.vector.tensor_copy(up[PACK if i == 0 else t][:].indirect(cell_sb[:, first // 16 : last // 16]), h[:])
-            if i == 0:
+            nc.vector.tensor_copy(up[window][:].indirect(cell_sb[:, first // 16 : last // 16]), h[:])
+            if window == FIFTH:
                 w1_bf[3] = sb("w1_bf3", [P, P, PACK], BF16, tag="h0")
-                for s in range(2):
-                    deal_single(3, s)
+                deal_plane(3)
                 quantize_w1(3)
 
         halves = [part[:].bitcast(BF16).rearrange("p (u r e) -> p u r e", u=2, e=2) for part in words]
-        for n in range(2):
-            lo, hi = parts[n]
+        for n, (lo, hi) in enumerate(parts):
             nc.gpsimd.tensor_tensor(halves[n][:, 1, :, 0], up[2][:, lo:hi], words[n][:, hi - lo :], ADD)
 
         def turn(dst, src, start, stop):
             nc.tensor.matmul(dst, src, ident[:], start=start, stop=stop, is_transpose=True)
 
         emb_psum = []
-        for g in range(2):
+        for g, (lo, hi) in enumerate(((0, EMB_CUT), (EMB_CUT, SPLIT))):
             flipped = bank(2 + g, "emb_flip%d" % g)
-            for b in range(3 + g):
-                o = (3 * g + b) * P
-                turn(flipped[:, b * P : (b + 1) * P], emb_plane[3][:, o : o + P], True, True)
-            staged = sb("emb_t%d" % g, [P, (3 + g) * P], F32)
-            nc.scalar.copy(staged[:], flipped[:, : (3 + g) * P])
+            for o in range(0, hi - lo, P):
+                turn(flipped[:, o : o + P], emb_plane[3][:, lo + o : lo + o + P], True, True)
+            staged = sb("emb_t%d" % g, [P, hi - lo], F32)
+            nc.scalar.copy(staged[:], flipped[:, : hi - lo])
             emb_psum.append(bank(g, "emb_back%d" % g))
-            for b in range(3 + g):
-                turn(emb_psum[g][:, b * P : (b + 1) * P], staged[:, b * P : (b + 1) * P], True, True)
+            for o in range(0, hi - lo, P):
+                turn(emb_psum[g][:, o : o + P], staged[:, o : o + P], True, True)
 
         pair_acc = [bank(4 + c, "pair_acc%d" % c) for c in range(4)]
-        sources = ((0, emb_plane[0]), (1, emb_plane[1]), (0, up[PACK][:]), (0, up[0][:]), (1, up[1][:]))
-        for n, (t, source) in enumerate(sources):
+        sources = ((0, emb_plane[0]), (1, emb_plane[1]), (0, up[FIFTH][:]), (0, up[0][:]), (1, up[1][:]))
+        for n, (s, source) in enumerate(sources):
             for r in range(U // P):
-                o = (2 * (r % 2) + t) * P
+                o = (2 * (r % 2) + s) * P
                 opens, closes = n == 0 and r % 2 == 0, n == len(sources) - 1 and r % 2 == 1
                 turn(pair_acc[r // 2][:, o : o + P], source[:, r * P : (r + 1) * P], opens, closes)
         for g in (1, 0):
@@ -203,40 +204,38 @@ def tile_picked_devox_relu_e_kernel(
             if g == 0:
                 nc.scalar.copy(words[0][:, :BANK], back[:])
             else:
-                nc.scalar.copy(words[1][:, :P], back[:, 384:])
-                nc.scalar.copy(words[0][:, BANK:896], back[:, :384])
+                nc.scalar.copy(words[1][:, : U - SPLIT], back[:, SPLIT - BANK :])
+                nc.scalar.copy(words[0][:, BANK:SPLIT], back[:, : SPLIT - BANK])
 
-        cuts = (0, 128, 384, 640, 768, 896, 1024)
-        chunks = list(zip(cuts[:-1], cuts[1:]))
-        z_bf = [
-            sb("z_bf%d" % c, [P, (hi - lo) * PACK], BF16, tag={3: "pair_t1", 4: "pair_t0"}.get(c))
-            for c, (lo, hi) in enumerate(chunks)
-        ]
-        z_codes = {c: sb("z_codes%d" % c, [P, hi - lo], U32) for c, (lo, hi) in enumerate(chunks[:5])}
+        chunks = list(zip(CELL_CUTS[:-1], CELL_CUTS[1:]))
+        side = len(chunks) - 1
+        reused = {side - 2: "pair_t1", side - 1: "pair_t0"}
+        z_bf = [sb("z_bf%d" % c, [P, (hi - lo) * PACK], BF16, tag=reused.get(c)) for c, (lo, hi) in enumerate(chunks)]
+        z_codes = {c: sb("z_codes%d" % c, [P, hi - lo], U32) for c, (lo, hi) in enumerate(chunks[:side])}
         z_sc = [sb("z_sc%d" % c, [P, hi - lo], U8) for c, (lo, hi) in enumerate(chunks)]
         pairs = [part[:].rearrange("p (u r) -> p u r", u=2) for part in words]
 
         def weave(c):
             lo, hi = chunks[c]
-            n = lo // 896
+            n = lo // SPLIT
             nc.scalar.copy(
                 z_bf[c][:].bitcast(F32).rearrange("p (r u) -> p r u", u=2),
-                pairs[n][:, :, lo - 896 * n : hi - 896 * n].rearrange("p u r -> p r u"),
+                pairs[n][:, :, lo - SPLIT * n : hi - SPLIT * n].rearrange("p u r -> p r u"),
             )
 
-        lo, hi = chunks[5]
-        weave(5)
+        lo, hi = chunks[side]
+        weave(side)
         nc.gpsimd.tensor_tensor(
-            z_bf[5][:].rearrange("p (r t) -> p r t", t=PACK)[:, :, 3], up[3][:, lo:hi], emb_plane[3][:, lo:hi], ADD
+            z_bf[side][:].rearrange("p (r t) -> p r t", t=PACK)[:, :, 3], up[3][:, lo:hi], emb_plane[3][:, lo:hi], ADD
         )
-        for c, (lo, hi) in enumerate(chunks[:5]):
-            g = min(lo // 384, 1)
+        for c, (lo, hi) in enumerate(chunks[:side]):
+            g = min(lo // EMB_CUT, 1)
             nc.vector.tensor_tensor(
-                halves[0][:, 1, lo:hi, 1], up[3][:, lo:hi], emb_psum[g][:, lo - 384 * g : hi - 384 * g], ADD
+                halves[0][:, 1, lo:hi, 1], up[3][:, lo:hi], emb_psum[g][:, lo - EMB_CUT * g : hi - EMB_CUT * g], ADD
             )
             weave(c)
 
-        z_codes[5] = sb("z_codes5", [P, P], U32, tag="up3")
+        z_codes[side] = sb("z_codes%d" % side, [P, U - SPLIT], U32, tag="up3")
         y = [sb("y0", [P, U], F32, tag="words0"), sb("y1", [P, U], F32)]
 
         def second_product(acc, m, c):
@@ -250,19 +249,19 @@ def tile_picked_devox_relu_e_kernel(
                 stop=True,
             )
 
-        for c in (0, 5, 1, 2, 3, 4):
+        for c in [0, side] + list(range(1, side)):
             lo, hi = chunks[c]
             nc.vector.quantize_mx(out=z_codes[c][:].bitcast(FP8X4), scales=z_sc[c][:], in_=z_bf[c][:])
             acc = bank(2 + c, "y0_acc%d" % c)
             second_product(acc[:, : hi - lo], 0, c)
-            if c == 4:
+            if c == side - 1:
                 nc.vector.tensor_scalar_max(y[0][:, lo:hi], acc[:, : hi - lo], 0.0)
             else:
                 nc.scalar.activation(y[0][:, lo:hi], acc[:, : hi - lo], RELU)
-        for b, group in ((4, (0, 1)), (5, (2, 3)), (6, (4, 5))):
-            acc = bank(b, "y1_acc%d" % b)
-            first, last = chunks[group[0]][0], chunks[group[-1]][1]
-            for c in group:
+        for i in range(len(chunks) // 2):
+            acc = bank(4 + i, "y1_acc%d" % (4 + i))
+            first, last = chunks[2 * i][0], chunks[2 * i + 1][1]
+            for c in (2 * i, 2 * i + 1):
                 lo, hi = chunks[c]
                 second_product(acc[:, lo - first : hi - first], 1, c)
             nc.scalar.activation(y[1][:, first:last], acc[:, : last - first], RELU)
@@ -276,54 +275,48 @@ def tile_picked_devox_relu_e_kernel(
             for o in range(lo, hi, P):
                 turn(acc[:, o - lo : o - lo + P], term[:, o : o + P], first and o == lo, last and o + P == hi)
 
-        TURNED = 4096
+        def turned_at(b):
+            return (2 + b) * BANK_BYTES
 
         def turn_back(acc, width, b, name):
-            turned = shared.tile([P, width], F32, name=name + "_t", align_bytes=64, offset=TURNED + b * BANK * 4)
-            nc.scalar.activation(turned[:], acc[:, :width], COPY)
+            turned_sum = placed(name + "_t", [P, width], F32, turned_at(b))
+            nc.scalar.activation(turned_sum[:], acc[:, :width], COPY)
             back = bank(b, name + "_back")
             for o in range(0, width, P):
-                turn(back[:, o : o + P], turned[:, o : o + P], True, True)
+                turn(back[:, o : o + P], turned_sum[:, o : o + P], True, True)
             return back
 
-        spans = ((0, 0, V), (1, 0, 256), (1, 256, V))
+        def finish(m, lo, hi, partial, term):
+            res = sb("res%d_%d" % (m, lo), [P, hi - lo], F32)
+            nc.vector.tensor_tensor(res[:], partial, term, ADD)
+            nc.sync.dma_start(out=out[m * P : (m + 1) * P, lo:hi], in_=res[:])
+
+        spans = ((0, 0, V), (1, 0, V // 2), (1, V // 2, V))
         sums = [bank(g, "sum%d" % g) for g in range(len(spans))]
         backs = []
         for m in range(2):
-            for d in range(2):
-                term = sb("term%d_%d" % (m, d), [P, V], F32)
-                if d == 0:
-                    fetch(term[:], m, d, 0, V)
-                for g, (rows, lo, hi) in enumerate(spans):
-                    if rows == m:
-                        if d == 1:
-                            fetch(term[:, lo:hi], m, d, lo, hi)
-                        pile(sums[g], term, lo, hi, d == 0, d == 1)
-                        if d == 1:
-                            backs.append(turn_back(sums[g], hi - lo, (4, 5, 6)[g], "sum%d" % g))
+            first_term = sb("term%d_0" % m, [P, V], F32)
+            fetch(first_term[:], m, 0, 0, V)
+            own = [(g, lo, hi) for g, (rows, lo, hi) in enumerate(spans) if rows == m]
+            for g, lo, hi in own:
+                pile(sums[g], first_term, lo, hi, True, False)
+            second_term = sb("term%d_1" % m, [P, V], F32)
+            for g, lo, hi in own:
+                fetch(second_term[:, lo:hi], m, 1, lo, hi)
+                pile(sums[g], second_term, lo, hi, False, True)
+                backs.append(turn_back(sums[g], hi - lo, 4 + g, "sum%d" % g))
 
-        ends = (
-            (0, 0, 256, backs[0][:, :256], None),
-            (0, 256, V, backs[0][:, 256:], None),
-            (1, 0, 256, backs[1][:, :256], TURNED + 4 * BANK * 4),
-            (1, 256, 384, backs[2][:, :P], TURNED + 4 * BANK * 4 + 1024),
-            (1, 384, V, backs[2][:, P : 2 * P], TURNED + 5 * BANK * 4),
-        )
+        mid, tail = V // 2, V - LAST
         last0 = sb("last0", [P, V], F32, tag="gate0")
-        lasts = []
-
-        def finish(g):
-            m, lo, hi, partial, tag = ends[g]
-            res = sb("res_end%d" % g, [P, hi - lo], F32)
-            nc.vector.tensor_tensor(res[:], partial, lasts[g][:], ADD)
-            nc.sync.dma_start(out=out[m * P : (m + 1) * P, lo:hi], in_=res[:])
-
-        for g, (m, lo, hi, partial, tag) in enumerate(ends):
-            if m == 0:
-                lasts.append(last0[:, lo:hi])
-            else:
-                lasts.append(shared.tile([P, hi - lo], F32, name="last%d" % g, align_bytes=64, offset=tag))
-            fetch(lasts[g][:], m, 2, lo, hi)
-            if g > 0:
-                finish(g - 1)
-        finish(len(ends) - 1)
+        fetch(last0[:], 0, 2, 0, V)
+        last1 = [sb("last1_0", [P, mid], F32, tag="gate1")]
+        fetch(last1[0][:], 1, 2, 0, mid)
+        for lo in (0, mid):
+            finish(0, lo, lo + mid, backs[0][:, lo : lo + mid], last0[:, lo : lo + mid])
+        last1.append(placed("last1_1", [P, tail - mid], F32, turned_at(4)))
+        fetch(last1[1][:], 1, 2, mid, tail)
+        finish(1, 0, mid, backs[1][:, :mid], last1[0][:])
+        last1.append(placed("last1_2", [P, LAST], F32, turned_at(5)))
+        fetch(last1[2][:], 1, 2, tail, V)
+        finish(1, mid, tail, backs[2][:, : tail - mid], last1[1][:])
+        finish(1, tail, V, backs[2][:, tail - mid : mid], last1[2][:])

@@ -20,13 +20,11 @@ P = 128
 PACK = 4
 HALF = S // 2
 BANK = 512
-BANK_BYTES = 4 * BANK
-FIFTH = PACK
-SPLIT = 896
-CELL_CUTS = (0, 128, 384, 640, 768, SPLIT, U)
-EMB_CUT = 384
-LAST = 64
 FLOPS = 2 * K * H * S + 2 * H * N * U
+CHUNK = 256
+FIRST = 128
+SIDE = U - CHUNK
+RAW = (384, 256)
 
 
 def tile_picked_devox_relu_e_kernel(
@@ -53,29 +51,26 @@ def tile_picked_devox_relu_e_kernel(
             return tile
 
         x_rows = xT.rearrange("(p j) t -> p j t", j=PACK)
-        x_plane = []
-        for j in range(PACK):
-            plane = sb("x_plane%d" % j, [P, T], F32)
-            nc.sync.dma_start(out=plane[:], in_=x_rows[:, j, :])
-            x_plane.append(plane)
-            if j == 0:
-                offs_sb = load_list("offs_sb", offs)
-        w1_rows = w1.rearrange("(p j) c -> p j c", j=PACK)
+        x_plane = [sb("x_plane%d" % j, [P, T], F32) for j in range(PACK)]
         w1_raw = [sb("w1_raw%d" % s, [P, PACK, H // 2], F32) for s in range(2)]
-        for u in range(2):
-            nc.sync.dma_start(out=w1_raw[0][:, 2 * u : 2 * u + 2, :], in_=w1_rows[:, 2 * u : 2 * u + 2, : H // 2])
-        nc.sync.dma_start(out=w1_raw[1][:], in_=w1_rows[:, :, H // 2 :])
-        cell_sb = load_list("cell_sb", cell)
+        nc.sync.dma_start(out=x_plane[0][:], in_=x_rows[:, 0, :])
+        offs_sb = load_list("offs_sb", offs)
+        for j in range(1, PACK):
+            nc.sync.dma_start(out=x_plane[j][:], in_=x_rows[:, j, :])
+        w1_rows = w1.rearrange("(p j) c -> p j c", j=PACK)
+        for s in range(2):
+            nc.sync.dma_start(out=w1_raw[s][:], in_=w1_rows[:, :, s * H // 2 : (s + 1) * H // 2])
+            if s == 0:
+                cell_sb = load_list("cell_sb", cell)
         emb_rows = emb.rearrange("(p t) r -> p t r", t=PACK)
-        parts = ((0, SPLIT), (SPLIT, U))
-        words = [sb("words%d" % n, [P, 2 * (hi - lo)], F32) for n, (lo, hi) in enumerate(parts)]
-        emb_plane = {t: sb("emb_plane%d" % t, [P, U], F32)[:] for t in (0, 1, 3)}
-        for t in range(2):
+        emb_sb = [sb("emb%d" % t, [P, U if t < 2 else SIDE], F32) for t in range(PACK)]
+        emb_top = sb("emb_top", [P, 2, CHUNK], F32)
+        for s in range(2):
             for e in range(2):
-                nc.sync.dma_start(out=emb_plane[t][e::2, :], in_=emb_rows[t * P // 2 : (t + 1) * P // 2, e, :])
-        for n, (lo, hi) in enumerate(parts):
-            nc.sync.dma_start(out=words[n][:, hi - lo :], in_=emb_rows[:, 2, lo:hi])
-        nc.sync.dma_start(out=emb_plane[3], in_=emb_rows[:, 3, :])
+                nc.sync.dma_start(out=emb_sb[s][e::2, :], in_=emb_rows[s * P // 2 : (s + 1) * P // 2, e, :])
+        nc.sync.dma_start(out=emb_top[:], in_=emb_rows[:, 2:, SIDE:])
+        for t in (3, 2):
+            nc.sync.dma_start(out=emb_sb[t][:], in_=emb_rows[:, t, :SIDE])
         w2_codes = sb("w2_codes", [P, N], I32)
         nc.sync.dma_start(out=w2_codes[:], in_=w2_words[0].rearrange("p n t -> p (n t)").bitcast(I32))
         w2_sc = sb("w2_sc", [P, N], U8)
@@ -85,158 +80,158 @@ def tile_picked_devox_relu_e_kernel(
                 out=w2_sc[32 * q : 32 * q + 4, :].bitcast(I32),
                 in_=w2_scales[0, 4 * q : 4 * q + 4, :].bitcast(I32),
             )
-        gate_sb = [sb("gate%d" % d, [P, V], F32) for d in range(D)]
-        for d in range(D):
-            nc.sync.dma_start(out=gate_sb[d][:], in_=gate[d])
         pos_sb = [load_list("pos%d_sb" % d, src) for d, src in enumerate((pos1, pos2, pos3))]
+        fused_from = RAW + (0,)
+        gate_sb = [sb("gate%d" % d, [P, V - fused_from[d]], F32) for d in range(D)]
+        for d in range(D):
+            nc.sync.dma_start(out=gate_sb[d][:], in_=gate[d][:, fused_from[d] :])
+        gate_col = [sb("gate_col%d" % d, [P, RAW[d] // P], F32) for d in range(2)]
+        with nc.allow_non_contiguous_dma(reason="one gate value a partition"):
+            for d in range(2):
+                nc.sync.dma_start(out=gate_col[d][:], in_=gate[d, 0, : RAW[d]].rearrange("(b p) -> p b", p=P))
 
         ident = sb("ident", [P, P], F32)
         make_identity(nc, ident[:])
 
-        up = [sb("up%d" % t, [P, U], F32) for t in range(PACK + 1)]
-        for t in (FIFTH, 0):
+        up = [sb("up%d" % t, [P, U], F32) for t in range(PACK)]
+        for t in (0, 1):
             nc.vector.memset(up[t][:], 0.0)
-        for t in (1, 2, 3):
+        for t in (2, 3):
             nc.gpsimd.memset(up[t][:], 0.0)
 
         x_bf = [sb("x_bf%d" % s, [P, HALF, PACK], BF16) for s in range(2)]
+        entries = [offs_sb[:, s * HALF // 16 : (s + 1) * HALF // 16] for s in range(2)]
+        x_late = sb("x_late", [P, 2 * HALF], BF16)
         for j in range(PACK):
-            for s in range(2):
-                entries = offs_sb[:, s * HALF // 16 : (s + 1) * HALF // 16]
-                nc.vector.tensor_copy(x_bf[s][:, :, j], x_plane[j][:].indirect(entries))
-        x_codes, x_sc = [], []
+            nc.vector.tensor_copy(x_bf[0][:, :, j], x_plane[j][:].indirect(entries[0]))
+            if j < 2:
+                nc.vector.tensor_copy(x_bf[1][:, :, j], x_plane[j][:].indirect(entries[1]))
+            else:
+                nc.scalar.activation(
+                    x_late[:, (j - 2) * HALF : (j - 1) * HALF], x_plane[j][:].indirect(entries[1]), COPY
+                )
+        nc.scalar.activation(x_bf[1][:, :, 2:], x_late[:].rearrange("p (e n) -> p n e", e=2), COPY)
+        x_codes = [sb("x_codes%d" % s, [P, HALF], U32) for s in range(2)]
+        x_sc = [sb("x_sc%d" % s, [P, HALF], U8) for s in range(2)]
 
-        def quantize_x(s, scales):
-            x_codes.append(sb("x_codes%d" % s, [P, HALF], U32))
-            x_sc.append(scales)
+        def quantize_x(s):
             nc.vector.quantize_mx(
-                out=x_codes[s][:].bitcast(FP8X4), scales=scales[:], in_=x_bf[s][:].rearrange("p n j -> p (n j)")
+                out=x_codes[s][:].bitcast(FP8X4), scales=x_sc[s][:], in_=x_bf[s][:].rearrange("p n j -> p (n j)")
             )
 
-        quantize_x(0, sb("x_sc0", [P, HALF], U8))
+        columns = [raw[:].rearrange("p j (q t) -> p q j t", t=PACK) for raw in w1_raw]
+        w1_codes, w1_sc = {}, {}
 
-        w1_bf = {2: sb("w1_bf2", [P, P, PACK], BF16), 0: placed("w1_bf0", [P, P, PACK], BF16, 0)}
-        w1_codes = [sb("w1_codes%d" % t, [P, P], U32) for t in range(PACK)]
-        w1_sc = [sb("w1_sc%d" % t, [P, P], U8) for t in range(PACK)]
-        columns = [raw[:].rearrange("p j (q t) -> p q t j", t=PACK) for raw in w1_raw]
+        def quantize_w1(ts, dealt):
+            codes = sb("w1_codes%d" % ts[0], [P, len(ts) * P], U32)
+            scales = sb("w1_sc%d" % ts[0], [P, len(ts) * P], U8)
+            nc.vector.quantize_mx(out=codes[:].bitcast(FP8X4), scales=scales[:], in_=dealt[:])
+            for i, t in enumerate(ts):
+                w1_codes[t], w1_sc[t] = codes[:, i * P : (i + 1) * P], scales[:, i * P : (i + 1) * P]
 
-        def pair_views(s):
-            return w1_bf[s][:].rearrange("p (q e) j -> p q e j", e=2), columns[s][:, :, 0:2, :]
+        quantize_x(0)
+        for s in range(2):
+            dealt = sb("w1_bf%d" % s, [P, P * PACK], BF16)
+            nc.vector.tensor_copy(dealt[:].rearrange("p (q e j) -> p q j e", e=2, j=PACK), columns[s][:, :, :, 0:2])
+            if s == 1:
+                quantize_x(1)
+            quantize_w1((s,), dealt)
+        dealt = sb("w1_bf2", [P, 2 * P * PACK], BF16)
+        halves = dealt[:].rearrange("p (e s q j) -> p s q j e", e=2, s=2, j=PACK)
+        for s in range(2):
+            nc.scalar.activation(halves[:, s], columns[s][:, :, :, 2:], COPY)
+        quantize_w1((2, 3), dealt)
 
-        def deal_plane(t):
-            for s in range(2):
-                nc.scalar.activation(w1_bf[t][:, s * P // 2 : (s + 1) * P // 2, :], columns[s][:, :, t, :], COPY)
-
-        def quantize_w1(t):
-            nc.vector.quantize_mx(
-                out=w1_codes[t][:].bitcast(FP8X4), scales=w1_sc[t][:], in_=w1_bf[t][:].rearrange("p m j -> p (m j)")
-            )
-
-        dst, src = pair_views(0)
-        for u in range(2):
-            nc.scalar.activation(dst[:, :, :, 2 * u : 2 * u + 2], src[:, :, :, 2 * u : 2 * u + 2], COPY)
-        quantize_w1(0)
-        quantize_x(1, placed("x_sc1", [P, HALF], U8, HALF))
-        w1_bf[1] = placed("w1_bf1", [P, P, PACK], BF16, S)
-        nc.vector.tensor_copy(*pair_views(1))
-        quantize_w1(1)
-        deal_plane(2)
-        quantize_w1(2)
-
-        whole = (0, HALF, S)
-        steps = ((0, 0, (0, P), FIFTH), (0, 1, (P, HALF, S), 0), (1, 0, whole, 1), (2, 1, whole, 2), (3, 0, whole, 3))
-        for i, (t, b, cuts, window) in enumerate(steps):
-            acc = bank(b, "h_acc%d" % i)
-            first, last = cuts[0], cuts[-1]
+        def first_product(acc, t, first, last):
+            cuts = sorted({first, min(max(HALF, first), last), last})
             for lo, hi in zip(cuts[:-1], cuts[1:]):
                 s = lo // HALF
                 picked = slice(lo - s * HALF, hi - s * HALF)
                 nc.tensor.matmul_mx(
                     out=acc[:, lo - first : hi - first],
-                    lhsT=w1_codes[t][:].bitcast(FP8X4),
-                    lhsT_scale=w1_sc[t][:],
+                    lhsT=w1_codes[t].bitcast(FP8X4),
+                    lhsT_scale=w1_sc[t],
                     rhs=x_codes[s][:, picked].bitcast(FP8X4),
                     rhs_scale=x_sc[s][:, picked],
                     start=True,
                     stop=True,
                 )
-            h = sb("h%d" % i, [P, last - first], F32, tag="w1_raw1" if t == 2 else None)
-            nc.scalar.activation(h[:], acc[:, : last - first], RELU)
-            nc.vector.tensor_copy(up[window][:].indirect(cell_sb[:, first // 16 : last // 16]), h[:])
-            if window == FIFTH:
-                w1_bf[3] = sb("w1_bf3", [P, P, PACK], BF16, tag="h0")
-                deal_plane(3)
-                quantize_w1(3)
 
-        halves = [part[:].bitcast(BF16).rearrange("p (u r e) -> p u r e", u=2, e=2) for part in words]
-        for n, (lo, hi) in enumerate(parts):
-            nc.gpsimd.tensor_tensor(halves[n][:, 1, :, 0], up[2][:, lo:hi], words[n][:, hi - lo :], ADD)
+        def places(t, lo, hi):
+            return up[t][:].indirect(cell_sb[:, lo // 16 : hi // 16])
 
         def turn(dst, src, start, stop):
             nc.tensor.matmul(dst, src, ident[:], start=start, stop=stop, is_transpose=True)
 
-        emb_psum = []
-        for g, (lo, hi) in enumerate(((0, EMB_CUT), (EMB_CUT, SPLIT))):
-            flipped = bank(2 + g, "emb_flip%d" % g)
-            for o in range(0, hi - lo, P):
-                turn(flipped[:, o : o + P], emb_plane[3][:, lo + o : lo + o + P], True, True)
-            staged = sb("emb_t%d" % g, [P, hi - lo], F32)
-            nc.scalar.copy(staged[:], flipped[:, : hi - lo])
-            emb_psum.append(bank(g, "emb_back%d" % g))
-            for o in range(0, hi - lo, P):
-                turn(emb_psum[g][:, o : o + P], staged[:, o : o + P], True, True)
-
-        pair_acc = [bank(4 + c, "pair_acc%d" % c) for c in range(4)]
-        sources = ((0, emb_plane[0]), (1, emb_plane[1]), (0, up[FIFTH][:]), (0, up[0][:]), (1, up[1][:]))
-        for n, (s, source) in enumerate(sources):
-            for r in range(U // P):
-                o = (2 * (r % 2) + s) * P
-                opens, closes = n == 0 and r % 2 == 0, n == len(sources) - 1 and r % 2 == 1
-                turn(pair_acc[r // 2][:, o : o + P], source[:, r * P : (r + 1) * P], opens, closes)
-        for g in (1, 0):
-            back = bank(2 + g, "pair_back%d" % g)
-            for i in range(2):
-                turned = sb("pair_t%d" % (2 * g + i), [P, BANK], BF16)
-                nc.scalar.activation(turned[:], pair_acc[2 * g + i][:], COPY)
-                for b in range(2):
-                    o = (2 * i + b) * P
-                    turn(back[:, o : o + P], turned[:].bitcast(F32)[:, b * P : (b + 1) * P], True, True)
-            if g == 0:
-                nc.scalar.copy(words[0][:, :BANK], back[:])
+        def hidden(engine, h, t, b, lo, hi):
+            acc = bank(b, "h_acc%d_%d" % (t, lo))
+            first_product(acc, t, lo, hi)
+            if engine is nc.scalar:
+                nc.scalar.activation(h, acc[:, : hi - lo], RELU)
             else:
-                nc.scalar.copy(words[1][:, : U - SPLIT], back[:, SPLIT - BANK :])
-                nc.scalar.copy(words[0][:, BANK:SPLIT], back[:, : SPLIT - BANK])
+                nc.vector.tensor_scalar_max(h, acc[:, : hi - lo], 0.0)
 
-        chunks = list(zip(CELL_CUTS[:-1], CELL_CUTS[1:]))
-        side = len(chunks) - 1
-        reused = {side - 2: "pair_t1", side - 1: "pair_t0"}
-        z_bf = [sb("z_bf%d" % c, [P, (hi - lo) * PACK], BF16, tag=reused.get(c)) for c, (lo, hi) in enumerate(chunks)]
-        z_codes = {c: sb("z_codes%d" % c, [P, hi - lo], U32) for c, (lo, hi) in enumerate(chunks[:side])}
-        z_sc = [sb("z_sc%d" % c, [P, hi - lo], U8) for c, (lo, hi) in enumerate(chunks)]
-        pairs = [part[:].rearrange("p (u r) -> p u r", u=2) for part in words]
+        h_first = sb("h_first", [P, S], F32, tag="w1_raw1")
+        h0 = [h_first[:, :FIRST], h_first[:, FIRST:]]
+        h1 = sb("h1", [P, S], F32)
+        hidden(nc.scalar, h0[0], 0, 0, 0, FIRST)
+        nc.scalar.activation(places(0, 0, FIRST), h0[0], COPY)
+        hidden(nc.scalar, h0[1], 0, 2, FIRST, S)
+        nc.scalar.activation(places(0, FIRST, S), h0[1], COPY)
+        hidden(nc.vector, h1[:], 1, 3, 0, S)
+        nc.vector.tensor_copy(places(1, 0, S), h1[:])
+        planes = sb("planes", [P, PACK, SIDE], BF16)
+        for s in range(2):
+            summed = sb("summed%d" % s, [P, SIDE], BF16)
+            nc.gpsimd.tensor_tensor(summed[:], up[s][:, :SIDE], emb_sb[s][:, :SIDE], ADD)
+            for e in range(2):
+                nc.sync.dma_start(out=planes[s * P // 2 : (s + 1) * P // 2, e, :], in_=summed[e::2, :])
+        late_h = sb("late_h", [P, 2 * S], F32)
+        hidden(nc.scalar, late_h[:, :S], 3, 2, 0, S)
+        nc.vector.tensor_copy(places(3, 0, S), late_h[:, :S])
+        hidden(nc.scalar, late_h[:, S:], 2, 3, 0, S)
+        for lo in (0, HALF):
+            nc.scalar.activation(places(2, lo, lo + HALF), late_h[:, S + lo : S + lo + HALF], COPY)
 
-        def weave(c):
-            lo, hi = chunks[c]
-            n = lo // SPLIT
-            nc.scalar.copy(
-                z_bf[c][:].bitcast(F32).rearrange("p (r u) -> p r u", u=2),
-                pairs[n][:, :, lo - SPLIT * n : hi - SPLIT * n].rearrange("p u r -> p r u"),
-            )
-
-        lo, hi = chunks[side]
-        weave(side)
-        nc.gpsimd.tensor_tensor(
-            z_bf[side][:].rearrange("p (r t) -> p r t", t=PACK)[:, :, 3], up[3][:, lo:hi], emb_plane[3][:, lo:hi], ADD
+        chunks = [(lo, lo + CHUNK) for lo in range(0, U, CHUNK)]
+        top = len(chunks) - 1
+        piles = [bank(4 + u, "pile%d" % u) for u in range(2)]
+        emb_turned = [emb_sb[0][:, SIDE:], emb_sb[1][:, SIDE:], emb_top[:, 0, :], emb_top[:, 1, :]]
+        for sources in (emb_turned, [window[:, SIDE:] for window in up]):
+            for u, order in enumerate(((0, 1), (3, 2))):
+                for n, t in enumerate(order):
+                    for b in range(2):
+                        o = (2 * b + t % 2) * P
+                        first = sources is emb_turned
+                        opens, closes = first and (n, b) == (0, 0), not first and (n, b) == (1, 1)
+                        turn(piles[u][:, o : o + P], sources[t][:, b * P : (b + 1) * P], opens, closes)
+        turned = [sb("turned0", [P, 2 * CHUNK], BF16, tag="late_h"), sb("turned1", [P, 2 * CHUNK], BF16)]
+        nc.scalar.activation(turned[0][:], piles[0][:], COPY)
+        nc.scalar.activation(
+            turned[1][:].rearrange("p (b q e) -> p b q e", b=2, e=2),
+            piles[1][:].rearrange("p (b e q) -> p b q e", b=2, e=2),
+            COPY,
         )
-        for c, (lo, hi) in enumerate(chunks[:side]):
-            g = min(lo // EMB_CUT, 1)
-            nc.vector.tensor_tensor(
-                halves[0][:, 1, lo:hi, 1], up[3][:, lo:hi], emb_psum[g][:, lo - EMB_CUT * g : hi - EMB_CUT * g], ADD
-            )
-            weave(c)
+        back = bank(6, "top_back")
+        for u in range(2):
+            for b in range(2):
+                o = (2 * u + b) * P
+                turn(back[:, o : o + P], turned[u][:].bitcast(F32)[:, b * P : (b + 1) * P], True, True)
 
-        z_codes[side] = sb("z_codes%d" % side, [P, U - SPLIT], U32, tag="up3")
-        y = [sb("y0", [P, U], F32, tag="words0"), sb("y1", [P, U], F32)]
+        for t in (3, 2):
+            nc.vector.tensor_tensor(planes[:, t, :], up[t][:, :SIDE], emb_sb[t][:, :SIDE], ADD)
+        z_bf = {}
+        for c, (lo, hi) in enumerate(chunks[:top]):
+            z_bf[c] = sb("z_bf%d" % c, [P, CHUNK * PACK], BF16, tag="up2" if c == top - 1 else None)
+            copy = nc.scalar.copy if c == top - 1 else nc.vector.tensor_copy
+            copy(z_bf[c][:].rearrange("p (r t) -> p r t", t=PACK), planes[:, :, lo:hi].rearrange("p t r -> p r t"))
+        z_bf[top] = sb("z_bf%d" % top, [P, CHUNK * PACK], BF16, tag="planes")
+        nc.scalar.copy(
+            z_bf[top][:].bitcast(F32).rearrange("p (r u) -> p r u", u=2), back[:].rearrange("p (u r) -> p r u", u=2)
+        )
+
+        order = (0, 1, 2, top)
+        z_codes, z_sc = {}, {}
 
         def second_product(acc, m, c):
             nc.tensor.matmul_mx(
@@ -249,74 +244,74 @@ def tile_picked_devox_relu_e_kernel(
                 stop=True,
             )
 
-        for c in [0, side] + list(range(1, side)):
-            lo, hi = chunks[c]
+        sums = {}
+        for n, c in enumerate(order):
+            z_codes[c] = sb("z_codes%d" % c, [P, CHUNK], U32, tag="turned1" if n == 0 else None)
+            z_sc[c] = sb("z_sc%d" % c, [P, CHUNK], U8)
             nc.vector.quantize_mx(out=z_codes[c][:].bitcast(FP8X4), scales=z_sc[c][:], in_=z_bf[c][:])
-            acc = bank(2 + c, "y0_acc%d" % c)
-            second_product(acc[:, : hi - lo], 0, c)
-            if c == side - 1:
-                nc.vector.tensor_scalar_max(y[0][:, lo:hi], acc[:, : hi - lo], 0.0)
+            sums[c] = bank((7, 0, 1, 2)[n], "y0_acc%d" % c)
+            second_product(sums[c][:, :CHUNK], 0, c)
+        y = [sb("y%d" % m, [P, U], F32) for m in range(2)]
+        for c in order:
+            if c == top:
+                nc.vector.tensor_scalar_max(y[0][:, chunks[c][0] : chunks[c][1]], sums[c][:, :CHUNK], 0.0)
             else:
-                nc.scalar.activation(y[0][:, lo:hi], acc[:, : hi - lo], RELU)
-        for i in range(len(chunks) // 2):
-            acc = bank(4 + i, "y1_acc%d" % (4 + i))
-            first, last = chunks[2 * i][0], chunks[2 * i + 1][1]
-            for c in (2 * i, 2 * i + 1):
-                lo, hi = chunks[c]
-                second_product(acc[:, lo - first : hi - first], 1, c)
-            nc.scalar.activation(y[1][:, first:last], acc[:, : last - first], RELU)
+                nc.scalar.activation(y[0][:, chunks[c][0] : chunks[c][1]], sums[c][:, :CHUNK], RELU)
+        for b, pair in ((0, (0, 1)), (1, (2, 3))):
+            acc = bank(b, "y1_acc%d" % b)
+            for i, c in enumerate(pair):
+                second_product(acc[:, i * CHUNK : (i + 1) * CHUNK], 1, c)
+            nc.scalar.activation(y[1][:, chunks[pair[0]][0] : chunks[pair[1]][1]], acc[:], RELU)
 
-        def fetch(term, m, d, lo, hi):
-            nc.vector.tensor_tensor(
-                term, y[m][:].indirect(pos_sb[d][:, lo // 16 : hi // 16]), gate_sb[d][:, lo:hi], MULT
-            )
+        def picks(d, lo, hi):
+            return pos_sb[d][:, lo // 16 : hi // 16]
 
-        def pile(acc, term, lo, hi, first, last):
-            for o in range(lo, hi, P):
-                turn(acc[:, o - lo : o - lo + P], term[:, o : o + P], first and o == lo, last and o + P == hi)
-
-        def turned_at(b):
-            return (2 + b) * BANK_BYTES
-
-        def turn_back(acc, width, b, name):
-            turned_sum = placed(name + "_t", [P, width], F32, turned_at(b))
-            nc.scalar.activation(turned_sum[:], acc[:, :width], COPY)
-            back = bank(b, name + "_back")
-            for o in range(0, width, P):
-                turn(back[:, o : o + P], turned_sum[:, o : o + P], True, True)
-            return back
-
-        def finish(m, lo, hi, partial, term):
-            res = sb("res%d_%d" % (m, lo), [P, hi - lo], F32)
-            nc.vector.tensor_tensor(res[:], partial, term, ADD)
-            nc.sync.dma_start(out=out[m * P : (m + 1) * P, lo:hi], in_=res[:])
-
-        spans = ((0, 0, V), (1, 0, V // 2), (1, V // 2, V))
-        sums = [bank(g, "sum%d" % g) for g in range(len(spans))]
-        backs = []
+        raw = {}
         for m in range(2):
-            first_term = sb("term%d_0" % m, [P, V], F32)
-            fetch(first_term[:], m, 0, 0, V)
-            own = [(g, lo, hi) for g, (rows, lo, hi) in enumerate(spans) if rows == m]
-            for g, lo, hi in own:
-                pile(sums[g], first_term, lo, hi, True, False)
-            second_term = sb("term%d_1" % m, [P, V], F32)
-            for g, lo, hi in own:
-                fetch(second_term[:, lo:hi], m, 1, lo, hi)
-                pile(sums[g], second_term, lo, hi, False, True)
-                backs.append(turn_back(sums[g], hi - lo, 4 + g, "sum%d" % g))
+            for d in range(2):
+                raw[m, d] = sb("raw%d_%d" % (m, d), [P, RAW[d]], F32)
+                nc.scalar.activation(raw[m, d][:], y[m][:].indirect(picks(d, 0, RAW[d])), COPY)
 
-        mid, tail = V // 2, V - LAST
-        last0 = sb("last0", [P, V], F32, tag="gate0")
-        fetch(last0[:], 0, 2, 0, V)
-        last1 = [sb("last1_0", [P, mid], F32, tag="gate1")]
-        fetch(last1[0][:], 1, 2, 0, mid)
-        for lo in (0, mid):
-            finish(0, lo, lo + mid, backs[0][:, lo : lo + mid], last0[:, lo : lo + mid])
-        last1.append(placed("last1_1", [P, tail - mid], F32, turned_at(4)))
-        fetch(last1[1][:], 1, 2, mid, tail)
-        finish(1, 0, mid, backs[1][:, :mid], last1[0][:])
-        last1.append(placed("last1_2", [P, LAST], F32, turned_at(5)))
-        fetch(last1[2][:], 1, 2, tail, V)
-        finish(1, mid, tail, backs[2][:, : tail - mid], last1[1][:])
-        finish(1, tail, V, backs[2][:, tail - mid : mid], last1[2][:])
+        out_rows = out.rearrange("(m p) v -> p m v", m=2)
+        terms = [sb("term%d" % d, [P, 2, V - fused_from[d]], F32) for d in range(D)]
+        for m in range(2):
+            for d in range(D):
+                nc.vector.tensor_tensor(
+                    terms[d][:, m, :], y[m][:].indirect(picks(d, fused_from[d], V)), gate_sb[d][:], MULT
+                )
+
+        def finish(lo, first, second):
+            res = sb("res%d" % lo, [P, 2, P], F32)
+            nc.vector.tensor_tensor(res[:], first, second, ADD)
+            nc.sync.dma_start(out=out_rows[:, :, lo : lo + P], in_=res[:])
+
+        both = sb("both", [P, 2, V - RAW[1]], F32)
+        nc.vector.tensor_tensor(both[:], terms[1][:], terms[2][:, :, RAW[1] :], ADD)
+        finish(RAW[0], terms[0][:], both[:, :, RAW[0] - RAW[1] :])
+
+        backs = {b: bank(4 + b, "back%d" % b) for b in range(RAW[0] // P)}
+        for d in range(2):
+            blocks = list(reversed(range(RAW[d] // P)))
+            flips = {b // 2: bank(2 * d + b // 2, "flip%d_%d" % (d, b // 2)) for b in blocks if b % 2 == 0}
+            for m in range(2):
+                for b in blocks:
+                    o = (2 * (b % 2) + m) * P
+                    turn(flips[b // 2][:, o : o + P], raw[m, d][:, b * P : (b + 1) * P], True, True)
+            for b in blocks:
+                scaled = sb("scaled%d_%d" % (b, d), [P, 2 * P], F32)
+                o = 2 * (b % 2) * P
+                nc.scalar.activation(
+                    scaled[:], flips[b // 2][:, o : o + 2 * P], COPY, scale=gate_col[d][:, b : b + 1]
+                )
+                closes = d == 1 or b * P >= RAW[1]
+                for m in range(2):
+                    turn(
+                        backs[b][:, m * P : (m + 1) * P],
+                        scaled[:, m * P : (m + 1) * P],
+                        (d, m) == (0, 0),
+                        closes and m == 1,
+                    )
+        for b in reversed(range(RAW[0] // P)):
+            lo = b * P
+            rest = both[:, :, lo - RAW[1] : lo - RAW[1] + P] if lo >= RAW[1] else terms[2][:, :, lo : lo + P]
+            finish(lo, backs[b][:, : 2 * P].rearrange("p (m v) -> p m v", m=2), rest)

@@ -33,14 +33,10 @@ def tile_picked_devox_relu_e_kernel(
     nc = tc.nc
     with ExitStack() as ctx:
         keep = ctx.enter_context(tc.tile_pool(name="keep", bufs=1))
-        shared = ctx.enter_context(tc.tile_pool(name="shared", bufs=1))
         psum = ctx.enter_context(tc.psum_pool(name="psum", bufs=1))
 
         def sb(name, shape, dtype, tag=None):
             return keep.tile(shape, dtype, name=name, tag=tag or name, align_bytes=64)
-
-        def placed(name, shape, dtype, offset):
-            return shared.tile(shape, dtype, name=name, align_bytes=64, offset=offset)
 
         def bank(b, name):
             return psum.tile([P, BANK], F32, name=name, tag="bank%d" % b)
@@ -52,25 +48,23 @@ def tile_picked_devox_relu_e_kernel(
 
         x_rows = xT.rearrange("(p j) t -> p j t", j=PACK)
         x_plane = [sb("x_plane%d" % j, [P, T], F32) for j in range(PACK)]
-        w1_raw = [sb("w1_raw%d" % s, [P, PACK, H // 2], F32) for s in range(2)]
+        w1_raw = [sb("w1_raw%d" % h, [P, 2, H], F32) for h in range(2)]
         nc.sync.dma_start(out=x_plane[0][:], in_=x_rows[:, 0, :])
         offs_sb = load_list("offs_sb", offs)
         for j in range(1, PACK):
             nc.sync.dma_start(out=x_plane[j][:], in_=x_rows[:, j, :])
         w1_rows = w1.rearrange("(p j) c -> p j c", j=PACK)
-        for s in range(2):
-            nc.sync.dma_start(out=w1_raw[s][:], in_=w1_rows[:, :, s * H // 2 : (s + 1) * H // 2])
-            if s == 0:
-                cell_sb = load_list("cell_sb", cell)
+        for h in range(2):
+            nc.sync.dma_start(out=w1_raw[h][:], in_=w1_rows[:, 2 * h : 2 * h + 2, :])
+        cell_sb = load_list("cell_sb", cell)
         emb_rows = emb.rearrange("(p t) r -> p t r", t=PACK)
-        emb_sb = [sb("emb%d" % t, [P, U if t < 2 else SIDE], F32) for t in range(PACK)]
-        emb_top = sb("emb_top", [P, 2, CHUNK], F32)
-        for s in range(2):
-            for e in range(2):
-                nc.sync.dma_start(out=emb_sb[s][e::2, :], in_=emb_rows[s * P // 2 : (s + 1) * P // 2, e, :])
-        nc.sync.dma_start(out=emb_top[:], in_=emb_rows[:, 2:, SIDE:])
-        for t in (3, 2):
+        emb_sb = {t: sb("emb%d" % t, [P, SIDE], F32) for t in (0, 1, 3)}
+        late = sb("late", [P, 2 * SIDE], F32)
+        emb_top = [sb("emb_top%d" % u, [P, 2, CHUNK], F32) for u in range(2)]
+        for t in (1, 0):
             nc.sync.dma_start(out=emb_sb[t][:], in_=emb_rows[:, t, :SIDE])
+        nc.sync.dma_start(out=emb_top[0][:], in_=emb_rows[:, :2, SIDE:])
+        nc.sync.dma_start(out=emb_sb[3][:], in_=emb_rows[:, 3, :SIDE])
         w2_codes = sb("w2_codes", [P, N], I32)
         nc.sync.dma_start(out=w2_codes[:], in_=w2_words[0].rearrange("p n t -> p (n t)").bitcast(I32))
         w2_sc = sb("w2_sc", [P, N], U8)
@@ -89,15 +83,17 @@ def tile_picked_devox_relu_e_kernel(
         with nc.allow_non_contiguous_dma(reason="one gate value a partition"):
             for d in range(2):
                 nc.sync.dma_start(out=gate_col[d][:], in_=gate[d, 0, : RAW[d]].rearrange("(b p) -> p b", p=P))
+        nc.sync.dma_start(out=emb_top[1][:], in_=emb_rows[:, 2:, SIDE:])
+        nc.sync.dma_start(out=late[:, :SIDE], in_=emb_rows[:, 2, :SIDE])
 
         ident = sb("ident", [P, P], F32)
         make_identity(nc, ident[:])
 
-        up = [sb("up%d" % t, [P, U], F32) for t in range(PACK)]
+        up = [sb("up%d" % t, [P, U + SIDE if t == 2 else U], F32) for t in range(PACK)]
         for t in (0, 1):
             nc.vector.memset(up[t][:], 0.0)
-        for t in (2, 3):
-            nc.gpsimd.memset(up[t][:], 0.0)
+        nc.scalar.activation(up[3][:], up[0][:], COPY)
+        nc.gpsimd.memset(up[2][:], 0.0)
 
         x_bf = [sb("x_bf%d" % s, [P, HALF, PACK], BF16) for s in range(2)]
         entries = [offs_sb[:, s * HALF // 16 : (s + 1) * HALF // 16] for s in range(2)]
@@ -119,28 +115,34 @@ def tile_picked_devox_relu_e_kernel(
                 out=x_codes[s][:].bitcast(FP8X4), scales=x_sc[s][:], in_=x_bf[s][:].rearrange("p n j -> p (n j)")
             )
 
-        columns = [raw[:].rearrange("p j (q t) -> p q j t", t=PACK) for raw in w1_raw]
+        dealt = [sb("w1_bf%d" % u, [P, 2 * P * PACK], BF16) for u in range(2)]
+
+        def deal(u, h):
+            dst = dealt[u][:].rearrange("p (e q j) -> p q j e", e=2, j=PACK)[:, :, 2 * h : 2 * h + 2, :]
+            src = w1_raw[h][:].rearrange("p j (q t) -> p q j t", t=PACK)[:, :, :, 2 * u : 2 * u + 2]
+            if u == 0:
+                nc.vector.tensor_copy(dst, src)
+            else:
+                nc.scalar.activation(dst, src, COPY)
+
         w1_codes, w1_sc = {}, {}
 
-        def quantize_w1(ts, dealt):
-            codes = sb("w1_codes%d" % ts[0], [P, len(ts) * P], U32)
-            scales = sb("w1_sc%d" % ts[0], [P, len(ts) * P], U8)
-            nc.vector.quantize_mx(out=codes[:].bitcast(FP8X4), scales=scales[:], in_=dealt[:])
-            for i, t in enumerate(ts):
-                w1_codes[t], w1_sc[t] = codes[:, i * P : (i + 1) * P], scales[:, i * P : (i + 1) * P]
+        def quantize_w1(u):
+            codes = sb("w1_codes%d" % u, [P, 2 * P], U32)
+            scales = sb("w1_sc%d" % u, [P, 2 * P], U8)
+            nc.vector.quantize_mx(out=codes[:].bitcast(FP8X4), scales=scales[:], in_=dealt[u][:])
+            for e in range(2):
+                w1_codes[2 * u + e] = codes[:, e * P : (e + 1) * P]
+                w1_sc[2 * u + e] = scales[:, e * P : (e + 1) * P]
 
         quantize_x(0)
-        for s in range(2):
-            dealt = sb("w1_bf%d" % s, [P, P * PACK], BF16)
-            nc.vector.tensor_copy(dealt[:].rearrange("p (q e j) -> p q j e", e=2, j=PACK), columns[s][:, :, :, 0:2])
-            if s == 1:
-                quantize_x(1)
-            quantize_w1((s,), dealt)
-        dealt = sb("w1_bf2", [P, 2 * P * PACK], BF16)
-        halves = dealt[:].rearrange("p (e s q j) -> p s q j e", e=2, s=2, j=PACK)
-        for s in range(2):
-            nc.scalar.activation(halves[:, s], columns[s][:, :, :, 2:], COPY)
-        quantize_w1((2, 3), dealt)
+        for u in range(2):
+            deal(u, 0)
+        quantize_x(1)
+        for u in range(2):
+            deal(u, 1)
+        for u in range(2):
+            quantize_w1(u)
 
         def first_product(acc, t, first, last):
             cuts = sorted({first, min(max(HALF, first), last), last})
@@ -157,78 +159,92 @@ def tile_picked_devox_relu_e_kernel(
                     stop=True,
                 )
 
-        def places(t, lo, hi):
-            return up[t][:].indirect(cell_sb[:, lo // 16 : hi // 16])
-
         def turn(dst, src, start, stop):
             nc.tensor.matmul(dst, src, ident[:], start=start, stop=stop, is_transpose=True)
 
-        def hidden(engine, h, t, b, lo, hi):
-            acc = bank(b, "h_acc%d_%d" % (t, lo))
-            first_product(acc, t, lo, hi)
-            if engine is nc.scalar:
-                nc.scalar.activation(h, acc[:, : hi - lo], RELU)
-            else:
-                nc.vector.tensor_scalar_max(h, acc[:, : hi - lo], 0.0)
+        pieces = [(0, 0, FIRST), (1, 0, FIRST), (1, FIRST, S), (3, 0, HALF), (0, FIRST, S), (3, HALF, S), (2, 0, S)]
+        hid = [sb("h%d" % t, [P, S], F32) for t in range(PACK)]
+        accs = {}
 
-        h_first = sb("h_first", [P, S], F32, tag="w1_raw1")
-        h0 = [h_first[:, :FIRST], h_first[:, FIRST:]]
-        h1 = sb("h1", [P, S], F32)
-        hidden(nc.scalar, h0[0], 0, 0, 0, FIRST)
-        nc.scalar.activation(places(0, 0, FIRST), h0[0], COPY)
-        hidden(nc.scalar, h0[1], 0, 2, FIRST, S)
-        nc.scalar.activation(places(0, FIRST, S), h0[1], COPY)
-        hidden(nc.vector, h1[:], 1, 3, 0, S)
-        nc.vector.tensor_copy(places(1, 0, S), h1[:])
-        planes = sb("planes", [P, PACK, SIDE], BF16)
-        for s in range(2):
-            summed = sb("summed%d" % s, [P, SIDE], BF16)
-            nc.gpsimd.tensor_tensor(summed[:], up[s][:, :SIDE], emb_sb[s][:, :SIDE], ADD)
-            for e in range(2):
-                nc.sync.dma_start(out=planes[s * P // 2 : (s + 1) * P // 2, e, :], in_=summed[e::2, :])
-        late_h = sb("late_h", [P, 2 * S], F32)
-        hidden(nc.scalar, late_h[:, :S], 3, 2, 0, S)
-        nc.vector.tensor_copy(places(3, 0, S), late_h[:, :S])
-        hidden(nc.scalar, late_h[:, S:], 2, 3, 0, S)
+        def multiply(b, t, lo, hi):
+            accs[t, lo] = bank(b, "h_acc%d_%d" % (t, lo))
+            first_product(accs[t, lo], t, lo, hi)
+
+        def empty(engine, t, lo, hi):
+            if engine is nc.scalar:
+                nc.scalar.activation(hid[t][:, lo:hi], accs[t, lo][:, : hi - lo], RELU)
+            else:
+                nc.vector.tensor_scalar_max(hid[t][:, lo:hi], accs[t, lo][:, : hi - lo], 0.0)
+
+        def scatter(engine, t, lo, hi):
+            places = up[t][:].indirect(cell_sb[:, lo // 16 : hi // 16])
+            if engine is nc.scalar:
+                nc.scalar.activation(places, hid[t][:, lo:hi], COPY)
+            else:
+                nc.vector.tensor_copy(places, hid[t][:, lo:hi])
+
+        for b, piece in enumerate(pieces):
+            multiply(b, *piece)
+        for t, engine in ((0, nc.scalar), (1, nc.vector)):
+            empty(engine, t, 0, FIRST)
+            scatter(engine, t, 0, FIRST)
+            empty(engine, t, FIRST, S)
+        empty(nc.vector, 3, 0, HALF)
+        empty(nc.scalar, 3, HALF, S)
+        empty(nc.scalar, 2, 0, S)
+        for t, engine in ((0, nc.scalar), (1, nc.vector)):
+            scatter(engine, t, FIRST, S)
+        scatter(nc.vector, 3, 0, S)
         for lo in (0, HALF):
-            nc.scalar.activation(places(2, lo, lo + HALF), late_h[:, S + lo : S + lo + HALF], COPY)
+            scatter(nc.scalar, 2, lo, lo + HALF)
 
         chunks = [(lo, lo + CHUNK) for lo in range(0, U, CHUNK)]
         top = len(chunks) - 1
-        piles = [bank(4 + u, "pile%d" % u) for u in range(2)]
-        emb_turned = [emb_sb[0][:, SIDE:], emb_sb[1][:, SIDE:], emb_top[:, 0, :], emb_top[:, 1, :]]
-        for sources in (emb_turned, [window[:, SIDE:] for window in up]):
-            for u, order in enumerate(((0, 1), (3, 2))):
-                for n, t in enumerate(order):
-                    for b in range(2):
-                        o = (2 * b + t % 2) * P
-                        first = sources is emb_turned
-                        opens, closes = first and (n, b) == (0, 0), not first and (n, b) == (1, 1)
-                        turn(piles[u][:, o : o + P], sources[t][:, b * P : (b + 1) * P], opens, closes)
-        turned = [sb("turned0", [P, 2 * CHUNK], BF16, tag="late_h"), sb("turned1", [P, 2 * CHUNK], BF16)]
-        nc.scalar.activation(turned[0][:], piles[0][:], COPY)
-        nc.scalar.activation(
-            turned[1][:].rearrange("p (b q e) -> p b q e", b=2, e=2),
-            piles[1][:].rearrange("p (b e q) -> p b q e", b=2, e=2),
-            COPY,
-        )
-        back = bank(6, "top_back")
+        words = sb("words", [P, top * 2 * CHUNK * 2], BF16)
+        halves = words[:].rearrange("p (c u r e) -> p c u r e", c=top, u=2, e=2)
+
+        for t in (1, 0):
+            nc.gpsimd.tensor_tensor(
+                halves[:, :, 0, :, t],
+                up[t][:, :SIDE].rearrange("p (c r) -> p c r", r=CHUNK),
+                emb_sb[t][:].rearrange("p (c r) -> p c r", r=CHUNK),
+                ADD,
+            )
+        turned = []
+        for u in range(2):
+            pile = bank((0, 7)[u], "pile%d" % u)
+            steps = [(emb_top[u][:, e, :], e) for e in (1, 0)] + [(up[2 * u + e][:, SIDE:U], e) for e in (1, 0)]
+            for n, (src, e) in enumerate(steps):
+                for b in range(2):
+                    o = (2 * b + e) * P
+                    turn(pile[:, o : o + P], src[:, b * P : (b + 1) * P], (n, b) == (0, 0), (n, b) == (3, 1))
+            turned.append(sb("turned%d" % u, [P, 2 * CHUNK], BF16, tag="h2" if u == 0 else None))
+            dst = turned[u][:].rearrange("p (b q e) -> p b q e", b=2, e=2)
+            src = pile[:].rearrange("p (b e q) -> p b q e", b=2, e=2)
+            nc.scalar.activation(dst, src, COPY)
+        back = bank(7, "top_back")
         for u in range(2):
             for b in range(2):
                 o = (2 * u + b) * P
                 turn(back[:, o : o + P], turned[u][:].bitcast(F32)[:, b * P : (b + 1) * P], True, True)
 
-        for t in (3, 2):
-            nc.vector.tensor_tensor(planes[:, t, :], up[t][:, :SIDE], emb_sb[t][:, :SIDE], ADD)
-        z_bf = {}
+        nc.vector.tensor_tensor(late[:, SIDE:], up[3][:, :SIDE], emb_sb[3][:], ADD)
         for c, (lo, hi) in enumerate(chunks[:top]):
-            z_bf[c] = sb("z_bf%d" % c, [P, CHUNK * PACK], BF16, tag="up2" if c == top - 1 else None)
-            copy = nc.scalar.copy if c == top - 1 else nc.vector.tensor_copy
-            copy(z_bf[c][:].rearrange("p (r t) -> p r t", t=PACK), planes[:, :, lo:hi].rearrange("p t r -> p r t"))
-        z_bf[top] = sb("z_bf%d" % top, [P, CHUNK * PACK], BF16, tag="planes")
-        nc.scalar.copy(
-            z_bf[top][:].bitcast(F32).rearrange("p (r u) -> p r u", u=2), back[:].rearrange("p (u r) -> p r u", u=2)
-        )
+            nc.vector.tensor_tensor(
+                halves[:, c, 1].rearrange("p (g i) e -> p g e i", i=2),
+                up[2][:, lo : lo + U + CHUNK].rearrange("p (e r) -> p e r", r=CHUNK)[:, :: U // CHUNK].rearrange("p e (g i) -> p g e i", i=2),
+                late[:].rearrange("p (e r) -> p e r", e=2)[:, :, lo:hi].rearrange("p e (g i) -> p g e i", i=2),
+                ADD,
+            )
+        z_bf = {c: sb("z_bf%d" % c, [P, CHUNK * PACK], BF16) for c in range(top + 1)}
+
+        def weave(copy, c, src):
+            copy(z_bf[c][:].bitcast(F32).rearrange("p (r u) -> p r u", u=2), src.rearrange("p (u r) -> p r u", u=2))
+
+        for c in range(top):
+            copy = nc.vector.tensor_copy if c == top - 1 else nc.scalar.copy
+            weave(copy, c, words[:].bitcast(F32)[:, c * 2 * CHUNK : (c + 1) * 2 * CHUNK])
+        weave(nc.scalar.copy, top, back[:])
 
         order = (0, 1, 2, top)
         z_codes, z_sc = {}, {}
@@ -246,10 +262,10 @@ def tile_picked_devox_relu_e_kernel(
 
         sums = {}
         for n, c in enumerate(order):
-            z_codes[c] = sb("z_codes%d" % c, [P, CHUNK], U32, tag="turned1" if n == 0 else None)
+            z_codes[c] = sb("z_codes%d" % c, [P, CHUNK], U32)
             z_sc[c] = sb("z_sc%d" % c, [P, CHUNK], U8)
             nc.vector.quantize_mx(out=z_codes[c][:].bitcast(FP8X4), scales=z_sc[c][:], in_=z_bf[c][:])
-            sums[c] = bank((7, 0, 1, 2)[n], "y0_acc%d" % c)
+            sums[c] = bank(1 + n, "y0_acc%d" % c)
             second_product(sums[c][:, :CHUNK], 0, c)
         y = [sb("y%d" % m, [P, U], F32) for m in range(2)]
         for c in order:
@@ -257,7 +273,7 @@ def tile_picked_devox_relu_e_kernel(
                 nc.vector.tensor_scalar_max(y[0][:, chunks[c][0] : chunks[c][1]], sums[c][:, :CHUNK], 0.0)
             else:
                 nc.scalar.activation(y[0][:, chunks[c][0] : chunks[c][1]], sums[c][:, :CHUNK], RELU)
-        for b, pair in ((0, (0, 1)), (1, (2, 3))):
+        for b, pair in ((5, (0, 1)), (6, (2, 3))):
             acc = bank(b, "y1_acc%d" % b)
             for i, c in enumerate(pair):
                 second_product(acc[:, i * CHUNK : (i + 1) * CHUNK], 1, c)

from contextlib import ExitStack

import concourse.mybir as mybir
from concourse.masks import make_identity

F32 = mybir.dt.float32
BF16 = mybir.dt.bfloat16
I32 = mybir.dt.int32
U32 = mybir.dt.uint32
U16 = mybir.dt.uint16
U8 = mybir.dt.uint8
FP8X4 = mybir.dt.float8_e4m3fn_x4
ADD = mybir.AluOpType.add
MULT = mybir.AluOpType.mult
RELU = mybir.ActivationFunctionType.Relu
COPY = mybir.ActivationFunctionType.Copy

K, T, S, D, V, H, N, U = 512, 2048, 512, 3, 512, 512, 256, 1024
P = 128
PACK = 4
HALF = S // 2
BANK = 512
FLOPS = 2 * K * H * S + 2 * H * N * U
CHUNK = 256
FIRST = 128
SIDE = U - CHUNK
RAW = (384, 256)


def tile_picked_devox_relu_e_kernel(
    tc, xT, w1, w2_words, w2_scales, gate, emb, offs, cell, pos1, pos2, pos3, out
):
    nc = tc.nc
    with ExitStack() as ctx:
        keep = ctx.enter_context(tc.tile_pool(name="keep", bufs=1))
        psum = ctx.enter_context(tc.psum_pool(name="psum", bufs=1))

        def sb(name, shape, dtype, tag=None):
            return keep.tile(shape, dtype, name=name, tag=tag or name, align_bytes=64)

        def bank(b, name):
            return psum.tile([P, BANK], F32, name=name, tag="bank%d" % b)

        def load_list(name, src):
            tile = keep.tile([P, S // 16], U16, name=name)
            nc.sync.dma_start(tile[:], src)
            return tile

        x_rows = xT.rearrange("(p j) t -> p j t", j=PACK)
        x_plane = [sb("x_plane%d" % j, [P, T], F32) for j in range(PACK)]
        w1_raw = [sb("w1_raw%d" % h, [P, 2, H], F32) for h in range(2)]
        nc.sync.dma_start(out=x_plane[0][:], in_=x_rows[:, 0, :])
        offs_sb = load_list("offs_sb", offs)
        for j in range(1, PACK):
            nc.sync.dma_start(out=x_plane[j][:], in_=x_rows[:, j, :])
        w1_rows = w1.rearrange("(p j) c -> p j c", j=PACK)
        for h in range(2):
            nc.sync.dma_start(out=w1_raw[h][:], in_=w1_rows[:, 2 * h : 2 * h + 2, :])
        cell_sb = load_list("cell_sb", cell)
        emb_rows = emb.rearrange("(p t) r -> p t r", t=PACK)
        emb_sb = {t: sb("emb%d" % t, [P, SIDE], F32) for t in (0, 1, 3)}
        late = sb("late", [P, 2 * SIDE], F32)
        emb_top = [sb("emb_top%d" % u, [P, 2, CHUNK], F32) for u in range(2)]
        for t in (1, 0):
            nc.sync.dma_start(out=emb_sb[t][:], in_=emb_rows[:, t, :SIDE])
        nc.sync.dma_start(out=emb_top[0][:], in_=emb_rows[:, :2, SIDE:])
        nc.sync.dma_start(out=emb_sb[3][:], in_=emb_rows[:, 3, :SIDE])
        w2_codes = sb("w2_codes", [P, N], I32)
        nc.sync.dma_start(out=w2_codes[:], in_=w2_words[0].rearrange("p n t -> p (n t)").bitcast(I32))
        w2_sc = sb("w2_sc", [P, N], U8)
        nc.gpsimd.memset(w2_sc[:], 0)
        for q in range(4):
            nc.sync.dma_start(
                out=w2_sc[32 * q : 32 * q + 4, :].bitcast(I32),
                in_=w2_scales[0, 4 * q : 4 * q + 4, :].bitcast(I32),
            )
        pos_sb = [load_list("pos%d_sb" % d, src) for d, src in enumerate((pos1, pos2, pos3))]
        fused_from = RAW + (0,)
        gate_sb = [sb("gate%d" % d, [P, V - fused_from[d]], F32) for d in range(D)]
        for d in range(D):
            nc.sync.dma_start(out=gate_sb[d][:], in_=gate[d][:, fused_from[d] :])
        gate_col = [sb("gate_col%d" % d, [P, RAW[d] // P], F32) for d in range(2)]
        with nc.allow_non_contiguous_dma(reason="one gate value a partition"):
            for d in range(2):
                nc.sync.dma_start(out=gate_col[d][:], in_=gate[d, 0, : RAW[d]].rearrange("(b p) -> p b", p=P))
        nc.sync.dma_start(out=emb_top[1][:], in_=emb_rows[:, 2:, SIDE:])
        nc.sync.dma_start(out=late[:, :SIDE], in_=emb_rows[:, 2, :SIDE])

        ident = sb("ident", [P, P], F32)
        make_identity(nc, ident[:])

        up = [sb("up%d" % t, [P, U + SIDE if t == 2 else U], F32) for t in range(PACK)]
        for t in (0, 1):
            nc.vector.memset(up[t][:], 0.0)
        nc.scalar.activation(up[3][:], up[0][:], COPY)
        nc.gpsimd.memset(up[2][:], 0.0)

        x_bf = [sb("x_bf%d" % s, [P, HALF, PACK], BF16) for s in range(2)]
        entries = [offs_sb[:, s * HALF // 16 : (s + 1) * HALF // 16] for s in range(2)]
        x_late = sb("x_late", [P, 2 * HALF], BF16)
        for j in range(PACK):
            nc.vector.tensor_copy(x_bf[0][:, :, j], x_plane[j][:].indirect(entries[0]))
            if j < 2:
                nc.vector.tensor_copy(x_bf[1][:, :, j], x_plane[j][:].indirect(entries[1]))
            else:
                nc.scalar.activation(
                    x_late[:, (j - 2) * HALF : (j - 1) * HALF], x_plane[j][:].indirect(entries[1]), COPY
                )
        nc.scalar.activation(x_bf[1][:, :, 2:], x_late[:].rearrange("p (e n) -> p n e", e=2), COPY)
        x_codes = [sb("x_codes%d" % s, [P, HALF], U32) for s in range(2)]
        x_sc = [sb("x_sc%d" % s, [P, HALF], U8) for s in range(2)]

        def quantize_x(s):
            nc.vector.quantize_mx(
                out=x_codes[s][:].bitcast(FP8X4), scales=x_sc[s][:], in_=x_bf[s][:].rearrange("p n j -> p (n j)")
            )

        dealt = [sb("w1_bf%d" % u, [P, 2 * P * PACK], BF16) for u in range(2)]

        def deal(u, h):
            dst = dealt[u][:].rearrange("p (e q j) -> p q j e", e=2, j=PACK)[:, :, 2 * h : 2 * h + 2, :]
            src = w1_raw[h][:].rearrange("p j (q t) -> p q j t", t=PACK)[:, :, :, 2 * u : 2 * u + 2]
            if u == 0:
                nc.vector.tensor_copy(dst, src)
            else:
                nc.scalar.activation(dst, src, COPY)

        w1_codes, w1_sc = {}, {}

        def quantize_w1(u):
            codes = sb("w1_codes%d" % u, [P, 2 * P], U32)
            scales = sb("w1_sc%d" % u, [P, 2 * P], U8)
            nc.vector.quantize_mx(out=codes[:].bitcast(FP8X4), scales=scales[:], in_=dealt[u][:])
            for e in range(2):
                w1_codes[2 * u + e] = codes[:, e * P : (e + 1) * P]
                w1_sc[2 * u + e] = scales[:, e * P : (e + 1) * P]

        quantize_x(0)
        for u in range(2):
            deal(u, 0)
        quantize_x(1)
        for u in range(2):
            deal(u, 1)
        for u in range(2):
            quantize_w1(u)

        def first_product(acc, t, first, last):
            cuts = sorted({first, min(max(HALF, first), last), last})
            for lo, hi in zip(cuts[:-1], cuts[1:]):
                s = lo // HALF
                picked = slice(lo - s * HALF, hi - s * HALF)
                nc.tensor.matmul_mx(
                    out=acc[:, lo - first : hi - first],
                    lhsT=w1_codes[t].bitcast(FP8X4),
                    lhsT_scale=w1_sc[t],
                    rhs=x_codes[s][:, picked].bitcast(FP8X4),
                    rhs_scale=x_sc[s][:, picked],
                    start=True,
                    stop=True,
                )

        def turn(dst, src, start, stop):
            nc.tensor.matmul(dst, src, ident[:], start=start, stop=stop, is_transpose=True)

        pieces = [(0, 0, FIRST), (1, 0, FIRST), (1, FIRST, S), (3, 0, HALF), (0, FIRST, S), (3, HALF, S), (2, 0, S)]
        hid = [sb("h%d" % t, [P, S], F32) for t in range(PACK)]
        accs = {}

        def multiply(b, t, lo, hi):
            accs[t, lo] = bank(b, "h_acc%d_%d" % (t, lo))
            first_product(accs[t, lo], t, lo, hi)

        def empty(engine, t, lo, hi):
            if engine is nc.scalar:
                nc.scalar.activation(hid[t][:, lo:hi], accs[t, lo][:, : hi - lo], RELU)
            else:
                nc.vector.tensor_scalar_max(hid[t][:, lo:hi], accs[t, lo][:, : hi - lo], 0.0)

        def scatter(engine, t, lo, hi):
            places = up[t][:].indirect(cell_sb[:, lo // 16 : hi // 16])
            if engine is nc.scalar:
                nc.scalar.activation(places, hid[t][:, lo:hi], COPY)
            else:
                nc.vector.tensor_copy(places, hid[t][:, lo:hi])

        for b, piece in enumerate(pieces):
            multiply(b, *piece)
        for t, engine in ((0, nc.scalar), (1, nc.vector)):
            empty(engine, t, 0, FIRST)
            scatter(engine, t, 0, FIRST)
            empty(engine, t, FIRST, S)
        empty(nc.vector, 3, 0, HALF)
        empty(nc.scalar, 3, HALF, S)
        empty(nc.scalar, 2, 0, S)
        for t, engine in ((0, nc.scalar), (1, nc.vector)):
            scatter(engine, t, FIRST, S)
        scatter(nc.vector, 3, 0, S)
        for lo in (0, HALF):
            scatter(nc.scalar, 2, lo, lo + HALF)

        chunks = [(lo, lo + CHUNK) for lo in range(0, U, CHUNK)]
        top = len(chunks) - 1
        words = sb("words", [P, top * 2 * CHUNK * 2], BF16)
        halves = words[:].rearrange("p (c u r e) -> p c u r e", c=top, u=2, e=2)

        for t in (1, 0):
            nc.gpsimd.tensor_tensor(
                halves[:, :, 0, :, t],
                up[t][:, :SIDE].rearrange("p (c r) -> p c r", r=CHUNK),
                emb_sb[t][:].rearrange("p (c r) -> p c r", r=CHUNK),
                ADD,
            )
        turned = []
        for u in range(2):
            pile = bank((0, 7)[u], "pile%d" % u)
            steps = [(emb_top[u][:, e, :], e) for e in (1, 0)] + [(up[2 * u + e][:, SIDE:U], e) for e in (1, 0)]
            for n, (src, e) in enumerate(steps):
                for b in range(2):
                    o = (2 * b + e) * P
                    turn(pile[:, o : o + P], src[:, b * P : (b + 1) * P], (n, b) == (0, 0), (n, b) == (3, 1))
            turned.append(sb("turned%d" % u, [P, 2 * CHUNK], BF16, tag="h2" if u == 0 else None))
            dst = turned[u][:].rearrange("p (b q e) -> p b q e", b=2, e=2)
            src = pile[:].rearrange("p (b e q) -> p b q e", b=2, e=2)
            nc.scalar.activation(dst, src, COPY)
        back = bank(7, "top_back")
        for u in range(2):
            for b in range(2):
                o = (2 * u + b) * P
                turn(back[:, o : o + P], turned[u][:].bitcast(F32)[:, b * P : (b + 1) * P], True, True)

        nc.vector.tensor_tensor(late[:, SIDE:], up[3][:, :SIDE], emb_sb[3][:], ADD)
        for c, (lo, hi) in enumerate(chunks[:top]):
            nc.vector.tensor_tensor(
                halves[:, c, 1].rearrange("p (g i) e -> p g e i", i=2),
                up[2][:, lo : lo + U + CHUNK].rearrange("p (e r) -> p e r", r=CHUNK)[:, :: U // CHUNK].rearrange("p e (g i) -> p g e i", i=2),
                late[:].rearrange("p (e r) -> p e r", e=2)[:, :, lo:hi].rearrange("p e (g i) -> p g e i", i=2),
                ADD,
            )
        z_bf = {c: sb("z_bf%d" % c, [P, CHUNK * PACK], BF16) for c in range(top + 1)}

        def weave(copy, c, src):
            copy(z_bf[c][:].bitcast(F32).rearrange("p (r u) -> p r u", u=2), src.rearrange("p (u r) -> p r u", u=2))

        for c in range(top):
            copy = nc.vector.tensor_copy if c == top - 1 else nc.scalar.copy
            weave(copy, c, words[:].bitcast(F32)[:, c * 2 * CHUNK : (c + 1) * 2 * CHUNK])
        weave(nc.scalar.copy, top, back[:])

        order = (0, 1, 2, top)
        z_codes, z_sc = {}, {}

        def second_product(acc, m, c):
            nc.tensor.matmul_mx(
                out=acc,
                lhsT=w2_codes[:, m * P : (m + 1) * P].bitcast(FP8X4),
                lhsT_scale=w2_sc[:, m * P : (m + 1) * P],
                rhs=z_codes[c][:].bitcast(FP8X4),
                rhs_scale=z_sc[c][:],
                start=True,
                stop=True,
            )

        sums = {}
        for n, c in enumerate(order):
            z_codes[c] = sb("z_codes%d" % c, [P, CHUNK], U32)
            z_sc[c] = sb("z_sc%d" % c, [P, CHUNK], U8)
            nc.vector.quantize_mx(out=z_codes[c][:].bitcast(FP8X4), scales=z_sc[c][:], in_=z_bf[c][:])
            sums[c] = bank(1 + n, "y0_acc%d" % c)
            second_product(sums[c][:, :CHUNK], 0, c)
        y = [sb("y%d" % m, [P, U], F32) for m in range(2)]
        for c in order:
            if c == top:
                nc.vector.tensor_scalar_max(y[0][:, chunks[c][0] : chunks[c][1]], sums[c][:, :CHUNK], 0.0)
            else:
                nc.scalar.activation(y[0][:, chunks[c][0] : chunks[c][1]], sums[c][:, :CHUNK], RELU)
        for b, pair in ((5, (0, 1)), (6, (2, 3))):
            acc = bank(b, "y1_acc%d" % b)
            for i, c in enumerate(pair):
                second_product(acc[:, i * CHUNK : (i + 1) * CHUNK], 1, c)
            nc.scalar.activation(y[1][:, chunks[pair[0]][0] : chunks[pair[1]][1]], acc[:], RELU)

        def picks(d, lo, hi):
            return pos_sb[d][:, lo // 16 : hi // 16]

        raw = {}
        for m in range(2):
            for d in range(2):
                raw[m, d] = sb("raw%d_%d" % (m, d), [P, RAW[d]], F32)
                nc.scalar.activation(raw[m, d][:], y[m][:].indirect(picks(d, 0, RAW[d])), COPY)

        out_rows = out.rearrange("(m p) v -> p m v", m=2)
        terms = [sb("term%d" % d, [P, 2, V - fused_from[d]], F32) for d in range(D)]
        for m in range(2):
            for d in range(D):
                nc.vector.tensor_tensor(
                    terms[d][:, m, :], y[m][:].indirect(picks(d, fused_from[d], V)), gate_sb[d][:], MULT
                )

        def finish(lo, first, second):
            res = sb("res%d" % lo, [P, 2, P], F32)
            nc.vector.tensor_tensor(res[:], first, second, ADD)
            nc.sync.dma_start(out=out_rows[:, :, lo : lo + P], in_=res[:])

        both = sb("both", [P, 2, V - RAW[1]], F32)
        nc.vector.tensor_tensor(both[:], terms[1][:], terms[2][:, :, RAW[1] :], ADD)
        finish(RAW[0], terms[0][:], both[:, :, RAW[0] - RAW[1] :])

        backs = {b: bank(4 + b, "back%d" % b) for b in range(RAW[0] // P)}
        for d in range(2):
            blocks = list(reversed(range(RAW[d] // P)))
            flips = {b // 2: bank(2 * d + b // 2, "flip%d_%d" % (d, b // 2)) for b in blocks if b % 2 == 0}
            for m in range(2):
                for b in blocks:
                    o = (2 * (b % 2) + m) * P
                    turn(flips[b // 2][:, o : o + P], raw[m, d][:, b * P : (b + 1) * P], True, True)
            for b in blocks:
                scaled = sb("scaled%d_%d" % (b, d), [P, 2 * P], F32)
                o = 2 * (b % 2) * P
                nc.scalar.activation(
                    scaled[:], flips[b // 2][:, o : o + 2 * P], COPY, scale=gate_col[d][:, b : b + 1]
                )
                closes = d == 1 or b * P >= RAW[1]
                for m in range(2):
                    turn(
                        backs[b][:, m * P : (m + 1) * P],
                        scaled[:, m * P : (m + 1) * P],
                        (d, m) == (0, 0),
                        closes and m == 1,
                    )
        for b in reversed(range(RAW[0] // P)):
            lo = b * P
            rest = both[:, :, lo - RAW[1] : lo - RAW[1] + P] if lo >= RAW[1] else terms[2][:, :, lo : lo + P]
            finish(lo, backs[b][:, : 2 * P].rearrange("p (m v) -> p m v", m=2), rest)
